import numpy as np
import ml_dtypes


def mxq(x, axis, fmt="e4m3"):
    dtype, down = {"e4m3": (ml_dtypes.float8_e4m3fn, 7), "e5m2": (ml_dtypes.float8_e5m2, 14)}[fmt]
    v = np.moveaxis(np.asarray(x, np.float32).astype(ml_dtypes.bfloat16).astype(np.float64), axis, -1)
    blocks = v.reshape(v.shape[:-1] + (-1, 32))
    amax = np.abs(blocks).max(-1, keepdims=True)
    byte = np.maximum(np.where(amax > 0, np.frexp(amax)[1] - 1 + 127, 0) - down, 1)
    scale = np.exp2(byte - 127.0)
    codes = (blocks / scale).astype(np.float32).astype(dtype).astype(np.float64)
    return np.moveaxis((codes * scale).reshape(v.shape), -1, axis)


WIDE = False


def mx_kscale(k):
    if not WIDE:
        return np.ones(k)
    levels = np.array([10, -10, 5, -5, 0])
    if k % 512:
        return np.exp2(np.random.permutation(np.resize(levels, k // 32))).repeat(32)
    a = np.empty((k // 512, 16))
    for p in range(k // 512):
        a[p, :8] = np.random.permutation(np.resize(levels, 8))
        for g in range(8):
            far = levels[np.abs(levels - a[p, g]) >= 10]
            a[p, g + 8] = far[np.random.randint(len(far))]
    return np.exp2(a.ravel()).repeat(32)


def f64(x):
    return np.asarray(x).astype(np.float64)


def striped(idx):
    return np.tile(idx.reshape(-1, 16).T, (8, 1)).astype(np.uint16)


def unstriped(offs):
    return offs[:16].T.reshape(-1).astype(np.int64)


E2M1 = np.array([0.0, 0.5, 1.0, 1.5, 2.0, 3.0, 4.0, 6.0, -0.0, -0.5, -1.0, -1.5, -2.0, -3.0, -4.0, -6.0])


def pack_weight(w, fmt):
    k, n = w.shape
    w = f64(np.asarray(w, np.float32).astype(ml_dtypes.bfloat16)).reshape(k // 32, 32, n)
    amax = np.abs(w).max(1)
    if fmt == "e4m3":
        byte = np.frexp(amax)[1] - 1 + 127 - 7
    else:
        mant, ex = np.frexp(amax / 6.0)
        byte = np.where(mant > 0.5, ex, ex - 1) + 127
    byte = np.clip(np.where(amax > 0, byte, 1), 1, 254)
    scaled = (w * np.exp2(127.0 - byte)[:, None, :]).reshape(k, n).astype(np.float32)
    by_word = np.ascontiguousarray(scaled.reshape(k // 512, 128, 4, n).transpose(0, 1, 3, 2))
    if fmt == "e4m3":
        words = by_word.astype(ml_dtypes.float8_e4m3fn).view(np.uint8)
    else:
        c = by_word.astype(ml_dtypes.float4_e2m1fn).view(np.uint8) & 0xF
        words = (c[..., 0::2] | (c[..., 1::2] << 4)).reshape(k // 512, 128, 2 * n)
    return np.ascontiguousarray(words), np.ascontiguousarray(byte.astype(np.uint8).reshape(k // 512, 16, n))


def unpack_weight(words, scales, fmt):
    g, _, n = scales.shape
    words = np.ascontiguousarray(words).reshape(g, 128, n, -1)
    if fmt == "e4m3":
        vals = words.view(ml_dtypes.float8_e4m3fn).astype(np.float64)
    else:
        nib = np.empty((g, 128, n, 4), np.uint8)
        nib[..., 0::2] = words & 0xF
        nib[..., 1::2] = words >> 4
        vals = E2M1[nib]
    vals = vals * np.repeat(np.exp2(scales.astype(np.float64) - 127.0), 8, axis=1)[..., None]
    return vals.transpose(0, 1, 3, 2).reshape(g * 512, n)


def gelu(v):
    return 0.5 * v * (1.0 + np.tanh(np.sqrt(2.0 / np.pi) * (v + 0.044715 * v**3)))


K, H, T, S, T2, S2, T3, P = 1024, 1024, 2048, 512, 1024, 1024, 2048, 512

def setup_inputs():
    n = np.random.standard_normal
    s = mx_kscale(K)[:, None]
    u = mx_kscale(H)[:, None]
    tab_words, tab_scales = pack_weight(n((K, T)) * s, "e4m3")
    tab2_words, tab2_scales = pack_weight(n((H, T3)) / np.sqrt(H) / u, "e4m3")
    w2_words, w2_scales = pack_weight(n((K, H)) / np.sqrt(K) / s, "e2m1")
    return {
        "tab_words": tab_words, "tab_scales": tab_scales,
        "tab2_words": tab2_words, "tab2_scales": tab2_scales,
        "w1": (n((K, H)) / np.sqrt(K) / s * u.T).astype(np.float32),
        "w2_words": w2_words, "w2_scales": w2_scales,
        "page0": (n((H, T2)) * u).astype(np.float32),
        "wgs": np.exp(0.3 * n((128, S))).astype(np.float32),
        "komi": n((S2, P)).astype(np.float32),
        "offs": striped(np.random.permutation(T)[:S]),
        "offs2": striped(np.random.permutation(T3)[:S2]),
        "offs3": striped(np.random.permutation(T2)[:S]),
        "offs4": striped(np.random.permutation(T2)[:P]),
    }

def reference(tab_words, tab_scales, tab2_words, tab2_scales, w1, w2_words, w2_scales, page0, wgs, komi, offs, offs2, offs3, offs4):
    v = unpack_weight(tab_words, tab_scales, "e4m3")[:, unstriped(offs)]
    v2 = unpack_weight(tab2_words, tab2_scales, "e4m3")[:, unstriped(offs2)]
    w2 = unpack_weight(w2_words, w2_scales, "e2m1")
    shape = mxq(f64(w1), 0, "e4m3").T @ v
    reach = w2.T @ v
    h = shape * reach
    page = f64(page0).copy()
    page[:, unstriped(offs3)] = np.tile(f64(wgs), (H // 128, 1)) * h
    e = v2.T @ mxq(page, 0, "e4m3")
    d = e[:, unstriped(offs4)] - f64(komi)
    return np.square(d)

@@ -1,0 +1,218 @@
+from contextlib import ExitStack
+
+import concourse.mybir as mybir
+
+K, H, T, S, T2, S2, T3, PICK = 1024, 1024, 2048, 512, 1024, 1024, 2048, 512
+FLOPS = 2 * (2 * K * H * S + H * S2 * T2)
+
+F32 = mybir.dt.float32
+BF16 = mybir.dt.bfloat16
+I32 = mybir.dt.int32
+U32 = mybir.dt.uint32
+U16 = mybir.dt.uint16
+U8 = mybir.dt.uint8
+FP8X4 = mybir.dt.float8_e4m3fn_x4
+FP4X4 = mybir.dt.float4_e2m1fn_x4
+MULT = mybir.AluOpType.mult
+SUB = mybir.AluOpType.subtract
+ACT = mybir.ActivationFunctionType
+
+P = 128
+PASS = 512
+
+
+def tile_list_joseki_lesson_gaps_kernel(tc, tab_words, tab_scales, tab2_words, tab2_scales, w1, w2_words,
+                                                  w2_scales, page0, wgs, komi, offs, offs2, offs3, offs4, out):
+    nc = tc.nc
+    with ExitStack() as ctx:
+        lists = ctx.enter_context(tc.tile_pool(name="lists", bufs=1))
+        keep = ctx.enter_context(tc.tile_pool(name="keep", bufs=1))
+        ring = ctx.enter_context(tc.tile_pool(name="ring", bufs=1))
+        psum = ctx.enter_context(tc.psum_pool(name="psum", bufs=8))
+
+        l1 = lists.tile([P, S // 16], U16, name="l1")
+        l2 = lists.tile([P, S2 // 16], U16, name="l2")
+        l3 = lists.tile([P, S // 16], U16, name="l3")
+        l4 = lists.tile([P, PICK // 16], U16, name="l4")
+
+        tab_s = keep.tile([P, 2, T], U8, name="tab_s", align_bytes=64)
+        w2_s_raw = keep.tile([P, 2, H], U8, name="w2_s_raw", align_bytes=64)
+        tab2_s = keep.tile([P, T3], U8, name="tab2_s", align_bytes=64)
+        nc.vector.memset(tab_s[:].bitcast(I32), 0)
+        nc.vector.memset(w2_s_raw[:].bitcast(I32), 0)
+        nc.vector.memset(tab2_s[:].bitcast(I32), 0)
+
+        def load_w1(a, h):
+            raw = ring.tile([P, 4, PASS], F32, name="w1_raw", tag="raw8k", bufs=4)
+            nc.sync.dma_start(out=raw[:], in_=w1[PASS * a:PASS * (a + 1), PASS * h:PASS * (h + 1)]
+                              .rearrange("(p j) c -> p j c", j=4))
+            return raw
+
+        def load_words(src, a, name):
+            t = keep.tile([P, T], I32, name=name, align_bytes=64)
+            nc.sync.dma_start(out=t[:], in_=src[a].rearrange("p t i -> p (t i)").bitcast(I32))
+            return t
+
+        def load_page(a, i):
+            t = ring.tile([P, T2], F32, name="page", tag="rows", bufs=8)
+            nc.sync.dma_start(out=t[:], in_=page0[PASS * a:PASS * (a + 1), :].rearrange("(p i) t -> p i t", i=4)[:, i, :])
+            return t
+
+        wgs_q = wgs.rearrange("(q i) j -> q i j", i=4)
+        wg0 = keep.tile([P, S], F32, name="wg0")
+        wg_rest = keep.tile([P, 3, S], F32, name="wg_rest")
+
+        nc.sync.dma_start(l1[:], offs)
+        w1_raw = {}
+        w1_raw[0, 0] = load_w1(0, 0)
+        for q in range(4):
+            nc.sync.dma_start(out=tab_s[32 * q:32 * q + 4, :, :].bitcast(I32),
+                                in_=tab_scales[:, 4 * q:4 * q + 4, :].rearrange("a r t -> r a t").bitcast(I32))
+        w1_raw[1, 0] = load_w1(1, 0)
+        for q in range(4):
+            nc.sync.dma_start(out=w2_s_raw[32 * q:32 * q + 4, :, :].bitcast(I32),
+                                in_=w2_scales[:, 4 * q:4 * q + 4, :].rearrange("a r t -> r a t").bitcast(I32))
+        w2_raw = keep.tile([P, 2, 2 * H], U8, name="w2_raw", align_bytes=64)
+        nc.sync.dma_start(out=w2_raw[:].bitcast(I32), in_=w2_words.rearrange("a p c -> p a c").bitcast(I32))
+        tab_w = [load_words(tab_words, a, "tab_w%d" % a) for a in range(2)]
+        nc.sync.dma_start(l3[:], offs3)
+        for q in range(4):
+            nc.sync.dma_start(out=wg0[32 * q:32 * q + 32, :], in_=wgs_q[:, 0, :])
+        page = {}
+        page[0] = load_page(0, 0)
+        for q in range(4):
+            nc.sync.dma_start(out=wg_rest[32 * q:32 * q + 32, :, :], in_=wgs_q[:, 1:4, :])
+        page[1] = load_page(0, 1)
+        w1_raw[0, 1] = load_w1(0, 1)
+        w1_raw[1, 1] = load_w1(1, 1)
+        for x in range(2, 8):
+            page[x] = load_page(x // 4, x % 4)
+        nc.sync.dma_start(l2[:], offs2)
+        nc.sync.dma_start(l4[:], offs4)
+        for q in range(4):
+            nc.sync.dma_start(out=tab2_s[32 * q:32 * q + 8, :].bitcast(I32),
+                              in_=tab2_scales[:, 4 * q:4 * q + 4, :].bitcast(I32))
+        tab2_w = [load_words(tab2_words, a, "tab2_w%d" % a) for a in range(2)]
+        komi_sb = []
+        for g in range(2):
+            kt = ring.tile([P, 4, PICK], F32, name="komi_sb", tag="raw8k", bufs=4)
+            nc.sync.dma_start(out=kt[:], in_=komi[PASS * g:PASS * (g + 1), :].rearrange("(n p) m -> p n m", p=P))
+            komi_sb.append(kt)
+
+        w1_c, w1_s = {}, {}
+
+        def quant_w1(a, h):
+            grouped = ring.tile([P, 4, P, 4], BF16, name="w1_grouped", bufs=2, align_bytes=64)
+            nc.scalar.activation(out=grouped[:].rearrange("p t m j -> p m j t"),
+                                 in_=w1_raw[a, h][:].rearrange("p j (m t) -> p m j t", t=4), func=ACT.Copy)
+            w1_c[a, h] = keep.tile([P, PASS], U32, name="w1_c%d%d" % (a, h), align_bytes=64)
+            w1_s[a, h] = keep.tile([P, PASS], U8, name="w1_s%d%d" % (a, h), align_bytes=64)
+            nc.vector.quantize_mx(out=w1_c[a, h][:].bitcast(FP8X4), scales=w1_s[a, h][:],
+                                  in_=grouped[:].rearrange("p t m j -> p (t m j)"))
+
+        quant_w1(0, 0)
+        v_s = []
+        for a in range(2):
+            vs = keep.tile([P, S], U8, name="v_s%d" % a, align_bytes=64)
+            nc.vector.tensor_copy(out=vs[:], in_=tab_s[:, a, :].indirect(l1[:]))
+            v_s.append(vs)
+        quant_w1(1, 0)
+        w2_p = keep.tile([P, 4, 4, 2 * P], U8, name="w2_p", align_bytes=64)
+        w2_sp = keep.tile([P, 4, 4, P], U8, name="w2_sp", align_bytes=64)
+        nc.vector.tensor_copy(out=w2_sp[:], in_=w2_s_raw[:].rearrange("p a (h m t) -> p (a h) t m", h=2, t=4))
+        nc.vector.tensor_copy(out=w2_p[:].bitcast(U16),
+                              in_=w2_raw[:].bitcast(U16).rearrange("p a (h m t) -> p (a h) t m", h=2, t=4))
+        v_w = []
+        for a in range(2):
+            vw = keep.tile([P, S], U32, name="v_w%d" % a, align_bytes=64)
+            nc.vector.tensor_copy(out=vw[:], in_=tab_w[a][:].bitcast(U32).indirect(l1[:]))
+            v_w.append(vw)
+
+        shape_sb, gated = {}, {}
+
+        def stage1(x):
+            h, i = x // 4, x % 4
+            cols = slice(P * i, P * (i + 1))
+            ps = psum.tile([P, S], F32, name="bank")
+            for a in range(2):
+                nc.tensor.matmul_mx(out=ps[:], lhsT=w1_c[a, h][:, cols].bitcast(FP8X4), lhsT_scale=w1_s[a, h][:, cols],
+                                    rhs=v_w[a][:].bitcast(FP8X4), rhs_scale=v_s[a][:], start=a == 0, stop=a == 1)
+            pr = psum.tile([P, S], F32, name="bank")
+            for a in range(2):
+                nc.tensor.matmul_mx(out=pr[:], lhsT=w2_p[:, 2 * a + h, i, :].bitcast(FP4X4),
+                                    lhsT_scale=w2_sp[:, 2 * a + h, i, :],
+                                    rhs=v_w[a][:].bitcast(FP8X4), rhs_scale=v_s[a][:], start=a == 0, stop=a == 1)
+            shape_sb[x] = ring.tile([P, S], F32, name="shape_sb", bufs=3)
+            nc.scalar.copy(out=shape_sb[x][:], in_=ps[:])
+            gated[x] = ring.tile([P, S], F32, name="gated", bufs=2)
+            wg = wg0[:] if i == 0 else wg_rest[:, i - 1, :]
+            nc.vector.tensor_tensor(out=gated[x][:], in0=pr[:], in1=wg, op=MULT)
+
+        def scatter(x):
+            nc.vector.tensor_tensor(out=page[x][:].indirect(l3[:]), in0=shape_sb[x][:], in1=gated[x][:], op=MULT)
+
+        pairs = {}
+        for a in range(2):
+            for c in range(2):
+                pairs[a, c] = keep.tile([P, 2, PASS, 2], BF16, name="pairs%d%d" % (a, c), align_bytes=64)
+
+        def cast(x, c):
+            a, i = x // 4, x % 4
+            nc.scalar.copy(out=pairs[a, c][:, i // 2, :, i % 2], in_=page[x][:, PASS * c:PASS * (c + 1)])
+
+        pg_c, pg_s = {}, {}
+
+        def quant_page(a, c):
+            grouped = ring.tile([P, PASS, 4], BF16, name="pg_grouped", bufs=2, align_bytes=64)
+            nc.scalar.copy(out=grouped[:].bitcast(F32),
+                           in_=pairs[a, c][:].rearrange("p u t e -> p (u t e)").bitcast(F32).rearrange("p (u t) -> p t u", u=2))
+            pg_c[a, c] = keep.tile([P, PASS], U32, name="pg_c%d%d" % (a, c), align_bytes=64)
+            pg_s[a, c] = keep.tile([P, PASS], U8, name="pg_s%d%d" % (a, c), align_bytes=64)
+            nc.vector.quantize_mx(out=pg_c[a, c][:].bitcast(FP8X4), scales=pg_s[a, c][:],
+                                  in_=grouped[:].rearrange("p t i -> p (t i)"))
+
+        v2_w = [keep.tile([P, S2], U32, name="v2_w%d" % a, align_bytes=64) for a in range(2)]
+        v2_s = keep.tile([P, S2], U8, name="v2_s", align_bytes=64)
+
+        def gather_v2(n0, n1):
+            sl = l2[:, n0 // 16:n1 // 16]
+            nc.vector.tensor_copy(out=v2_s[:, n0:n1], in_=tab2_s[:].indirect(sl))
+            for a in range(2):
+                nc.vector.tensor_copy(out=v2_w[a][:, n0:n1], in_=tab2_w[a][:].bitcast(U32).indirect(sl))
+
+        stage1(0)
+        for x in range(8):
+            if x + 1 < 8:
+                if x + 1 == 2:
+                    quant_w1(0, 1)
+                if x + 1 == 3:
+                    quant_w1(1, 1)
+                stage1(x + 1)
+            scatter(x)
+            if x == 7:
+                gather_v2(0, 256)
+            for c in range(2):
+                cast(x, c)
+                if x == 7:
+                    quant_page(1, c)
+                    gather_v2(256 + 256 * c, 512 + 512 * c)
+            if x == 4:
+                quant_page(0, 0)
+            if x == 5:
+                quant_page(0, 1)
+
+        for n in range(8):
+            cols = slice(P * n, P * (n + 1))
+            e_sb = ring.tile([P, T2], F32, name="e_sb", tag="rows", bufs=8)
+            for c in range(2):
+                pe = psum.tile([P, PASS], F32, name="bank")
+                for a in range(2):
+                    nc.tensor.matmul_mx(out=pe[:], lhsT=v2_w[a][:, cols].bitcast(FP8X4), lhsT_scale=v2_s[4 * a:P, cols],
+                                        rhs=pg_c[a, c][:].bitcast(FP8X4), rhs_scale=pg_s[a, c][:],
+                                        start=a == 0, stop=a == 1)
+                nc.scalar.copy(out=e_sb[:, PASS * c:PASS * (c + 1)], in_=pe[:])
+            gap = ring.tile([P, PICK], F32, name="gap", bufs=3)
+            nc.vector.tensor_tensor(out=gap[:], in0=e_sb[:].indirect(l4[:]), in1=komi_sb[n // 4][:, n % 4, :], op=SUB)
+            sq = ring.tile([P, PICK], F32, name="sq", bufs=3)
+            nc.scalar.activation(out=sq[:], in_=gap[:], func=ACT.Square)
+            nc.sync.dma_start(out=out[cols, :], in_=sq[:])

@@ -1,6 +1,7 @@
 from contextlib import ExitStack
 
 import concourse.mybir as mybir
+from concourse.masks import make_identity
 
 K, H, T, S, T2, S2, T3, PICK = 1024, 1024, 2048, 512, 1024, 1024, 2048, 512
 FLOPS = 2 * (2 * K * H * S + H * S2 * T2)
@@ -28,7 +29,7 @@ def tile_list_joseki_lesson_gaps_kernel(tc, tab_words, tab_scales, tab2_words, t
         lists = ctx.enter_context(tc.tile_pool(name="lists", bufs=1))
         keep = ctx.enter_context(tc.tile_pool(name="keep", bufs=1))
         ring = ctx.enter_context(tc.tile_pool(name="ring", bufs=1))
-        psum = ctx.enter_context(tc.psum_pool(name="psum", bufs=8))
+        psum = ctx.enter_context(tc.psum_pool(name="psum", bufs=4))
 
         l1 = lists.tile([P, S // 16], U16, name="l1")
         l2 = lists.tile([P, S2 // 16], U16, name="l2")
@@ -43,7 +44,7 @@ def tile_list_joseki_lesson_gaps_kernel(tc, tab_words, tab_scales, tab2_words, t
         nc.vector.memset(tab2_s[:].bitcast(I32), 0)
 
         def load_w1(a, h):
-            raw = ring.tile([P, 4, PASS], F32, name="w1_raw", tag="raw8k", bufs=4)
+            raw = ring.tile([P, 4, PASS], F32, name="w1_raw", tag="raw%d%d" % (a, h), bufs=1)
             nc.sync.dma_start(out=raw[:], in_=w1[PASS * a:PASS * (a + 1), PASS * h:PASS * (h + 1)]
                               .rearrange("(p j) c -> p j c", j=4))
             return raw
@@ -58,161 +59,220 @@ def tile_list_joseki_lesson_gaps_kernel(tc, tab_words, tab_scales, tab2_words, t
             nc.sync.dma_start(out=t[:], in_=page0[PASS * a:PASS * (a + 1), :].rearrange("(p i) t -> p i t", i=4)[:, i, :])
             return t
 
-        wgs_q = wgs.rearrange("(q i) j -> q i j", i=4)
-        wg0 = keep.tile([P, S], F32, name="wg0")
-        wg_rest = keep.tile([P, 3, S], F32, name="wg_rest")
+        def load_komi(g):
+            kt = ring.tile([P, 4, PICK], F32, name="komi_sb", tag=("raw00", "raw01")[g], bufs=1)
+            nc.sync.dma_start(out=kt[:], in_=komi[PASS * g:PASS * (g + 1), :].rearrange("(n p) m -> p n m", p=P))
+            return kt
 
         nc.sync.dma_start(l1[:], offs)
-        w1_raw = {}
-        w1_raw[0, 0] = load_w1(0, 0)
-        for q in range(4):
-            nc.sync.dma_start(out=tab_s[32 * q:32 * q + 4, :, :].bitcast(I32),
-                                in_=tab_scales[:, 4 * q:4 * q + 4, :].rearrange("a r t -> r a t").bitcast(I32))
-        w1_raw[1, 0] = load_w1(1, 0)
-        for q in range(4):
-            nc.sync.dma_start(out=w2_s_raw[32 * q:32 * q + 4, :, :].bitcast(I32),
-                                in_=w2_scales[:, 4 * q:4 * q + 4, :].rearrange("a r t -> r a t").bitcast(I32))
+        wgs_sb = keep.tile([P, S], F32, name="wgs_sb")
+        nc.sync.dma_start(out=wgs_sb[:], in_=wgs)
         w2_raw = keep.tile([P, 2, 2 * H], U8, name="w2_raw", align_bytes=64)
         nc.sync.dma_start(out=w2_raw[:].bitcast(I32), in_=w2_words.rearrange("a p c -> p a c").bitcast(I32))
-        tab_w = [load_words(tab_words, a, "tab_w%d" % a) for a in range(2)]
+        for q in range(4):
+            nc.sync.dma_start(out=tab_s[32 * q:32 * q + 4, :, :].bitcast(I32),
+                              in_=tab_scales[:, 4 * q:4 * q + 4, :].rearrange("a r t -> r a t").bitcast(I32))
+        tab_w = [load_words(tab_words, 0, "tab_w0")]
+        for q in range(4):
+            nc.sync.dma_start(out=w2_s_raw[32 * q:32 * q + 4, :, :].bitcast(I32),
+                              in_=w2_scales[:, 4 * q:4 * q + 4, :].rearrange("a r t -> r a t").bitcast(I32))
+        w1_raw = {}
+        w1_raw[0, 0] = load_w1(0, 0)
         nc.sync.dma_start(l3[:], offs3)
-        for q in range(4):
-            nc.sync.dma_start(out=wg0[32 * q:32 * q + 32, :], in_=wgs_q[:, 0, :])
-        page = {}
-        page[0] = load_page(0, 0)
-        for q in range(4):
-            nc.sync.dma_start(out=wg_rest[32 * q:32 * q + 32, :, :], in_=wgs_q[:, 1:4, :])
-        page[1] = load_page(0, 1)
-        w1_raw[0, 1] = load_w1(0, 1)
-        w1_raw[1, 1] = load_w1(1, 1)
-        for x in range(2, 8):
-            page[x] = load_page(x // 4, x % 4)
         nc.sync.dma_start(l2[:], offs2)
-        nc.sync.dma_start(l4[:], offs4)
         for q in range(4):
             nc.sync.dma_start(out=tab2_s[32 * q:32 * q + 8, :].bitcast(I32),
                               in_=tab2_scales[:, 4 * q:4 * q + 4, :].bitcast(I32))
+        w1_raw[1, 0] = load_w1(1, 0)
+        tab_w.append(load_words(tab_words, 1, "tab_w1"))
+        page = {}
+        page[0] = load_page(0, 0)
+        page[1] = load_page(0, 1)
+        w1_raw[0, 1] = load_w1(0, 1)
+        w1_raw[1, 1] = load_w1(1, 1)
+        page[2] = load_page(0, 2)
+        komi_sb = [load_komi(0)]
+        for x in range(3, 7):
+            page[x] = load_page(x // 4, x % 4)
+        nc.sync.dma_start(l4[:], offs4)
         tab2_w = [load_words(tab2_words, a, "tab2_w%d" % a) for a in range(2)]
-        komi_sb = []
-        for g in range(2):
-            kt = ring.tile([P, 4, PICK], F32, name="komi_sb", tag="raw8k", bufs=4)
-            nc.sync.dma_start(out=kt[:], in_=komi[PASS * g:PASS * (g + 1), :].rearrange("(n p) m -> p n m", p=P))
-            komi_sb.append(kt)
+        page[7] = load_page(1, 3)
+        komi_sb.append(load_komi(1))
 
-        w1_c, w1_s = {}, {}
+        ident = keep.tile([P, P], F32, name="ident")
+        make_identity(nc, ident[:])
+        wgs_t_ps = psum.tile([P, 4, P], F32, name="wgs_t_ps", tag="bank_a")
+        for b in range(4):
+            nc.tensor.transpose(wgs_t_ps[:, b, :], wgs_sb[:, P * b:P * (b + 1)], ident[:])
+        wgs_t = keep.tile([P, 4, 4, 4, 32], F32, name="wgs_t")
+        nc.scalar.copy(out=wgs_t[:],
+                       in_=wgs_t_ps[:].rearrange("j b (q i) -> j b i q", i=4).unsqueeze(3).to_broadcast([P, 4, 4, 4, 32]))
+        wg_first = keep.tile([P, S], F32, name="wg_first")
+        wg_ps = []
+        for i in range(4):
+            bank = psum.tile([P, 4, P], F32, name="wg_ps", tag="bank_b")
+            for b in range(4):
+                nc.tensor.transpose(bank[:, b, :], wgs_t[:, b, i, :, :].rearrange("j g q -> j (g q)"), ident[:])
+            wg_ps.append(bank[:].rearrange("p b j -> p (b j)"))
+        nc.scalar.copy(out=wg_first[:], in_=wg_ps[0])
 
-        def quant_w1(a, h):
-            grouped = ring.tile([P, 4, P, 4], BF16, name="w1_grouped", bufs=2, align_bytes=64)
+        w1_q = {}
+
+        def quant_w1(a, h, t0, t1, tag, codes_tag=None):
+            nt = t1 - t0
+            grouped = ring.tile([P, nt, P, 4], BF16, name="w1_grouped", tag=tag, bufs=1, align_bytes=64)
             nc.scalar.activation(out=grouped[:].rearrange("p t m j -> p m j t"),
-                                 in_=w1_raw[a, h][:].rearrange("p j (m t) -> p m j t", t=4), func=ACT.Copy)
-            w1_c[a, h] = keep.tile([P, PASS], U32, name="w1_c%d%d" % (a, h), align_bytes=64)
-            w1_s[a, h] = keep.tile([P, PASS], U8, name="w1_s%d%d" % (a, h), align_bytes=64)
-            nc.vector.quantize_mx(out=w1_c[a, h][:].bitcast(FP8X4), scales=w1_s[a, h][:],
+                                 in_=w1_raw[a, h][:].rearrange("p j (m t) -> p m j t", t=4)[:, :, :, t0:t1], func=ACT.Copy)
+            codes = keep.tile([P, nt * P], U32, name="w1_c", tag=codes_tag or "w1_c%d%d" % (a, h), align_bytes=64)
+            scales = keep.tile([P, nt * P], U8, name="w1_s%d%d%d" % (a, h, t0), align_bytes=64)
+            nc.vector.quantize_mx(out=codes[:].bitcast(FP8X4), scales=scales[:],
                                   in_=grouped[:].rearrange("p t m j -> p (t m j)"))
+            for t in range(t0, t1):
+                cols = slice(P * (t - t0), P * (t - t0 + 1))
+                w1_q[a, h, t] = (codes[:, cols].bitcast(FP8X4), scales[:, cols])
 
-        quant_w1(0, 0)
-        v_s = []
+        v2 = {}
+
+        def gather_v2(kind, n0, n1, tag):
+            window = tab2_s[:] if kind == "s" else tab2_w[kind][:].bitcast(U32)
+            t = ring.tile([P, n1 - n0], U8 if kind == "s" else U32, name="v2", tag=tag, bufs=1, align_bytes=64)
+            nc.vector.tensor_copy(out=t[:], in_=window.indirect(l2[:, n0 // 16:n1 // 16]))
+            for n in range(n0 // P, n1 // P):
+                v2[kind, n] = (t, slice(P * n - n0, P * (n + 1) - n0))
+
+        w2_p = keep.tile([P, 4, 4, 2 * P], U8, name="w2_p", align_bytes=64)
+        w2_sp = keep.tile([P, 4, 4, P], U8, name="w2_sp", align_bytes=64)
+        nc.vector.tensor_copy(out=w2_p[:].bitcast(U16),
+                              in_=w2_raw[:].bitcast(U16).rearrange("p a (h m t) -> p (a h) t m", h=2, t=4))
+        v_s, v_w = [], []
         for a in range(2):
             vs = keep.tile([P, S], U8, name="v_s%d" % a, align_bytes=64)
             nc.vector.tensor_copy(out=vs[:], in_=tab_s[:, a, :].indirect(l1[:]))
             v_s.append(vs)
-        quant_w1(1, 0)
-        w2_p = keep.tile([P, 4, 4, 2 * P], U8, name="w2_p", align_bytes=64)
-        w2_sp = keep.tile([P, 4, 4, P], U8, name="w2_sp", align_bytes=64)
-        nc.vector.tensor_copy(out=w2_sp[:], in_=w2_s_raw[:].rearrange("p a (h m t) -> p (a h) t m", h=2, t=4))
-        nc.vector.tensor_copy(out=w2_p[:].bitcast(U16),
-                              in_=w2_raw[:].bitcast(U16).rearrange("p a (h m t) -> p (a h) t m", h=2, t=4))
-        v_w = []
-        for a in range(2):
+
+        def gather_v(a):
             vw = keep.tile([P, S], U32, name="v_w%d" % a, align_bytes=64)
             nc.vector.tensor_copy(out=vw[:], in_=tab_w[a][:].bitcast(U32).indirect(l1[:]))
             v_w.append(vw)
+
+        gather_v(0)
+        nc.vector.tensor_copy(out=w2_sp[:], in_=w2_s_raw[:].rearrange("p a (h m t) -> p (a h) t m", h=2, t=4))
+        quant_w1(0, 0, 0, 4, "half0")
+        gather_v2("s", 0, 512, "v2a")
+        quant_w1(1, 0, 0, 2, "half1")
+        gather_v(1)
+        quant_w1(1, 0, 2, 4, "quarter", "tab_w1")
+        gather_v2("s", 512, 1024, "quarter")
+        wg_rest = ring.tile([P, 3, S], F32, name="wg_rest", tag="raw10", bufs=1)
+        for i in range(1, 4):
+            nc.scalar.copy(out=wg_rest[:, i - 1, :], in_=wg_ps[i])
+        wg = [wg_first[:]] + [wg_rest[:, i, :] for i in range(3)]
 
         shape_sb, gated = {}, {}
 
         def stage1(x):
             h, i = x // 4, x % 4
-            cols = slice(P * i, P * (i + 1))
-            ps = psum.tile([P, S], F32, name="bank")
+            ps = psum.tile([P, S], F32, name="bank", tag="bank_a")
+            pr = psum.tile([P, S], F32, name="bank", tag="bank_a")
             for a in range(2):
-                nc.tensor.matmul_mx(out=ps[:], lhsT=w1_c[a, h][:, cols].bitcast(FP8X4), lhsT_scale=w1_s[a, h][:, cols],
+                nc.tensor.matmul_mx(out=ps[:], lhsT=w1_q[a, h, i][0], lhsT_scale=w1_q[a, h, i][1],
                                     rhs=v_w[a][:].bitcast(FP8X4), rhs_scale=v_s[a][:], start=a == 0, stop=a == 1)
-            pr = psum.tile([P, S], F32, name="bank")
-            for a in range(2):
                 nc.tensor.matmul_mx(out=pr[:], lhsT=w2_p[:, 2 * a + h, i, :].bitcast(FP4X4),
                                     lhsT_scale=w2_sp[:, 2 * a + h, i, :],
                                     rhs=v_w[a][:].bitcast(FP8X4), rhs_scale=v_s[a][:], start=a == 0, stop=a == 1)
-            shape_sb[x] = ring.tile([P, S], F32, name="shape_sb", bufs=3)
+            if x < 7:
+                shape_sb[x] = ring.tile([P, S], F32, name="shape_sb", bufs=4)
+            else:
+                shape_sb[x] = ring.tile([P, S], F32, name="shape_last", tag="last", bufs=1, align_bytes=64)
             nc.scalar.copy(out=shape_sb[x][:], in_=ps[:])
             gated[x] = ring.tile([P, S], F32, name="gated", bufs=2)
-            wg = wg0[:] if i == 0 else wg_rest[:, i - 1, :]
-            nc.vector.tensor_tensor(out=gated[x][:], in0=pr[:], in1=wg, op=MULT)
+            nc.vector.tensor_tensor(out=gated[x][:], in0=pr[:], in1=wg[i], op=MULT)
 
         def scatter(x):
             nc.vector.tensor_tensor(out=page[x][:].indirect(l3[:]), in0=shape_sb[x][:], in1=gated[x][:], op=MULT)
 
         pairs = {}
-        for a in range(2):
-            for c in range(2):
-                pairs[a, c] = keep.tile([P, 2, PASS, 2], BF16, name="pairs%d%d" % (a, c), align_bytes=64)
 
         def cast(x, c):
             a, i = x // 4, x % 4
+            if i == 0:
+                pairs[a, c] = ring.tile([P, 2, PASS, 2], BF16, name="pairs", tag=("half%d" if a == 0 else "pairs%d") % c,
+                                        bufs=1, align_bytes=64)
             nc.scalar.copy(out=pairs[a, c][:, i // 2, :, i % 2], in_=page[x][:, PASS * c:PASS * (c + 1)])
 
-        pg_c, pg_s = {}, {}
+        pg_g, pg_c, pg_s = {}, {}, {}
+
+        def weave_page(a, c):
+            grouped = ring.tile([P, PASS, 4], BF16, name="pg_grouped", tag="pg%d" % c, bufs=1, align_bytes=64)
+            weave = nc.scalar.copy if a == 0 else nc.vector.tensor_copy
+            weave(out=grouped[:].bitcast(F32),
+                  in_=pairs[a, c][:].rearrange("p u t e -> p (u t e)").bitcast(F32).rearrange("p (u t) -> p t u", u=2))
+            pg_g[a, c] = grouped
 
         def quant_page(a, c):
-            grouped = ring.tile([P, PASS, 4], BF16, name="pg_grouped", bufs=2, align_bytes=64)
-            nc.scalar.copy(out=grouped[:].bitcast(F32),
-                           in_=pairs[a, c][:].rearrange("p u t e -> p (u t e)").bitcast(F32).rearrange("p (u t) -> p t u", u=2))
+            grouped = pg_g[a, c]
             pg_c[a, c] = keep.tile([P, PASS], U32, name="pg_c%d%d" % (a, c), align_bytes=64)
             pg_s[a, c] = keep.tile([P, PASS], U8, name="pg_s%d%d" % (a, c), align_bytes=64)
             nc.vector.quantize_mx(out=pg_c[a, c][:].bitcast(FP8X4), scales=pg_s[a, c][:],
                                   in_=grouped[:].rearrange("p t i -> p (t i)"))
 
-        v2_w = [keep.tile([P, S2], U32, name="v2_w%d" % a, align_bytes=64) for a in range(2)]
-        v2_s = keep.tile([P, S2], U8, name="v2_s", align_bytes=64)
-
-        def gather_v2(n0, n1):
-            sl = l2[:, n0 // 16:n1 // 16]
-            nc.vector.tensor_copy(out=v2_s[:, n0:n1], in_=tab2_s[:].indirect(sl))
-            for a in range(2):
-                nc.vector.tensor_copy(out=v2_w[a][:, n0:n1], in_=tab2_w[a][:].bitcast(U32).indirect(sl))
-
         stage1(0)
+        stage1(1)
         for x in range(8):
-            if x + 1 < 8:
-                if x + 1 == 2:
-                    quant_w1(0, 1)
-                if x + 1 == 3:
-                    quant_w1(1, 1)
-                stage1(x + 1)
+            if x + 2 < 8:
+                stage1(x + 2)
             scatter(x)
-            if x == 7:
-                gather_v2(0, 256)
-            for c in range(2):
-                cast(x, c)
-                if x == 7:
-                    quant_page(1, c)
-                    gather_v2(256 + 256 * c, 512 + 512 * c)
-            if x == 4:
-                quant_page(0, 0)
+            if x == 1:
+                quant_w1(0, 1, 0, 4, "half0")
+                quant_w1(1, 1, 0, 4, "half1")
+            if x == 3:
+                for y in range(3):
+                    cast(y, 0)
+                    cast(y, 1)
             if x == 5:
-                quant_page(0, 1)
+                gather_v2(0, 0, 256, "v2b")
+                gather_v2(1, 0, 256, "v2c")
+            if x == 7:
+                gather_v2(1, 256, 512, "last")
+            if x >= 3:
+                cast(x, 0)
+                cast(x, 1)
+            if x in (4, 5):
+                weave_page(0, x - 4)
+                quant_page(0, x - 4)
+        weave_page(1, 0)
+        weave_page(1, 1)
+        quant_page(1, 0)
+        quant_page(1, 1)
+        gather_v2(0, 256, 512, "pairs1")
+        gather_v2(0, 512, 1024, "pg0")
+        gather_v2(1, 512, 1024, "pg1")
 
-        for n in range(8):
-            cols = slice(P * n, P * (n + 1))
-            e_sb = ring.tile([P, T2], F32, name="e_sb", tag="rows", bufs=8)
+        e_sb = {}
+
+        def scores(n):
+            e_sb[n] = ring.tile([P, T2], F32, name="e_sb", tag="rows", bufs=8)
             for c in range(2):
-                pe = psum.tile([P, PASS], F32, name="bank")
+                pe = psum.tile([P, PASS], F32, name="bank", tag="bank_b" if n % 2 == 0 else "bank_a")
                 for a in range(2):
-                    nc.tensor.matmul_mx(out=pe[:], lhsT=v2_w[a][:, cols].bitcast(FP8X4), lhsT_scale=v2_s[4 * a:P, cols],
+                    wt, wc = v2[a, n]
+                    st, sc = v2["s", n]
+                    nc.tensor.matmul_mx(out=pe[:], lhsT=wt[:, wc].bitcast(FP8X4), lhsT_scale=st[4 * a:P, sc],
                                         rhs=pg_c[a, c][:].bitcast(FP8X4), rhs_scale=pg_s[a, c][:],
                                         start=a == 0, stop=a == 1)
-                nc.scalar.copy(out=e_sb[:, PASS * c:PASS * (c + 1)], in_=pe[:])
-            gap = ring.tile([P, PICK], F32, name="gap", bufs=3)
-            nc.vector.tensor_tensor(out=gap[:], in0=e_sb[:].indirect(l4[:]), in1=komi_sb[n // 4][:, n % 4, :], op=SUB)
-            sq = ring.tile([P, PICK], F32, name="sq", bufs=3)
-            nc.scalar.activation(out=sq[:], in_=gap[:], func=ACT.Square)
-            nc.sync.dma_start(out=out[cols, :], in_=sq[:])
+                nc.scalar.copy(out=e_sb[n][:, PASS * c:PASS * (c + 1)], in_=pe[:])
+
+        scores(0)
+        scores(1)
+        for n in range(8):
+            if n + 2 < 8:
+                scores(n + 2)
+            for m0, m1 in ([(0, PICK)] if n < 7 else [(0, PICK // 2), (PICK // 2, PICK)]):
+                gap = ring.tile([P, m1 - m0], F32, name="gap", bufs=9)
+                nc.vector.tensor_tensor(out=gap[:], in0=e_sb[n][:].indirect(l4[:, m0 // 16:m1 // 16]),
+                                        in1=komi_sb[n // 4][:, n % 4, m0:m1], op=SUB)
+                if n < 2:
+                    nc.vector.tensor_tensor(out=gap[:], in0=gap[:], in1=gap[:], op=MULT)
+                else:
+                    nc.scalar.activation(out=gap[:], in_=gap[:], func=ACT.Square)
+                nc.sync.dma_start(out=out[P * n:P * (n + 1), m0:m1], in_=gap[:])

@@ -20,6 +20,10 @@ ACT = mybir.ActivationFunctionType
 
 P = 128
 PASS = 512
+ROW_TILES = 8
+MOVE_TILES = S2 // P
+SHAPE_BUFS = 4
+SQUARES_ON_VECTOR = 2
 
 
 def tile_list_joseki_lesson_gaps_kernel(tc, tab_words, tab_scales, tab2_words, tab2_scales, w1, w2_words,
@@ -31,10 +35,10 @@ def tile_list_joseki_lesson_gaps_kernel(tc, tab_words, tab_scales, tab2_words, t
         ring = ctx.enter_context(tc.tile_pool(name="ring", bufs=1))
         psum = ctx.enter_context(tc.psum_pool(name="psum", bufs=4))
 
-        l1 = lists.tile([P, S // 16], U16, name="l1")
-        l2 = lists.tile([P, S2 // 16], U16, name="l2")
-        l3 = lists.tile([P, S // 16], U16, name="l3")
-        l4 = lists.tile([P, PICK // 16], U16, name="l4")
+        corners = lists.tile([P, S // 16], U16, name="corners")
+        moves = lists.tile([P, S2 // 16], U16, name="moves")
+        edited = lists.tile([P, S // 16], U16, name="edited")
+        open_lessons = lists.tile([P, PICK // 16], U16, name="open_lessons")
 
         tab_s = keep.tile([P, 2, T], U8, name="tab_s", align_bytes=64)
         w2_s_raw = keep.tile([P, 2, H], U8, name="w2_s_raw", align_bytes=64)
@@ -50,21 +54,23 @@ def tile_list_joseki_lesson_gaps_kernel(tc, tab_words, tab_scales, tab2_words, t
             return raw
 
         def load_words(src, a, name):
-            t = keep.tile([P, T], I32, name=name, align_bytes=64)
-            nc.sync.dma_start(out=t[:], in_=src[a].rearrange("p t i -> p (t i)").bitcast(I32))
-            return t
+            words = keep.tile([P, T], I32, name=name, align_bytes=64)
+            nc.sync.dma_start(out=words[:], in_=src[a].rearrange("p t i -> p (t i)").bitcast(I32))
+            return words
 
-        def load_page(a, i):
-            t = ring.tile([P, T2], F32, name="page", tag="rows", bufs=8)
-            nc.sync.dma_start(out=t[:], in_=page0[PASS * a:PASS * (a + 1), :].rearrange("(p i) t -> p i t", i=4)[:, i, :])
-            return t
+        def load_page(x):
+            h, i = x // 4, x % 4
+            rows = ring.tile([P, T2], F32, name="page", tag="rows", bufs=ROW_TILES)
+            nc.sync.dma_start(out=rows[:],
+                              in_=page0[PASS * h:PASS * (h + 1), :].rearrange("(p i) t -> p i t", i=4)[:, i, :])
+            return rows
 
         def load_komi(g):
-            kt = ring.tile([P, 4, PICK], F32, name="komi_sb", tag=("raw00", "raw01")[g], bufs=1)
-            nc.sync.dma_start(out=kt[:], in_=komi[PASS * g:PASS * (g + 1), :].rearrange("(n p) m -> p n m", p=P))
-            return kt
+            rows = ring.tile([P, 4, PICK], F32, name="komi_sb", tag=("raw00", "raw01")[g], bufs=1)
+            nc.sync.dma_start(out=rows[:], in_=komi[PASS * g:PASS * (g + 1), :].rearrange("(c p) m -> p c m", p=P))
+            return rows
 
-        nc.sync.dma_start(l1[:], offs)
+        nc.sync.dma_start(corners[:], offs)
         wgs_sb = keep.tile([P, S], F32, name="wgs_sb")
         nc.sync.dma_start(out=wgs_sb[:], in_=wgs)
         w2_raw = keep.tile([P, 2, 2 * H], U8, name="w2_raw", align_bytes=64)
@@ -78,25 +84,24 @@ def tile_list_joseki_lesson_gaps_kernel(tc, tab_words, tab_scales, tab2_words, t
                               in_=w2_scales[:, 4 * q:4 * q + 4, :].rearrange("a r t -> r a t").bitcast(I32))
         w1_raw = {}
         w1_raw[0, 0] = load_w1(0, 0)
-        nc.sync.dma_start(l3[:], offs3)
-        nc.sync.dma_start(l2[:], offs2)
+        nc.sync.dma_start(edited[:], offs3)
+        nc.sync.dma_start(moves[:], offs2)
         for q in range(4):
             nc.sync.dma_start(out=tab2_s[32 * q:32 * q + 8, :].bitcast(I32),
                               in_=tab2_scales[:, 4 * q:4 * q + 4, :].bitcast(I32))
         w1_raw[1, 0] = load_w1(1, 0)
         tab_w.append(load_words(tab_words, 1, "tab_w1"))
         page = {}
-        page[0] = load_page(0, 0)
-        page[1] = load_page(0, 1)
+        page[0] = load_page(0)
+        page[1] = load_page(1)
         w1_raw[0, 1] = load_w1(0, 1)
         w1_raw[1, 1] = load_w1(1, 1)
-        page[2] = load_page(0, 2)
         komi_sb = [load_komi(0)]
-        for x in range(3, 7):
-            page[x] = load_page(x // 4, x % 4)
-        nc.sync.dma_start(l4[:], offs4)
+        for x in range(2, ROW_TILES - 1):
+            page[x] = load_page(x)
+        nc.sync.dma_start(open_lessons[:], offs4)
         tab2_w = [load_words(tab2_words, a, "tab2_w%d" % a) for a in range(2)]
-        page[7] = load_page(1, 3)
+        page[ROW_TILES - 1] = load_page(ROW_TILES - 1)
         komi_sb.append(load_komi(1))
 
         ident = keep.tile([P, P], F32, name="ident")
@@ -110,130 +115,137 @@ def tile_list_joseki_lesson_gaps_kernel(tc, tab_words, tab_scales, tab2_words, t
         wg_first = keep.tile([P, S], F32, name="wg_first")
         wg_ps = []
         for i in range(4):
-            bank = psum.tile([P, 4, P], F32, name="wg_ps", tag="bank_b")
+            wg_bank = psum.tile([P, 4, P], F32, name="wg_bank", tag="bank_b")
             for b in range(4):
-                nc.tensor.transpose(bank[:, b, :], wgs_t[:, b, i, :, :].rearrange("j g q -> j (g q)"), ident[:])
-            wg_ps.append(bank[:].rearrange("p b j -> p (b j)"))
+                nc.tensor.transpose(wg_bank[:, b, :], wgs_t[:, b, i, :, :].rearrange("j g q -> j (g q)"), ident[:])
+            wg_ps.append(wg_bank[:].rearrange("p b j -> p (b j)"))
         nc.scalar.copy(out=wg_first[:], in_=wg_ps[0])
 
         w1_q = {}
 
-        def quant_w1(a, h, t0, t1, tag, codes_tag=None):
-            nt = t1 - t0
-            grouped = ring.tile([P, nt, P, 4], BF16, name="w1_grouped", tag=tag, bufs=1, align_bytes=64)
-            nc.scalar.activation(out=grouped[:].rearrange("p t m j -> p m j t"),
-                                 in_=w1_raw[a, h][:].rearrange("p j (m t) -> p m j t", t=4)[:, :, :, t0:t1], func=ACT.Copy)
-            codes = keep.tile([P, nt * P], U32, name="w1_c", tag=codes_tag or "w1_c%d%d" % (a, h), align_bytes=64)
-            scales = keep.tile([P, nt * P], U8, name="w1_s%d%d%d" % (a, h, t0), align_bytes=64)
+        def quant_w1(a, h, i0, i1, tag, codes_tag):
+            count = i1 - i0
+            grouped = ring.tile([P, count, P, 4], BF16, name="w1_grouped", tag=tag, bufs=1, align_bytes=64)
+            nc.scalar.activation(out=grouped[:].rearrange("p i m j -> p m j i"),
+                                 in_=w1_raw[a, h][:].rearrange("p j (m i) -> p m j i", i=4)[:, :, :, i0:i1],
+                                 func=ACT.Copy)
+            codes = keep.tile([P, count * P], U32, name="w1_c", tag=codes_tag, align_bytes=64)
+            scales = keep.tile([P, count * P], U8, name="w1_s%d%d%d" % (a, h, i0), align_bytes=64)
             nc.vector.quantize_mx(out=codes[:].bitcast(FP8X4), scales=scales[:],
-                                  in_=grouped[:].rearrange("p t m j -> p (t m j)"))
-            for t in range(t0, t1):
-                cols = slice(P * (t - t0), P * (t - t0 + 1))
-                w1_q[a, h, t] = (codes[:, cols].bitcast(FP8X4), scales[:, cols])
+                                  in_=grouped[:].rearrange("p i m j -> p (i m j)"))
+            for i in range(i0, i1):
+                cols = slice(P * (i - i0), P * (i - i0 + 1))
+                w1_q[a, h, i] = (codes[:, cols].bitcast(FP8X4), scales[:, cols])
 
         v2 = {}
 
-        def gather_v2(kind, n0, n1, tag):
-            window = tab2_s[:] if kind == "s" else tab2_w[kind][:].bitcast(U32)
-            t = ring.tile([P, n1 - n0], U8 if kind == "s" else U32, name="v2", tag=tag, bufs=1, align_bytes=64)
-            nc.vector.tensor_copy(out=t[:], in_=window.indirect(l2[:, n0 // 16:n1 // 16]))
+        def gather_v2(part, n0, n1, tag):
+            window = tab2_s[:] if part == "scales" else tab2_w[part][:].bitcast(U32)
+            picked = ring.tile([P, n1 - n0], U8 if part == "scales" else U32, name="v2", tag=tag, bufs=1, align_bytes=64)
+            nc.vector.tensor_copy(out=picked[:], in_=window.indirect(moves[:, n0 // 16:n1 // 16]))
             for n in range(n0 // P, n1 // P):
-                v2[kind, n] = (t, slice(P * n - n0, P * (n + 1) - n0))
+                v2[part, n] = (picked, slice(P * n - n0, P * (n + 1) - n0))
 
-        w2_p = keep.tile([P, 4, 4, 2 * P], U8, name="w2_p", align_bytes=64)
-        w2_sp = keep.tile([P, 4, 4, P], U8, name="w2_sp", align_bytes=64)
-        nc.vector.tensor_copy(out=w2_p[:].bitcast(U16),
-                              in_=w2_raw[:].bitcast(U16).rearrange("p a (h m t) -> p (a h) t m", h=2, t=4))
+        w2_w = keep.tile([P, 4, 4, 2 * P], U8, name="w2_w", align_bytes=64)
+        w2_s = keep.tile([P, 4, 4, P], U8, name="w2_s", align_bytes=64)
+        nc.vector.tensor_copy(out=w2_w[:].bitcast(U16),
+                              in_=w2_raw[:].bitcast(U16).rearrange("p a (h m i) -> p (a h) i m", h=2, i=4))
         v_s, v_w = [], []
         for a in range(2):
-            vs = keep.tile([P, S], U8, name="v_s%d" % a, align_bytes=64)
-            nc.vector.tensor_copy(out=vs[:], in_=tab_s[:, a, :].indirect(l1[:]))
-            v_s.append(vs)
+            picked_s = keep.tile([P, S], U8, name="v_s%d" % a, align_bytes=64)
+            nc.vector.tensor_copy(out=picked_s[:], in_=tab_s[:, a, :].indirect(corners[:]))
+            v_s.append(picked_s)
 
         def gather_v(a):
-            vw = keep.tile([P, S], U32, name="v_w%d" % a, align_bytes=64)
-            nc.vector.tensor_copy(out=vw[:], in_=tab_w[a][:].bitcast(U32).indirect(l1[:]))
-            v_w.append(vw)
+            picked_w = keep.tile([P, S], U32, name="v_w%d" % a, align_bytes=64)
+            nc.vector.tensor_copy(out=picked_w[:], in_=tab_w[a][:].bitcast(U32).indirect(corners[:]))
+            v_w.append(picked_w)
 
         gather_v(0)
-        nc.vector.tensor_copy(out=w2_sp[:], in_=w2_s_raw[:].rearrange("p a (h m t) -> p (a h) t m", h=2, t=4))
-        quant_w1(0, 0, 0, 4, "half0")
-        gather_v2("s", 0, 512, "v2a")
-        quant_w1(1, 0, 0, 2, "half1")
+        nc.vector.tensor_copy(out=w2_s[:], in_=w2_s_raw[:].rearrange("p a (h m i) -> p (a h) i m", h=2, i=4))
+        quant_w1(0, 0, 0, 4, "half0", "w1_c00")
+        gather_v2("scales", 0, S2 // 2, "v2_scales")
+        quant_w1(1, 0, 0, 2, "half1", "w1_c10")
         gather_v(1)
         quant_w1(1, 0, 2, 4, "quarter", "tab_w1")
-        gather_v2("s", 512, 1024, "quarter")
+        gather_v2("scales", S2 // 2, S2, "quarter")
         wg_rest = ring.tile([P, 3, S], F32, name="wg_rest", tag="raw10", bufs=1)
         for i in range(1, 4):
             nc.scalar.copy(out=wg_rest[:, i - 1, :], in_=wg_ps[i])
         wg = [wg_first[:]] + [wg_rest[:, i, :] for i in range(3)]
 
-        shape_sb, gated = {}, {}
+        lesson = {}
 
-        def stage1(x):
+        def first_stage(x):
             h, i = x // 4, x % 4
-            ps = psum.tile([P, S], F32, name="bank", tag="bank_a")
-            pr = psum.tile([P, S], F32, name="bank", tag="bank_a")
+            shape = psum.tile([P, S], F32, name="shape", tag="bank_a")
+            reach = psum.tile([P, S], F32, name="reach", tag="bank_a")
             for a in range(2):
-                nc.tensor.matmul_mx(out=ps[:], lhsT=w1_q[a, h, i][0], lhsT_scale=w1_q[a, h, i][1],
+                nc.tensor.matmul_mx(out=shape[:], lhsT=w1_q[a, h, i][0], lhsT_scale=w1_q[a, h, i][1],
                                     rhs=v_w[a][:].bitcast(FP8X4), rhs_scale=v_s[a][:], start=a == 0, stop=a == 1)
-                nc.tensor.matmul_mx(out=pr[:], lhsT=w2_p[:, 2 * a + h, i, :].bitcast(FP4X4),
-                                    lhsT_scale=w2_sp[:, 2 * a + h, i, :],
+                nc.tensor.matmul_mx(out=reach[:], lhsT=w2_w[:, 2 * a + h, i, :].bitcast(FP4X4),
+                                    lhsT_scale=w2_s[:, 2 * a + h, i, :],
                                     rhs=v_w[a][:].bitcast(FP8X4), rhs_scale=v_s[a][:], start=a == 0, stop=a == 1)
-            if x < 7:
-                shape_sb[x] = ring.tile([P, S], F32, name="shape_sb", bufs=4)
+            if x < ROW_TILES - 1:
+                lesson[x] = ring.tile([P, S], F32, name="lesson", bufs=SHAPE_BUFS)
             else:
-                shape_sb[x] = ring.tile([P, S], F32, name="shape_last", tag="last", bufs=1, align_bytes=64)
-            nc.scalar.copy(out=shape_sb[x][:], in_=ps[:])
-            gated[x] = ring.tile([P, S], F32, name="gated", bufs=2)
-            nc.vector.tensor_tensor(out=gated[x][:], in0=pr[:], in1=wg[i], op=MULT)
+                lesson[x] = ring.tile([P, S], F32, name="lesson_last", tag="last", bufs=1, align_bytes=64)
+            factor = ring.tile([P, S], F32, name="factor", bufs=2)
+            if x == 0:
+                nc.vector.tensor_tensor(out=factor[:], in0=shape[:], in1=wg[i], op=MULT)
+                nc.vector.tensor_tensor(out=lesson[x][:], in0=reach[:], in1=factor[:], op=MULT)
+            else:
+                nc.scalar.copy(out=lesson[x][:], in_=shape[:])
+                nc.scalar.copy(out=factor[:], in_=reach[:])
+                nc.gpsimd.tensor_tensor(out=lesson[x][:], in0=lesson[x][:], in1=wg[i], op=MULT)
+                nc.gpsimd.tensor_tensor(out=lesson[x][:], in0=lesson[x][:], in1=factor[:], op=MULT)
 
         def scatter(x):
-            nc.vector.tensor_tensor(out=page[x][:].indirect(l3[:]), in0=shape_sb[x][:], in1=gated[x][:], op=MULT)
+            nc.vector.tensor_copy(out=page[x][:].indirect(edited[:]), in_=lesson[x][:])
 
         pairs = {}
 
         def cast(x, c):
-            a, i = x // 4, x % 4
+            h, i = x // 4, x % 4
             if i == 0:
-                pairs[a, c] = ring.tile([P, 2, PASS, 2], BF16, name="pairs", tag=("half%d" if a == 0 else "pairs%d") % c,
+                pairs[h, c] = ring.tile([P, 2, PASS, 2], BF16, name="pairs", tag=("half%d" if h == 0 else "pairs%d") % c,
                                         bufs=1, align_bytes=64)
-            nc.scalar.copy(out=pairs[a, c][:, i // 2, :, i % 2], in_=page[x][:, PASS * c:PASS * (c + 1)])
+            nc.scalar.copy(out=pairs[h, c][:, i // 2, :, i % 2], in_=page[x][:, PASS * c:PASS * (c + 1)])
 
-        pg_g, pg_c, pg_s = {}, {}, {}
+        page_grouped, page_c, page_s = {}, {}, {}
 
-        def weave_page(a, c):
-            grouped = ring.tile([P, PASS, 4], BF16, name="pg_grouped", tag="pg%d" % c, bufs=1, align_bytes=64)
-            weave = nc.scalar.copy if a == 0 else nc.vector.tensor_copy
+        def weave_page(h, c):
+            grouped = ring.tile([P, PASS, 4], BF16, name="page_grouped", tag="woven%d" % c, bufs=1, align_bytes=64)
+            weave = nc.scalar.copy if h == 0 else nc.vector.tensor_copy
             weave(out=grouped[:].bitcast(F32),
-                  in_=pairs[a, c][:].rearrange("p u t e -> p (u t e)").bitcast(F32).rearrange("p (u t) -> p t u", u=2))
-            pg_g[a, c] = grouped
+                  in_=pairs[h, c][:].rearrange("p u t e -> p (u t e)").bitcast(F32).rearrange("p (u t) -> p t u", u=2))
+            page_grouped[h, c] = grouped
 
-        def quant_page(a, c):
-            grouped = pg_g[a, c]
-            pg_c[a, c] = keep.tile([P, PASS], U32, name="pg_c%d%d" % (a, c), align_bytes=64)
-            pg_s[a, c] = keep.tile([P, PASS], U8, name="pg_s%d%d" % (a, c), align_bytes=64)
-            nc.vector.quantize_mx(out=pg_c[a, c][:].bitcast(FP8X4), scales=pg_s[a, c][:],
-                                  in_=grouped[:].rearrange("p t i -> p (t i)"))
+        def quant_page(h, c):
+            page_c[h, c] = keep.tile([P, PASS], U32, name="page_c%d%d" % (h, c), align_bytes=64)
+            page_s[h, c] = keep.tile([P, PASS], U8, name="page_s%d%d" % (h, c), align_bytes=64)
+            nc.vector.quantize_mx(out=page_c[h, c][:].bitcast(FP8X4), scales=page_s[h, c][:],
+                                  in_=page_grouped[h, c][:].rearrange("p t i -> p (t i)"))
 
-        stage1(0)
-        stage1(1)
-        for x in range(8):
-            if x + 2 < 8:
-                stage1(x + 2)
+        quarter = S2 // 4
+        first_stage(0)
+        first_stage(1)
+        for x in range(ROW_TILES):
+            if x + 2 < ROW_TILES:
+                first_stage(x + 2)
             scatter(x)
             if x == 1:
-                quant_w1(0, 1, 0, 4, "half0")
-                quant_w1(1, 1, 0, 4, "half1")
+                quant_w1(0, 1, 0, 4, "half0", "w1_c01")
+                quant_w1(1, 1, 0, 4, "half1", "w1_c11")
             if x == 3:
                 for y in range(3):
                     cast(y, 0)
                     cast(y, 1)
             if x == 5:
-                gather_v2(0, 0, 256, "v2b")
-                gather_v2(1, 0, 256, "v2c")
-            if x == 7:
-                gather_v2(1, 256, 512, "last")
+                gather_v2(0, 0, quarter, "v2_first0")
+                gather_v2(1, 0, quarter, "v2_first1")
+            if x == ROW_TILES - 1:
+                gather_v2(1, quarter, 2 * quarter, "last")
             if x >= 3:
                 cast(x, 0)
                 cast(x, 1)
@@ -244,34 +256,35 @@ def tile_list_joseki_lesson_gaps_kernel(tc, tab_words, tab_scales, tab2_words, t
         weave_page(1, 1)
         quant_page(1, 0)
         quant_page(1, 1)
-        gather_v2(0, 256, 512, "pairs1")
-        gather_v2(0, 512, 1024, "pg0")
-        gather_v2(1, 512, 1024, "pg1")
+        gather_v2(0, quarter, 2 * quarter, "pairs1")
+        gather_v2(0, 2 * quarter, S2, "woven0")
+        gather_v2(1, 2 * quarter, S2, "woven1")
 
-        e_sb = {}
+        scores = {}
 
-        def scores(n):
-            e_sb[n] = ring.tile([P, T2], F32, name="e_sb", tag="rows", bufs=8)
+        def second_stage(n):
+            scores[n] = ring.tile([P, T2], F32, name="scores", tag="rows", bufs=ROW_TILES)
             for c in range(2):
-                pe = psum.tile([P, PASS], F32, name="bank", tag="bank_b" if n % 2 == 0 else "bank_a")
-                for a in range(2):
-                    wt, wc = v2[a, n]
-                    st, sc = v2["s", n]
-                    nc.tensor.matmul_mx(out=pe[:], lhsT=wt[:, wc].bitcast(FP8X4), lhsT_scale=st[4 * a:P, sc],
-                                        rhs=pg_c[a, c][:].bitcast(FP8X4), rhs_scale=pg_s[a, c][:],
-                                        start=a == 0, stop=a == 1)
-                nc.scalar.copy(out=e_sb[n][:, PASS * c:PASS * (c + 1)], in_=pe[:])
+                acc = psum.tile([P, PASS], F32, name="acc", tag="bank_b" if n % 2 == 0 else "bank_a")
+                for h in range(2):
+                    words, word_cols = v2[h, n]
+                    scales, scale_cols = v2["scales", n]
+                    nc.tensor.matmul_mx(out=acc[:], lhsT=words[:, word_cols].bitcast(FP8X4),
+                                        lhsT_scale=scales[4 * h:P, scale_cols],
+                                        rhs=page_c[h, c][:].bitcast(FP8X4), rhs_scale=page_s[h, c][:],
+                                        start=h == 0, stop=h == 1)
+                nc.scalar.copy(out=scores[n][:, PASS * c:PASS * (c + 1)], in_=acc[:])
 
-        scores(0)
-        scores(1)
-        for n in range(8):
-            if n + 2 < 8:
-                scores(n + 2)
-            for m0, m1 in ([(0, PICK)] if n < 7 else [(0, PICK // 2), (PICK // 2, PICK)]):
-                gap = ring.tile([P, m1 - m0], F32, name="gap", bufs=9)
-                nc.vector.tensor_tensor(out=gap[:], in0=e_sb[n][:].indirect(l4[:, m0 // 16:m1 // 16]),
+        second_stage(0)
+        second_stage(1)
+        for n in range(MOVE_TILES):
+            if n + 2 < MOVE_TILES:
+                second_stage(n + 2)
+            for m0, m1 in ([(0, PICK)] if n < MOVE_TILES - 1 else [(0, PICK // 2), (PICK // 2, PICK)]):
+                gap = ring.tile([P, m1 - m0], F32, name="gap", bufs=MOVE_TILES + 1)
+                nc.vector.tensor_tensor(out=gap[:], in0=scores[n][:].indirect(open_lessons[:, m0 // 16:m1 // 16]),
                                         in1=komi_sb[n // 4][:, n % 4, m0:m1], op=SUB)
-                if n < 2:
+                if n < SQUARES_ON_VECTOR:
                     nc.vector.tensor_tensor(out=gap[:], in0=gap[:], in1=gap[:], op=MULT)
                 else:
                     nc.scalar.activation(out=gap[:], in_=gap[:], func=ACT.Square)

@@ -20,20 +20,25 @@ ACT = mybir.ActivationFunctionType
 
 P = 128
 PASS = 512
-ROW_TILES = 8
+ROW_TILES = H // P
 MOVE_TILES = S2 // P
-SHAPE_BUFS = 4
 SQUARES_ON_VECTOR = 2
+CELL = 4096
 
 
 def tile_list_joseki_lesson_gaps_kernel(tc, tab_words, tab_scales, tab2_words, tab2_scales, w1, w2_words,
-                                                  w2_scales, page0, wgs, komi, offs, offs2, offs3, offs4, out):
+                                                      w2_scales, page0, wgs, komi, offs, offs2, offs3, offs4, out):
     nc = tc.nc
     with ExitStack() as ctx:
         lists = ctx.enter_context(tc.tile_pool(name="lists", bufs=1))
         keep = ctx.enter_context(tc.tile_pool(name="keep", bufs=1))
         ring = ctx.enter_context(tc.tile_pool(name="ring", bufs=1))
-        psum = ctx.enter_context(tc.psum_pool(name="psum", bufs=4))
+        cells = ctx.enter_context(tc.tile_pool(name="cells", bufs=1))
+        psum = ctx.enter_context(tc.psum_pool(name="psum", bufs=1))
+
+        def cell(shape, dtype, name, x, start):
+            base = CELL * (x + (x > 1) + (x > 6))
+            return cells.tile(shape, dtype, name=name, tag=name, offset=base + start, align_bytes=64)
 
         corners = lists.tile([P, S // 16], U16, name="corners")
         moves = lists.tile([P, S2 // 16], U16, name="moves")
@@ -41,237 +46,273 @@ def tile_list_joseki_lesson_gaps_kernel(tc, tab_words, tab_scales, tab2_words, t
         open_lessons = lists.tile([P, PICK // 16], U16, name="open_lessons")
 
         tab_s = keep.tile([P, 2, T], U8, name="tab_s", align_bytes=64)
-        w2_s_raw = keep.tile([P, 2, H], U8, name="w2_s_raw", align_bytes=64)
+        w2_s = keep.tile([P, 2, H], U8, name="w2_s", align_bytes=64)
         tab2_s = keep.tile([P, T3], U8, name="tab2_s", align_bytes=64)
         nc.vector.memset(tab_s[:].bitcast(I32), 0)
-        nc.vector.memset(w2_s_raw[:].bitcast(I32), 0)
+        nc.gpsimd.memset(w2_s[:].bitcast(I32), 0)
         nc.vector.memset(tab2_s[:].bitcast(I32), 0)
 
-        def load_w1(a, h):
-            raw = ring.tile([P, 4, PASS], F32, name="w1_raw", tag="raw%d%d" % (a, h), bufs=1)
-            nc.sync.dma_start(out=raw[:], in_=w1[PASS * a:PASS * (a + 1), PASS * h:PASS * (h + 1)]
-                              .rearrange("(p j) c -> p j c", j=4))
-            return raw
-
-        def load_words(src, a, name):
-            words = keep.tile([P, T], I32, name=name, align_bytes=64)
+        def load_words(src, a, tag):
+            words = ring.tile([P, T], I32, name="words", tag=tag, align_bytes=64)
             nc.sync.dma_start(out=words[:], in_=src[a].rearrange("p t i -> p (t i)").bitcast(I32))
             return words
 
+        def load_scales(queue, plane, src):
+            for r in range(4):
+                queue.dma_start(out=plane[r:P:32, :, :].bitcast(I32),
+                                  in_=src.rearrange("a (q r) t -> r q a t", r=4)[r].bitcast(I32))
+
+        w1_raw = {}
+
+        def load_w1(x):
+            for a in range(2):
+                if a == 0:
+                    w1_raw[x, a] = ring.tile([P, 4, P], F32, name="w1_raw", tag="raw%d0" % x, align_bytes=64)
+                else:
+                    w1_raw[x, a] = cell([P, 4, P], F32, "w1_raw%d" % x, x, 0)
+                nc.sync.dma_start(out=w1_raw[x, a][:],
+                                  in_=w1[PASS * a:PASS * (a + 1), P * x:P * (x + 1)].rearrange("(p j) c -> p j c", j=4))
+
+        page = {}
+
         def load_page(x):
-            h, i = x // 4, x % 4
-            rows = ring.tile([P, T2], F32, name="page", tag="rows", bufs=ROW_TILES)
-            nc.sync.dma_start(out=rows[:],
-                              in_=page0[PASS * h:PASS * (h + 1), :].rearrange("(p i) t -> p i t", i=4)[:, i, :])
-            return rows
+            page[x] = ring.tile([P, T2], F32, name="page", tag="rows", bufs=ROW_TILES)
+            nc.sync.dma_start(out=page[x][:], in_=page0[P * x:P * (x + 1), :])
 
         def load_komi(g):
-            rows = ring.tile([P, 4, PICK], F32, name="komi_sb", tag=("raw00", "raw01")[g], bufs=1)
+            rows = ring.tile([P, 4, PICK], F32, name="komi_sb", tag="tab_w%d" % g, align_bytes=64)
             nc.sync.dma_start(out=rows[:], in_=komi[PASS * g:PASS * (g + 1), :].rearrange("(c p) m -> p c m", p=P))
             return rows
 
+        w2_w = {}
+
+        def load_w2(x0, x1):
+            words = keep.tile([P, 2, 2 * P * (x1 - x0)], U8, name="w2_w%d" % x0, align_bytes=64)
+            nc.sync.dma_start(out=words[:].bitcast(I32),
+                              in_=w2_words[:, :, 2 * P * x0:2 * P * x1].rearrange("a p c -> p a c").bitcast(I32))
+            for x in range(x0, x1):
+                for a in range(2):
+                    w2_w[x, a] = words[:, a, 2 * P * (x - x0):2 * P * (x - x0 + 1)]
+
+        tab_w = [load_words(tab_words, 0, "tab_w0")]
         nc.sync.dma_start(corners[:], offs)
+        load_scales(nc.sync, tab_s, tab_scales)
+        tab_w.append(load_words(tab_words, 1, "tab_w1"))
+        load_w2(0, 4)
+        load_scales(nc.sync, w2_s, w2_scales)
+        load_w1(0)
         wgs_sb = keep.tile([P, S], F32, name="wgs_sb")
         nc.sync.dma_start(out=wgs_sb[:], in_=wgs)
-        w2_raw = keep.tile([P, 2, 2 * H], U8, name="w2_raw", align_bytes=64)
-        nc.sync.dma_start(out=w2_raw[:].bitcast(I32), in_=w2_words.rearrange("a p c -> p a c").bitcast(I32))
-        for q in range(4):
-            nc.sync.dma_start(out=tab_s[32 * q:32 * q + 4, :, :].bitcast(I32),
-                              in_=tab_scales[:, 4 * q:4 * q + 4, :].rearrange("a r t -> r a t").bitcast(I32))
-        tab_w = [load_words(tab_words, 0, "tab_w0")]
-        for q in range(4):
-            nc.sync.dma_start(out=w2_s_raw[32 * q:32 * q + 4, :, :].bitcast(I32),
-                              in_=w2_scales[:, 4 * q:4 * q + 4, :].rearrange("a r t -> r a t").bitcast(I32))
-        w1_raw = {}
-        w1_raw[0, 0] = load_w1(0, 0)
+        load_w1(1)
+        load_page(0)
         nc.sync.dma_start(edited[:], offs3)
+        load_w1(2)
+        load_page(1)
+        load_w1(3)
+        load_w2(4, ROW_TILES)
         nc.sync.dma_start(moves[:], offs2)
         for q in range(4):
             nc.sync.dma_start(out=tab2_s[32 * q:32 * q + 8, :].bitcast(I32),
                               in_=tab2_scales[:, 4 * q:4 * q + 4, :].bitcast(I32))
-        w1_raw[1, 0] = load_w1(1, 0)
-        tab_w.append(load_words(tab_words, 1, "tab_w1"))
-        page = {}
-        page[0] = load_page(0)
-        page[1] = load_page(1)
-        w1_raw[0, 1] = load_w1(0, 1)
-        w1_raw[1, 1] = load_w1(1, 1)
-        komi_sb = [load_komi(0)]
-        for x in range(2, ROW_TILES - 1):
-            page[x] = load_page(x)
-        nc.sync.dma_start(open_lessons[:], offs4)
+        for x in range(2, 6):
+            load_page(x)
+            load_w1(x + 2)
         tab2_w = [load_words(tab2_words, a, "tab2_w%d" % a) for a in range(2)]
-        page[ROW_TILES - 1] = load_page(ROW_TILES - 1)
-        komi_sb.append(load_komi(1))
+        load_page(6)
+        load_page(7)
+        nc.sync.dma_start(open_lessons[:], offs4)
 
         ident = keep.tile([P, P], F32, name="ident")
         make_identity(nc, ident[:])
-        wgs_t_ps = psum.tile([P, 4, P], F32, name="wgs_t_ps", tag="bank_a")
-        for b in range(4):
-            nc.tensor.transpose(wgs_t_ps[:, b, :], wgs_sb[:, P * b:P * (b + 1)], ident[:])
-        wgs_t = keep.tile([P, 4, 4, 4, 32], F32, name="wgs_t")
-        nc.scalar.copy(out=wgs_t[:],
-                       in_=wgs_t_ps[:].rearrange("j b (q i) -> j b i q", i=4).unsqueeze(3).to_broadcast([P, 4, 4, 4, 32]))
-        wg_first = keep.tile([P, S], F32, name="wg_first")
-        wg_ps = []
-        for i in range(4):
-            wg_bank = psum.tile([P, 4, P], F32, name="wg_bank", tag="bank_b")
-            for b in range(4):
-                nc.tensor.transpose(wg_bank[:, b, :], wgs_t[:, b, i, :, :].rearrange("j g q -> j (g q)"), ident[:])
-            wg_ps.append(wg_bank[:].rearrange("p b j -> p (b j)"))
-        nc.scalar.copy(out=wg_first[:], in_=wg_ps[0])
 
-        w1_q = {}
-
-        def quant_w1(a, h, i0, i1, tag, codes_tag):
-            count = i1 - i0
-            grouped = ring.tile([P, count, P, 4], BF16, name="w1_grouped", tag=tag, bufs=1, align_bytes=64)
-            nc.scalar.activation(out=grouped[:].rearrange("p i m j -> p m j i"),
-                                 in_=w1_raw[a, h][:].rearrange("p j (m i) -> p m j i", i=4)[:, :, :, i0:i1],
-                                 func=ACT.Copy)
-            codes = keep.tile([P, count * P], U32, name="w1_c", tag=codes_tag, align_bytes=64)
-            scales = keep.tile([P, count * P], U8, name="w1_s%d%d%d" % (a, h, i0), align_bytes=64)
-            nc.vector.quantize_mx(out=codes[:].bitcast(FP8X4), scales=scales[:],
-                                  in_=grouped[:].rearrange("p i m j -> p (i m j)"))
-            for i in range(i0, i1):
-                cols = slice(P * (i - i0), P * (i - i0 + 1))
-                w1_q[a, h, i] = (codes[:, cols].bitcast(FP8X4), scales[:, cols])
-
-        v2 = {}
-
-        def gather_v2(part, n0, n1, tag):
-            window = tab2_s[:] if part == "scales" else tab2_w[part][:].bitcast(U32)
-            picked = ring.tile([P, n1 - n0], U8 if part == "scales" else U32, name="v2", tag=tag, bufs=1, align_bytes=64)
-            nc.vector.tensor_copy(out=picked[:], in_=window.indirect(moves[:, n0 // 16:n1 // 16]))
-            for n in range(n0 // P, n1 // P):
-                v2[part, n] = (picked, slice(P * n - n0, P * (n + 1) - n0))
-
-        w2_w = keep.tile([P, 4, 4, 2 * P], U8, name="w2_w", align_bytes=64)
-        w2_s = keep.tile([P, 4, 4, P], U8, name="w2_s", align_bytes=64)
-        nc.vector.tensor_copy(out=w2_w[:].bitcast(U16),
-                              in_=w2_raw[:].bitcast(U16).rearrange("p a (h m i) -> p (a h) i m", h=2, i=4))
         v_s, v_w = [], []
         for a in range(2):
             picked_s = keep.tile([P, S], U8, name="v_s%d" % a, align_bytes=64)
             nc.vector.tensor_copy(out=picked_s[:], in_=tab_s[:, a, :].indirect(corners[:]))
             v_s.append(picked_s)
-
-        def gather_v(a):
+        for a in range(2):
             picked_w = keep.tile([P, S], U32, name="v_w%d" % a, align_bytes=64)
             nc.vector.tensor_copy(out=picked_w[:], in_=tab_w[a][:].bitcast(U32).indirect(corners[:]))
             v_w.append(picked_w)
+        komi_sb = [load_komi(0), load_komi(1)]
 
-        gather_v(0)
-        nc.vector.tensor_copy(out=w2_s[:], in_=w2_s_raw[:].rearrange("p a (h m i) -> p (a h) i m", h=2, i=4))
-        quant_w1(0, 0, 0, 4, "half0", "w1_c00")
-        gather_v2("scales", 0, S2 // 2, "v2_scales")
-        quant_w1(1, 0, 0, 2, "half1", "w1_c10")
-        gather_v(1)
-        quant_w1(1, 0, 2, 4, "quarter", "tab_w1")
-        gather_v2("scales", S2 // 2, S2, "quarter")
-        wg_rest = ring.tile([P, 3, S], F32, name="wg_rest", tag="raw10", bufs=1)
-        for i in range(1, 4):
-            nc.scalar.copy(out=wg_rest[:, i - 1, :], in_=wg_ps[i])
-        wg = [wg_first[:]] + [wg_rest[:, i, :] for i in range(3)]
+        w1_grouped, w1_q = {}, {}
 
-        lesson = {}
-
-        def first_stage(x):
-            h, i = x // 4, x % 4
-            shape = psum.tile([P, S], F32, name="shape", tag="bank_a")
-            reach = psum.tile([P, S], F32, name="reach", tag="bank_a")
+        def cast_w1(x):
+            w1_grouped[x] = cell([P, 2, P, 4], BF16, "w1_grouped%d" % x, x, CELL // 2)
             for a in range(2):
-                nc.tensor.matmul_mx(out=shape[:], lhsT=w1_q[a, h, i][0], lhsT_scale=w1_q[a, h, i][1],
-                                    rhs=v_w[a][:].bitcast(FP8X4), rhs_scale=v_s[a][:], start=a == 0, stop=a == 1)
-                nc.tensor.matmul_mx(out=reach[:], lhsT=w2_w[:, 2 * a + h, i, :].bitcast(FP4X4),
-                                    lhsT_scale=w2_s[:, 2 * a + h, i, :],
-                                    rhs=v_w[a][:].bitcast(FP8X4), rhs_scale=v_s[a][:], start=a == 0, stop=a == 1)
-            if x < ROW_TILES - 1:
-                lesson[x] = ring.tile([P, S], F32, name="lesson", bufs=SHAPE_BUFS)
+                nc.scalar.copy(out=w1_grouped[x][:, a].rearrange("p (c i) j -> p c j i", i=4),
+                               in_=w1_raw[x, a][:].rearrange("p j (c i) -> p c j i", i=4))
+
+        def quant_w1(x, parts):
+            if x >= 2:
+                codes = cell([P, 2 * P], U32, "w1_c%d" % x, max(x - 2, 1), CELL if x == 2 else CELL // 4)
             else:
-                lesson[x] = ring.tile([P, S], F32, name="lesson_last", tag="last", bufs=1, align_bytes=64)
-            factor = ring.tile([P, S], F32, name="factor", bufs=2)
+                codes = keep.tile([P, 2 * P], U32, name="w1_c%d" % x, align_bytes=64)
+            scales = ring.tile([P, 2 * P], U8, name="w1_s", bufs=3, align_bytes=64)
+            width = 2 * P // parts
+            for k in range(parts):
+                cols = slice(width * k, width * (k + 1))
+                nc.vector.quantize_mx(out=codes[:, cols].bitcast(FP8X4), scales=scales[:, cols],
+                                      in_=w1_grouped[x][:].rearrange("p a c j -> p (a c j)")[:, 4 * width * k:4 * width * (k + 1)])
+            w1_q[x] = (codes, scales)
+
+        v2 = {}
+
+        def gather_v2(part, n0, n1, picked):
+            window = tab2_s[:] if part == "scales" else tab2_w[part][:].bitcast(U32)
+            nc.vector.tensor_copy(out=picked[:], in_=window.indirect(moves[:, n0 // 16:n1 // 16]))
+            for n in range(n0 // P, n1 // P):
+                v2[part, n] = (picked, slice(P * n - n0, P * (n + 1) - n0))
+
+        reach_sb, shape_sb, lesson = {}, {}, {}
+
+        def reach_stage(x):
+            reach = psum.tile([P, S], F32, name="reach", tag="bank_e%d" % x if x in (1, 2) else "bank_r")
+            for a in range(2):
+                nc.tensor.matmul_mx(out=reach[:], lhsT=w2_w[x, a].bitcast(FP4X4), lhsT_scale=w2_s[:, a, P * x:P * (x + 1)],
+                                    rhs=v_w[a][:].bitcast(FP8X4), rhs_scale=v_s[a][:], start=a == 0, stop=a == 1)
+            reach_sb[x] = ring.tile([P, S], F32, name="reach_sb", tag="raw%d0" % x if x else "reach_first", align_bytes=64)
             if x == 0:
-                nc.vector.tensor_tensor(out=factor[:], in0=shape[:], in1=wg[i], op=MULT)
-                nc.vector.tensor_tensor(out=lesson[x][:], in0=reach[:], in1=factor[:], op=MULT)
+                nc.vector.tensor_tensor(out=reach_sb[x][:], in0=reach[:], in1=wgs_sb[:], op=MULT)
             else:
-                nc.scalar.copy(out=lesson[x][:], in_=shape[:])
-                nc.scalar.copy(out=factor[:], in_=reach[:])
-                nc.gpsimd.tensor_tensor(out=lesson[x][:], in0=lesson[x][:], in1=wg[i], op=MULT)
-                nc.gpsimd.tensor_tensor(out=lesson[x][:], in0=lesson[x][:], in1=factor[:], op=MULT)
+                nc.scalar.copy(out=reach_sb[x][:], in_=reach[:])
+
+        def shape_stage(x):
+            shape = psum.tile([P, S], F32, name="shape", tag="bank_s")
+            codes, scales = w1_q[x]
+            for a in range(2):
+                nc.tensor.matmul_mx(out=shape[:], lhsT=codes[:, P * a:P * (a + 1)].bitcast(FP8X4),
+                                    lhsT_scale=scales[:, P * a:P * (a + 1)],
+                                    rhs=v_w[a][:].bitcast(FP8X4), rhs_scale=v_s[a][:], start=a == 0, stop=a == 1)
+            if x == 0:
+                lesson[x] = cell([P, S], F32, "lesson0", 1, 3 * CELL // 4)
+                nc.vector.tensor_tensor(out=lesson[x][:], in0=shape[:], in1=reach_sb[x][:], op=MULT)
+            else:
+                if x < ROW_TILES - 1:
+                    shape_sb[x] = cell([P, S], F32, "shape_sb%d" % x, x + 1, 0)
+                else:
+                    shape_sb[x] = ring.tile([P, S], F32, name="shape_sb")
+                nc.scalar.copy(out=shape_sb[x][:], in_=shape[:])
+
+        def products(x):
+            lesson[x] = cell([P, S], F32, "lesson%d" % x, x, CELL // 4)
+            nc.gpsimd.tensor_tensor(out=lesson[x][:], in0=reach_sb[x][:], in1=wgs_sb[:], op=MULT)
+            nc.gpsimd.tensor_tensor(out=lesson[x][:], in0=lesson[x][:], in1=shape_sb[x][:], op=MULT)
 
         def scatter(x):
             nc.vector.tensor_copy(out=page[x][:].indirect(edited[:]), in_=lesson[x][:])
 
-        pairs = {}
+        blocks = (4, 2)
+        turned = {}
 
-        def cast(x, c):
-            h, i = x // 4, x % 4
-            if i == 0:
-                pairs[h, c] = ring.tile([P, 2, PASS, 2], BF16, name="pairs", tag=("half%d" if h == 0 else "pairs%d") % c,
-                                        bufs=1, align_bytes=64)
-            nc.scalar.copy(out=pairs[h, c][:, i // 2, :, i % 2], in_=page[x][:, PASS * c:PASS * (c + 1)])
+        def turn_rows(x):
+            h, quarter = x // 4, x % 4
+            count = blocks[h]
+            for bank_index in range(2):
+                bank = psum.tile([P, 4, P], F32, name="turn_bank", tag=(("bank_s", "bank_r") if x < ROW_TILES - 1 else ("bank_e0", "bank_e1"))[bank_index])
+                for b in range(4):
+                    tb = 4 * bank_index + b
+                    nc.tensor.transpose(bank[:, b, :], page[x][:, P * tb:P * (tb + 1)], ident[:])
+                for b0 in range(0, 4, count):
+                    g = (4 * bank_index + b0) // count
+                    if quarter == 0:
+                        turned[h, g] = ring.tile([P, count, 2, P, 2], BF16, name="turned", tag="turned%d%d" % (h, g),
+                                                 align_bytes=64)
+                    nc.scalar.copy(out=turned[h, g][:, :, :, 32 * quarter:32 * (quarter + 1), :].rearrange("t b u q e -> t u b q e"),
+                                   in_=bank[:, b0:b0 + count, :].rearrange("t b (q u e) -> t u b q e", u=2, e=2))
 
-        page_grouped, page_c, page_s = {}, {}, {}
+        page_c, page_s, grouped_page = {}, {}, {}
 
-        def weave_page(h, c):
-            grouped = ring.tile([P, PASS, 4], BF16, name="page_grouped", tag="woven%d" % c, bufs=1, align_bytes=64)
-            weave = nc.scalar.copy if h == 0 else nc.vector.tensor_copy
-            weave(out=grouped[:].bitcast(F32),
-                  in_=pairs[h, c][:].rearrange("p u t e -> p (u t e)").bitcast(F32).rearrange("p (u t) -> p t u", u=2))
-            page_grouped[h, c] = grouped
+        def turn_back(h, pair, tag):
+            count = blocks[h]
+            bank = psum.tile([P, 2, 2, P], F32, name="back_bank", tag=tag)
+            for b in range(2):
+                tb = 2 * pair + b
+                for u in range(2):
+                    nc.tensor.transpose(bank[:, b, u, :],
+                                        turned[h, tb // count][:, tb % count, u].rearrange("t p e -> t (p e)").bitcast(F32),
+                                        ident[:])
+            g = 2 * pair // count
+            if (2 * pair) % count == 0:
+                if (h, g) == (0, 0):
+                    grouped_page[h, g] = cell([P, count * P, 4], BF16, "grouped_first", ROW_TILES - 1, -3 * CELL // 4)
+                elif h == 1:
+                    grouped_page[h, g] = cell([P, count * P, 4], BF16, "grouped_late%d" % g, g, 0)
+                else:
+                    grouped_page[h, g] = ring.tile([P, count * P, 4], BF16, name="grouped_page",
+                                                   tag="grouped%d%d" % (h, g), align_bytes=64)
+            t0 = (2 * pair) % count * P
+            nc.scalar.copy(out=grouped_page[h, g][:, t0:t0 + 2 * P, :].bitcast(F32).rearrange("p (b t) u -> p b t u", b=2),
+                           in_=bank[:].rearrange("p b u t -> p b t u"))
 
-        def quant_page(h, c):
-            page_c[h, c] = keep.tile([P, PASS], U32, name="page_c%d%d" % (h, c), align_bytes=64)
-            page_s[h, c] = keep.tile([P, PASS], U8, name="page_s%d%d" % (h, c), align_bytes=64)
-            nc.vector.quantize_mx(out=page_c[h, c][:].bitcast(FP8X4), scales=page_s[h, c][:],
-                                  in_=page_grouped[h, c][:].rearrange("p t i -> p (t i)"))
+        def quant_page(h, g):
+            width = blocks[h] * P
+            if g == 0:
+                if h == 0:
+                    page_c[h] = cell([P, T2], U32, "page_c0", 6, -CELL // 2)
+                else:
+                    page_c[h] = keep.tile([P, T2], U32, name="page_c1", align_bytes=64)
+                page_s[h] = keep.tile([P, T2], U8, name="page_s%d" % h, align_bytes=64)
+            cols = slice(width * g, width * (g + 1))
+            nc.vector.quantize_mx(out=page_c[h][:, cols].bitcast(FP8X4), scales=page_s[h][:, cols],
+                                  in_=grouped_page[h, g][:].rearrange("p t i -> p (t i)"))
 
-        quarter = S2 // 4
-        first_stage(0)
-        first_stage(1)
+        reach_stage(0)
+        cast_w1(0)
+        quant_w1(0, 2)
+        cast_w1(1)
+        quant_w1(1, 1)
+        shape_stage(0)
+        reach_stage(1)
+        cast_w1(2)
+        shape_stage(1)
+        reach_stage(2)
+        products(1)
+        half, quarter = S2 // 2, S2 // 4
         for x in range(ROW_TILES):
-            if x + 2 < ROW_TILES:
-                first_stage(x + 2)
+            if x == 7:
+                quant_page(0, 0)
+                gather_v2("scales", 0, half, cell([P, half], U8, "v2_s_first", 6, CELL // 2))
+                gather_v2(0, 0, quarter, cell([P, quarter], U32, "v2_first", 6, 5 * CELL // 8))
+                quant_page(0, 1)
             scatter(x)
-            if x == 1:
-                quant_w1(0, 1, 0, 4, "half0", "w1_c01")
-                quant_w1(1, 1, 0, 4, "half1", "w1_c11")
-            if x == 3:
-                for y in range(3):
-                    cast(y, 0)
-                    cast(y, 1)
+            if x + 2 < ROW_TILES:
+                quant_w1(x + 2, 1)
+                if x + 3 < ROW_TILES:
+                    cast_w1(x + 3)
+                shape_stage(x + 2)
+                if x + 3 < ROW_TILES:
+                    reach_stage(x + 3)
+                products(x + 2)
             if x == 5:
-                gather_v2(0, 0, quarter, "v2_first0")
-                gather_v2(1, 0, quarter, "v2_first1")
-            if x == ROW_TILES - 1:
-                gather_v2(1, quarter, 2 * quarter, "last")
-            if x >= 3:
-                cast(x, 0)
-                cast(x, 1)
-            if x in (4, 5):
-                weave_page(0, x - 4)
-                quant_page(0, x - 4)
-        weave_page(1, 0)
-        weave_page(1, 1)
-        quant_page(1, 0)
-        quant_page(1, 1)
-        gather_v2(0, quarter, 2 * quarter, "pairs1")
-        gather_v2(0, 2 * quarter, S2, "woven0")
-        gather_v2(1, 2 * quarter, S2, "woven1")
+                for pair in range(4):
+                    turn_back(0, pair, "bank_b%d" % (pair % 2))
+            if x < ROW_TILES - 1:
+                turn_rows(x)
+        gather_v2(1, 0, half, cell([P, half], U32, "v2_second", ROW_TILES - 1, CELL // 2))
+        gather_v2(0, quarter, half, cell([P, quarter], U32, "v2_third", ROW_TILES - 1, CELL // 4))
+        turn_rows(ROW_TILES - 1)
+        for pair in range(4):
+            turn_back(1, pair, "bank_e%d" % ((pair + 2) % 4))
+            quant_page(1, pair)
+            gather_v2(pair % 2, half + quarter * (pair // 2), half + quarter * (pair // 2 + 1),
+                      cell([P, quarter], U32, "v2_late%d" % pair, pair, 0))
+        gather_v2("scales", half, S2, cell([P, half], U8, "v2_s_late", 3, CELL // 4))
 
         scores = {}
 
         def second_stage(n):
             scores[n] = ring.tile([P, T2], F32, name="scores", tag="rows", bufs=ROW_TILES)
             for c in range(2):
-                acc = psum.tile([P, PASS], F32, name="acc", tag="bank_b" if n % 2 == 0 else "bank_a")
+                acc = psum.tile([P, PASS], F32, name="acc", tag=(("bank_s", "bank_b0"), ("bank_r", "bank_b1"), ("bank_e2", "bank_e0"), ("bank_e3", "bank_e1"))[n % 4][c])
                 for h in range(2):
                     words, word_cols = v2[h, n]
                     scales, scale_cols = v2["scales", n]
                     nc.tensor.matmul_mx(out=acc[:], lhsT=words[:, word_cols].bitcast(FP8X4),
                                         lhsT_scale=scales[4 * h:P, scale_cols],
-                                        rhs=page_c[h, c][:].bitcast(FP8X4), rhs_scale=page_s[h, c][:],
+                                        rhs=page_c[h][:, PASS * c:PASS * (c + 1)].bitcast(FP8X4),
+                                        rhs_scale=page_s[h][:, PASS * c:PASS * (c + 1)],
                                         start=h == 0, stop=h == 1)
                 nc.scalar.copy(out=scores[n][:, PASS * c:PASS * (c + 1)], in_=acc[:])
 

@@ -23,7 +23,18 @@ PASS = 512
 ROW_TILES = H // P
 MOVE_TILES = S2 // P
 SQUARES_ON_VECTOR = 2
-CELL = 4096
+PLACE = {
+    "grouped1": 1, "lesson1": 0, "lesson0": 2, "codes3": 0, "codes4": 1,
+    "grouped2": 4, "weighted2": 4, "grouped3": 6, "weighted3": 6,  "lesson2": 41, "codes5": 41,
+    "lesson3": 9, "grouped5": 11, "lesson4": 12, "codes6": 9, "codes7": 10,
+    "raw61": 15, "shape5": 15, "shape4": 17, "lesson6": 13.5, "grouped7": 19, "lesson5": 18, "shape6": 21,
+    "lesson7": 19.5, "page_c0": 15.75, "v2_s_first": 19.75, "v2_first": 20.25, "v2_second": 21.25,
+    "woven00": 43, "v2_third": 43,
+    "woven10": 0, "woven11": 2, "woven12": 4, "woven13": 6,
+    "v2_late0": 0, "v2_late1": 2, "v2_late2": 4, "v2_late3": 6, "v2_s_late": 7,
+    "raw20": 23, "reach2": 23, "reach3": 25, "raw40": 27, "reach4": 27, "reach5": 29,
+    "raw60": 33, "turned00": 31, "turned01": 35, "raw10": 39, "reach1": 39,
+}
 
 
 def tile_list_joseki_lesson_gaps_kernel(tc, tab_words, tab_scales, tab2_words, tab2_scales, w1, w2_words,
@@ -36,9 +47,10 @@ def tile_list_joseki_lesson_gaps_kernel(tc, tab_words, tab_scales, tab2_words, t
         cells = ctx.enter_context(tc.tile_pool(name="cells", bufs=1))
         psum = ctx.enter_context(tc.psum_pool(name="psum", bufs=1))
 
-        def cell(shape, dtype, name, x, start):
-            base = CELL * (x + (x > 1) + (x > 6))
-            return cells.tile(shape, dtype, name=name, tag=name, offset=base + start, align_bytes=64)
+        def cell(shape, dtype, name):
+            if name in PLACE:
+                return cells.tile(shape, dtype, name=name, tag=name, offset=int(1024 * PLACE[name]), align_bytes=64)
+            return ring.tile(shape, dtype, name=name, tag=name, align_bytes=64)
 
         corners = lists.tile([P, S // 16], U16, name="corners")
         moves = lists.tile([P, S2 // 16], U16, name="moves")
@@ -64,14 +76,13 @@ def tile_list_joseki_lesson_gaps_kernel(tc, tab_words, tab_scales, tab2_words, t
 
         w1_raw = {}
 
-        def load_w1(x):
+        def load_w1(x0, x1):
             for a in range(2):
-                if a == 0:
-                    w1_raw[x, a] = ring.tile([P, 4, P], F32, name="w1_raw", tag="raw%d0" % x, align_bytes=64)
-                else:
-                    w1_raw[x, a] = cell([P, 4, P], F32, "w1_raw%d" % x, x, 0)
-                nc.sync.dma_start(out=w1_raw[x, a][:],
-                                  in_=w1[PASS * a:PASS * (a + 1), P * x:P * (x + 1)].rearrange("(p j) c -> p j c", j=4))
+                raw = cell([P, 4, P * (x1 - x0)], F32, "raw%d%d" % (x0, a))
+                nc.sync.dma_start(out=raw[:],
+                                  in_=w1[PASS * a:PASS * (a + 1), P * x0:P * x1].rearrange("(p j) c -> p j c", j=4))
+                for x in range(x0, x1):
+                    w1_raw[x, a] = raw[:, :, P * (x - x0):P * (x - x0 + 1)]
 
         page = {}
 
@@ -100,27 +111,29 @@ def tile_list_joseki_lesson_gaps_kernel(tc, tab_words, tab_scales, tab2_words, t
         tab_w.append(load_words(tab_words, 1, "tab_w1"))
         load_w2(0, 4)
         load_scales(nc.sync, w2_s, w2_scales)
-        load_w1(0)
+        load_w1(0, 1)
         wgs_sb = keep.tile([P, S], F32, name="wgs_sb")
         nc.sync.dma_start(out=wgs_sb[:], in_=wgs)
-        load_w1(1)
+        load_w1(1, 2)
         load_page(0)
         nc.sync.dma_start(edited[:], offs3)
-        load_w1(2)
-        load_page(1)
-        load_w1(3)
+        load_w1(2, 4)
         load_w2(4, ROW_TILES)
+        load_page(1)
+        load_w1(4, 6)
         nc.sync.dma_start(moves[:], offs2)
+        nc.sync.dma_start(open_lessons[:], offs4)
+        load_page(2)
+        load_w1(6, 8)
+        load_page(3)
+        load_page(4)
         for q in range(4):
             nc.sync.dma_start(out=tab2_s[32 * q:32 * q + 8, :].bitcast(I32),
                               in_=tab2_scales[:, 4 * q:4 * q + 4, :].bitcast(I32))
-        for x in range(2, 6):
-            load_page(x)
-            load_w1(x + 2)
+        load_page(5)
         tab2_w = [load_words(tab2_words, a, "tab2_w%d" % a) for a in range(2)]
         load_page(6)
         load_page(7)
-        nc.sync.dma_start(open_lessons[:], offs4)
 
         ident = keep.tile([P, P], F32, name="ident")
         make_identity(nc, ident[:])
@@ -139,17 +152,14 @@ def tile_list_joseki_lesson_gaps_kernel(tc, tab_words, tab_scales, tab2_words, t
         w1_grouped, w1_q = {}, {}
 
         def cast_w1(x):
-            w1_grouped[x] = cell([P, 2, P, 4], BF16, "w1_grouped%d" % x, x, CELL // 2)
+            w1_grouped[x] = cell([P, 2, P, 4], BF16, "grouped%d" % x)
             for a in range(2):
                 nc.scalar.copy(out=w1_grouped[x][:, a].rearrange("p (c i) j -> p c j i", i=4),
-                               in_=w1_raw[x, a][:].rearrange("p j (c i) -> p c j i", i=4))
+                               in_=w1_raw[x, a].rearrange("p j (c i) -> p c j i", i=4))
 
         def quant_w1(x, parts):
-            if x >= 2:
-                codes = cell([P, 2 * P], U32, "w1_c%d" % x, max(x - 2, 1), CELL if x == 2 else CELL // 4)
-            else:
-                codes = keep.tile([P, 2 * P], U32, name="w1_c%d" % x, align_bytes=64)
-            scales = ring.tile([P, 2 * P], U8, name="w1_s", bufs=3, align_bytes=64)
+            codes = cell([P, 2 * P], U32, "codes%d" % x)
+            scales = keep.tile([P, 2 * P], U8, name="w1_s%d" % x, align_bytes=64)
             width = 2 * P // parts
             for k in range(parts):
                 cols = slice(width * k, width * (k + 1))
@@ -165,40 +175,42 @@ def tile_list_joseki_lesson_gaps_kernel(tc, tab_words, tab_scales, tab2_words, t
             for n in range(n0 // P, n1 // P):
                 v2[part, n] = (picked, slice(P * n - n0, P * (n + 1) - n0))
 
-        reach_sb, shape_sb, lesson = {}, {}, {}
+        reach_sb, shape_ps, weighted, lesson = {}, {}, {}, {}
 
         def reach_stage(x):
-            reach = psum.tile([P, S], F32, name="reach", tag="bank_e%d" % x if x in (1, 2) else "bank_r")
+            reach = psum.tile([P, S], F32, name="reach", tag="bank_r%d" % (x % 2))
             for a in range(2):
                 nc.tensor.matmul_mx(out=reach[:], lhsT=w2_w[x, a].bitcast(FP4X4), lhsT_scale=w2_s[:, a, P * x:P * (x + 1)],
                                     rhs=v_w[a][:].bitcast(FP8X4), rhs_scale=v_s[a][:], start=a == 0, stop=a == 1)
-            reach_sb[x] = ring.tile([P, S], F32, name="reach_sb", tag="raw%d0" % x if x else "reach_first", align_bytes=64)
             if x == 0:
-                nc.vector.tensor_tensor(out=reach_sb[x][:], in0=reach[:], in1=wgs_sb[:], op=MULT)
+                weighted[x] = cell([P, S], F32, "weighted0")
+                nc.vector.tensor_tensor(out=weighted[x][:], in0=reach[:], in1=wgs_sb[:], op=MULT)
             else:
+                reach_sb[x] = cell([P, S], F32, "reach%d" % x)
                 nc.scalar.copy(out=reach_sb[x][:], in_=reach[:])
 
         def shape_stage(x):
-            shape = psum.tile([P, S], F32, name="shape", tag="bank_s")
+            shape_ps[x] = psum.tile([P, S], F32, name="shape", tag="bank_s%d" % (x % 4))
             codes, scales = w1_q[x]
             for a in range(2):
-                nc.tensor.matmul_mx(out=shape[:], lhsT=codes[:, P * a:P * (a + 1)].bitcast(FP8X4),
+                nc.tensor.matmul_mx(out=shape_ps[x][:], lhsT=codes[:, P * a:P * (a + 1)].bitcast(FP8X4),
                                     lhsT_scale=scales[:, P * a:P * (a + 1)],
                                     rhs=v_w[a][:].bitcast(FP8X4), rhs_scale=v_s[a][:], start=a == 0, stop=a == 1)
-            if x == 0:
-                lesson[x] = cell([P, S], F32, "lesson0", 1, 3 * CELL // 4)
-                nc.vector.tensor_tensor(out=lesson[x][:], in0=shape[:], in1=reach_sb[x][:], op=MULT)
-            else:
-                if x < ROW_TILES - 1:
-                    shape_sb[x] = cell([P, S], F32, "shape_sb%d" % x, x + 1, 0)
-                else:
-                    shape_sb[x] = ring.tile([P, S], F32, name="shape_sb")
-                nc.scalar.copy(out=shape_sb[x][:], in_=shape[:])
+
+        def weigh(x):
+            weighted[x] = cell([P, S], F32, "weighted%d" % x)
+            nc.gpsimd.tensor_tensor(out=weighted[x][:], in0=reach_sb[x][:], in1=wgs_sb[:], op=MULT)
+
+        def product_on_vector(x):
+            lesson[x] = cell([P, S], F32, "lesson%d" % x)
+            nc.vector.tensor_tensor(out=lesson[x][:], in0=shape_ps[x][:], in1=weighted[x][:], op=MULT)
 
         def products(x):
-            lesson[x] = cell([P, S], F32, "lesson%d" % x, x, CELL // 4)
+            shape_sb = cell([P, S], F32, "shape%d" % x)
+            nc.scalar.copy(out=shape_sb[:], in_=shape_ps[x][:])
+            lesson[x] = cell([P, S], F32, "lesson%d" % x)
             nc.gpsimd.tensor_tensor(out=lesson[x][:], in0=reach_sb[x][:], in1=wgs_sb[:], op=MULT)
-            nc.gpsimd.tensor_tensor(out=lesson[x][:], in0=lesson[x][:], in1=shape_sb[x][:], op=MULT)
+            nc.gpsimd.tensor_tensor(out=lesson[x][:], in0=lesson[x][:], in1=shape_sb[:], op=MULT)
 
         def scatter(x):
             nc.vector.tensor_copy(out=page[x][:].indirect(edited[:]), in_=lesson[x][:])
@@ -206,19 +218,18 @@ def tile_list_joseki_lesson_gaps_kernel(tc, tab_words, tab_scales, tab2_words, t
         blocks = (4, 2)
         turned = {}
 
-        def turn_rows(x):
+        def turn_rows(x, tags, first=0):
             h, quarter = x // 4, x % 4
             count = blocks[h]
             for bank_index in range(2):
-                bank = psum.tile([P, 4, P], F32, name="turn_bank", tag=(("bank_s", "bank_r") if x < ROW_TILES - 1 else ("bank_e0", "bank_e1"))[bank_index])
+                bank = psum.tile([P, 4, P], F32, name="turn_bank", tag=tags % (first + bank_index))
                 for b in range(4):
                     tb = 4 * bank_index + b
                     nc.tensor.transpose(bank[:, b, :], page[x][:, P * tb:P * (tb + 1)], ident[:])
                 for b0 in range(0, 4, count):
                     g = (4 * bank_index + b0) // count
                     if quarter == 0:
-                        turned[h, g] = ring.tile([P, count, 2, P, 2], BF16, name="turned", tag="turned%d%d" % (h, g),
-                                                 align_bytes=64)
+                        turned[h, g] = cell([P, count, 2, P, 2], BF16, "turned%d%d" % (h, g))
                     nc.scalar.copy(out=turned[h, g][:, :, :, 32 * quarter:32 * (quarter + 1), :].rearrange("t b u q e -> t u b q e"),
                                    in_=bank[:, b0:b0 + count, :].rearrange("t b (q u e) -> t u b q e", u=2, e=2))
 
@@ -235,13 +246,7 @@ def tile_list_joseki_lesson_gaps_kernel(tc, tab_words, tab_scales, tab2_words, t
                                         ident[:])
             g = 2 * pair // count
             if (2 * pair) % count == 0:
-                if (h, g) == (0, 0):
-                    grouped_page[h, g] = cell([P, count * P, 4], BF16, "grouped_first", ROW_TILES - 1, -3 * CELL // 4)
-                elif h == 1:
-                    grouped_page[h, g] = cell([P, count * P, 4], BF16, "grouped_late%d" % g, g, 0)
-                else:
-                    grouped_page[h, g] = ring.tile([P, count * P, 4], BF16, name="grouped_page",
-                                                   tag="grouped%d%d" % (h, g), align_bytes=64)
+                grouped_page[h, g] = cell([P, count * P, 4], BF16, "woven%d%d" % (h, g))
             t0 = (2 * pair) % count * P
             nc.scalar.copy(out=grouped_page[h, g][:, t0:t0 + 2 * P, :].bitcast(F32).rearrange("p (b t) u -> p b t u", b=2),
                            in_=bank[:].rearrange("p b u t -> p b t u"))
@@ -249,63 +254,94 @@ def tile_list_joseki_lesson_gaps_kernel(tc, tab_words, tab_scales, tab2_words, t
         def quant_page(h, g):
             width = blocks[h] * P
             if g == 0:
-                if h == 0:
-                    page_c[h] = cell([P, T2], U32, "page_c0", 6, -CELL // 2)
-                else:
-                    page_c[h] = keep.tile([P, T2], U32, name="page_c1", align_bytes=64)
+                page_c[h] = cell([P, T2], U32, "page_c%d" % h)
                 page_s[h] = keep.tile([P, T2], U8, name="page_s%d" % h, align_bytes=64)
             cols = slice(width * g, width * (g + 1))
             nc.vector.quantize_mx(out=page_c[h][:, cols].bitcast(FP8X4), scales=page_s[h][:, cols],
                                   in_=grouped_page[h, g][:].rearrange("p t i -> p (t i)"))
 
+        half, quarter = S2 // 2, S2 // 4
         reach_stage(0)
         cast_w1(0)
         quant_w1(0, 2)
         cast_w1(1)
         quant_w1(1, 1)
         shape_stage(0)
+        product_on_vector(0)
         reach_stage(1)
-        cast_w1(2)
         shape_stage(1)
-        reach_stage(2)
         products(1)
-        half, quarter = S2 // 2, S2 // 4
-        for x in range(ROW_TILES):
-            if x == 7:
-                quant_page(0, 0)
-                gather_v2("scales", 0, half, cell([P, half], U8, "v2_s_first", 6, CELL // 2))
-                gather_v2(0, 0, quarter, cell([P, quarter], U32, "v2_first", 6, 5 * CELL // 8))
-                quant_page(0, 1)
-            scatter(x)
-            if x + 2 < ROW_TILES:
-                quant_w1(x + 2, 1)
-                if x + 3 < ROW_TILES:
-                    cast_w1(x + 3)
-                shape_stage(x + 2)
-                if x + 3 < ROW_TILES:
-                    reach_stage(x + 3)
-                products(x + 2)
-            if x == 5:
-                for pair in range(4):
-                    turn_back(0, pair, "bank_b%d" % (pair % 2))
-            if x < ROW_TILES - 1:
-                turn_rows(x)
-        gather_v2(1, 0, half, cell([P, half], U32, "v2_second", ROW_TILES - 1, CELL // 2))
-        gather_v2(0, quarter, half, cell([P, quarter], U32, "v2_third", ROW_TILES - 1, CELL // 4))
-        turn_rows(ROW_TILES - 1)
+        scatter(0)
+        cast_w1(2)
+        cast_w1(3)
+        quant_w1(2, 1)
+        shape_stage(2)
+        reach_stage(2)
+        reach_stage(3)
+        weigh(2)
+        scatter(1)
+        product_on_vector(2)
+        cast_w1(4)
+        cast_w1(5)
+        quant_w1(3, 1)
+        quant_w1(4, 1)
+        shape_stage(3)
+        shape_stage(4)
+        reach_stage(4)
+        reach_stage(5)
+        weigh(3)
+        scatter(2)
+        product_on_vector(3)
+        cast_w1(6)
+        cast_w1(7)
+        quant_w1(5, 1)
+        shape_stage(5)
+        products(4)
+        reach_stage(6)
+        reach_stage(7)
+        turn_rows(0, "bank_b%d")
+        turn_rows(1, "bank_r%d")
+        turn_rows(2, "bank_s%d", 2)
+        scatter(3)
+        quant_w1(6, 1)
+        quant_w1(7, 1)
+        shape_stage(6)
+        shape_stage(7)
+        products(5)
+        scatter(4)
+        products(6)
+        scatter(5)
+        products(7)
+        turn_rows(3, "bank_b%d")
+        turn_back(0, 0, "bank_r0")
+        turn_back(0, 1, "bank_r1")
+        turn_back(0, 2, "bank_b0")
+        turn_back(0, 3, "bank_b1")
+        turn_rows(4, "bank_r%d")
+        turn_rows(5, "bank_b%d")
+        scatter(6)
+        turn_rows(6, "bank_r%d")
+        scatter(7)
+        gather_v2("scales", 0, half, cell([P, half], U8, "v2_s_first"))
+        quant_page(0, 0)
+        gather_v2(0, 0, quarter, cell([P, quarter], U32, "v2_first"))
+        quant_page(0, 1)
+        gather_v2(1, 0, half, cell([P, half], U32, "v2_second"))
+        gather_v2(0, quarter, half, cell([P, quarter], U32, "v2_third"))
+        turn_rows(7, "bank_s%d")
         for pair in range(4):
-            turn_back(1, pair, "bank_e%d" % ((pair + 2) % 4))
+            turn_back(1, pair, "bank_s%d" % ((pair + 2) % 4))
             quant_page(1, pair)
             gather_v2(pair % 2, half + quarter * (pair // 2), half + quarter * (pair // 2 + 1),
-                      cell([P, quarter], U32, "v2_late%d" % pair, pair, 0))
-        gather_v2("scales", half, S2, cell([P, half], U8, "v2_s_late", 3, CELL // 4))
+                      cell([P, quarter], U32, "v2_late%d" % pair))
+        gather_v2("scales", half, S2, cell([P, half], U8, "v2_s_late"))
 
         scores = {}
 
         def second_stage(n):
             scores[n] = ring.tile([P, T2], F32, name="scores", tag="rows", bufs=ROW_TILES)
             for c in range(2):
-                acc = psum.tile([P, PASS], F32, name="acc", tag=(("bank_s", "bank_b0"), ("bank_r", "bank_b1"), ("bank_e2", "bank_e0"), ("bank_e3", "bank_e1"))[n % 4][c])
+                acc = psum.tile([P, PASS], F32, name="acc", tag=(("bank_r0", "bank_b0"), ("bank_r1", "bank_b1"), ("bank_s2", "bank_s0"), ("bank_s3", "bank_s1"))[n % 4][c])
                 for h in range(2):
                     words, word_cols = v2[h, n]
                     scales, scale_cols = v2["scales", n]

@@ -22,18 +22,17 @@ P = 128
 PASS = 512
 ROW_TILES = H // P
 MOVE_TILES = S2 // P
-SQUARES_ON_VECTOR = 2
+SQUARES_ON_VECTOR = 0
 PLACE = {
-    "grouped1": 1, "lesson1": 0, "lesson0": 2, "codes3": 0, "codes4": 1,
-    "grouped2": 4, "weighted2": 4, "grouped3": 6, "weighted3": 6,  "lesson2": 41, "codes5": 41,
-    "lesson3": 9, "grouped5": 11, "lesson4": 12, "codes6": 9, "codes7": 10,
-    "raw61": 15, "shape5": 15, "shape4": 17, "lesson6": 13.5, "grouped7": 19, "lesson5": 18, "shape6": 21,
-    "lesson7": 19.5, "page_c0": 15.75, "v2_s_first": 19.75, "v2_first": 20.25, "v2_second": 21.25,
-    "woven00": 43, "v2_third": 43,
-    "woven10": 0, "woven11": 2, "woven12": 4, "woven13": 6,
-    "v2_late0": 0, "v2_late1": 2, "v2_late2": 4, "v2_late3": 6, "v2_s_late": 7,
-    "raw20": 23, "reach2": 23, "reach3": 25, "raw40": 27, "reach4": 27, "reach5": 29,
-    "raw60": 33, "turned00": 31, "turned01": 35, "raw10": 39, "reach1": 39,
+    "raw01": 2, "reach1": 0.25, "reach2": 2.25, "reach3": 4.25, "wg2": 6.25, "wg3": 8.25,
+    "raw10": 11, "reach4": 11, "reach5": 13, "reach6": 15, "reach7": 17,
+    "raw11": 22, "pairs00": 19, "pairs01": 23, "shape3": 27, "shape6": 29,
+    "grouped012": 33, "lesson1": 32, "v2_s_late": 34, "lesson0": 34.5, "lesson2": 35.5, "shape1": 37, "shape2": 30, "lesson3": 31,
+    "codes100": 34.5, "codes110": 36.5, "grouped110": 40, "weighted4": 40, "lesson4": 44, "shape5": 46, "lesson6": 45,
+    "lesson5": 32, "lesson7": 30.5,
+    "page_c0": 26.75, "v2_00": 30.75, "v2_10": 31.75,
+    "woven11": 56, "v2_01": 55.5, "v2_11": 56.5, "v2_02": 58, "v2_12": 59,
+    "w2_s1": 38.5, "scores0": 48, "v2_03": 48, "v2_13": 49,
 }
 
 
@@ -58,10 +57,10 @@ def tile_list_joseki_lesson_gaps_kernel(tc, tab_words, tab_scales, tab2_words, t
         open_lessons = lists.tile([P, PICK // 16], U16, name="open_lessons")
 
         tab_s = keep.tile([P, 2, T], U8, name="tab_s", align_bytes=64)
-        w2_s = keep.tile([P, 2, H], U8, name="w2_s", align_bytes=64)
+        w2_s_raw = keep.tile([P, 2, H], U8, name="w2_s_raw", align_bytes=64)
         tab2_s = keep.tile([P, T3], U8, name="tab2_s", align_bytes=64)
         nc.vector.memset(tab_s[:].bitcast(I32), 0)
-        nc.gpsimd.memset(w2_s[:].bitcast(I32), 0)
+        nc.gpsimd.memset(w2_s_raw[:].bitcast(I32), 0)
         nc.vector.memset(tab2_s[:].bitcast(I32), 0)
 
         def load_words(src, a, tag):
@@ -76,60 +75,48 @@ def tile_list_joseki_lesson_gaps_kernel(tc, tab_words, tab_scales, tab2_words, t
 
         w1_raw = {}
 
-        def load_w1(x0, x1):
-            for a in range(2):
-                raw = cell([P, 4, P * (x1 - x0)], F32, "raw%d%d" % (x0, a))
-                nc.sync.dma_start(out=raw[:],
-                                  in_=w1[PASS * a:PASS * (a + 1), P * x0:P * x1].rearrange("(p j) c -> p j c", j=4))
-                for x in range(x0, x1):
-                    w1_raw[x, a] = raw[:, :, P * (x - x0):P * (x - x0 + 1)]
+        def load_w1(h, a):
+            w1_raw[h, a] = cell([P, 4, PASS], F32, "raw%d%d" % (h, a))
+            nc.sync.dma_start(out=w1_raw[h, a][:], in_=w1[PASS * a:PASS * (a + 1), PASS * h:PASS * (h + 1)]
+                              .rearrange("(p j) c -> p j c", j=4))
 
         page = {}
 
         def load_page(x):
+            h, i = divmod(x, 4)
             page[x] = ring.tile([P, T2], F32, name="page", tag="rows", bufs=ROW_TILES)
-            nc.sync.dma_start(out=page[x][:], in_=page0[P * x:P * (x + 1), :])
+            nc.sync.dma_start(out=page[x][:],
+                              in_=page0[PASS * h:PASS * (h + 1), :].rearrange("(p i) t -> p i t", i=4)[:, i, :])
 
         def load_komi(g):
             rows = ring.tile([P, 4, PICK], F32, name="komi_sb", tag="tab_w%d" % g, align_bytes=64)
             nc.sync.dma_start(out=rows[:], in_=komi[PASS * g:PASS * (g + 1), :].rearrange("(c p) m -> p c m", p=P))
             return rows
 
-        w2_w = {}
-
-        def load_w2(x0, x1):
-            words = keep.tile([P, 2, 2 * P * (x1 - x0)], U8, name="w2_w%d" % x0, align_bytes=64)
-            nc.sync.dma_start(out=words[:].bitcast(I32),
-                              in_=w2_words[:, :, 2 * P * x0:2 * P * x1].rearrange("a p c -> p a c").bitcast(I32))
-            for x in range(x0, x1):
-                for a in range(2):
-                    w2_w[x, a] = words[:, a, 2 * P * (x - x0):2 * P * (x - x0 + 1)]
-
         tab_w = [load_words(tab_words, 0, "tab_w0")]
         nc.sync.dma_start(corners[:], offs)
-        load_scales(nc.sync, tab_s, tab_scales)
-        tab_w.append(load_words(tab_words, 1, "tab_w1"))
-        load_w2(0, 4)
-        load_scales(nc.sync, w2_s, w2_scales)
-        load_w1(0, 1)
         wgs_sb = keep.tile([P, S], F32, name="wgs_sb")
         nc.sync.dma_start(out=wgs_sb[:], in_=wgs)
-        load_w1(1, 2)
-        load_page(0)
-        nc.sync.dma_start(edited[:], offs3)
-        load_w1(2, 4)
-        load_w2(4, ROW_TILES)
-        load_page(1)
-        load_w1(4, 6)
+        load_scales(nc.sync, tab_s, tab_scales)
+        tab_w.append(load_words(tab_words, 1, "tab_w1"))
+        w2_raw = keep.tile([P, 2, 2 * H], U8, name="w2_raw", align_bytes=64)
+        nc.sync.dma_start(out=w2_raw[:].bitcast(I32), in_=w2_words.rearrange("a p c -> p a c").bitcast(I32))
+        load_scales(nc.sync, w2_s_raw, w2_scales)
+        load_w1(0, 0)
         nc.sync.dma_start(moves[:], offs2)
-        nc.sync.dma_start(open_lessons[:], offs4)
-        load_page(2)
-        load_w1(6, 8)
-        load_page(3)
-        load_page(4)
         for q in range(4):
             nc.sync.dma_start(out=tab2_s[32 * q:32 * q + 8, :].bitcast(I32),
                               in_=tab2_scales[:, 4 * q:4 * q + 4, :].bitcast(I32))
+        load_w1(0, 1)
+        load_page(0)
+        nc.sync.dma_start(edited[:], offs3)
+        load_page(1)
+        load_w1(1, 0)
+        load_w1(1, 1)
+        nc.sync.dma_start(open_lessons[:], offs4)
+        load_page(2)
+        load_page(3)
+        load_page(4)
         load_page(5)
         tab2_w = [load_words(tab2_words, a, "tab2_w%d" % a) for a in range(2)]
         load_page(6)
@@ -149,23 +136,48 @@ def tile_list_joseki_lesson_gaps_kernel(tc, tab_words, tab_scales, tab2_words, t
             v_w.append(picked_w)
         komi_sb = [load_komi(0), load_komi(1)]
 
+        w2_w = keep.tile([P, 4, 4, 2 * P], U8, name="w2_w", align_bytes=64)
+        w2_s = {}
+        nc.vector.tensor_copy(out=w2_w[:].bitcast(U16),
+                              in_=w2_raw[:].bitcast(U16).rearrange("p a (h m i) -> p (a h) i m", h=2, i=4))
+
+        def deal_w2_scales(h):
+            w2_s[h] = cell([P, 2, 4, P], U8, "w2_s%d" % h)
+            nc.gpsimd.tensor_copy(out=w2_s[h][:],
+                                  in_=w2_s_raw[:, :, PASS * h:PASS * (h + 1)].rearrange("p a (m i) -> p a i m", i=4))
+
+        deal_w2_scales(0)
+
+        wgs_t_ps = psum.tile([P, 4, P], F32, name="wgs_t_ps", tag="bank_s3")
+        for b in range(4):
+            nc.tensor.transpose(wgs_t_ps[:, b, :], wgs_sb[:, P * b:P * (b + 1)], ident[:])
+        wgs_t = keep.tile([P, 4, 4, 4, 32], F32, name="wgs_t")
+        nc.scalar.copy(out=wgs_t[:],
+                       in_=wgs_t_ps[:].rearrange("j b (q i) -> j b i q", i=4).unsqueeze(3).to_broadcast([P, 4, 4, 4, 32]))
+        wg = {}
+
+        def deal_wgs(i):
+            bank = psum.tile([P, 4, P], F32, name="wg_bank", tag=("bank_b0", "bank_b1", "bank_s2", "bank_s3")[i])
+            for b in range(4):
+                nc.tensor.transpose(bank[:, b, :], wgs_t[:, b, i, :, :].rearrange("j g q -> j (g q)"), ident[:])
+            wg[i] = cell([P, S], F32, "wg%d" % i)
+            nc.scalar.copy(out=wg[i][:], in_=bank[:].rearrange("p b j -> p (b j)"))
+
         w1_grouped, w1_q = {}, {}
 
-        def cast_w1(x):
-            w1_grouped[x] = cell([P, 2, P, 4], BF16, "grouped%d" % x)
-            for a in range(2):
-                nc.scalar.copy(out=w1_grouped[x][:, a].rearrange("p (c i) j -> p c j i", i=4),
-                               in_=w1_raw[x, a].rearrange("p j (c i) -> p c j i", i=4))
+        def cast_w1(h, a, i0, i1, copy):
+            w1_grouped[h, a, i0] = cell([P, i1 - i0, P, 4], BF16, "grouped%d%d%d" % (h, a, i0))
+            copy(out=w1_grouped[h, a, i0][:].rearrange("p i m j -> p m j i"),
+                 in_=w1_raw[h, a][:].rearrange("p j (m i) -> p m j i", i=4)[:, :, :, i0:i1])
 
-        def quant_w1(x, parts):
-            codes = cell([P, 2 * P], U32, "codes%d" % x)
-            scales = keep.tile([P, 2 * P], U8, name="w1_s%d" % x, align_bytes=64)
-            width = 2 * P // parts
-            for k in range(parts):
-                cols = slice(width * k, width * (k + 1))
-                nc.vector.quantize_mx(out=codes[:, cols].bitcast(FP8X4), scales=scales[:, cols],
-                                      in_=w1_grouped[x][:].rearrange("p a c j -> p (a c j)")[:, 4 * width * k:4 * width * (k + 1)])
-            w1_q[x] = (codes, scales)
+        def quant_w1(h, a, i0, i1):
+            codes = cell([P, (i1 - i0) * P], U32, "codes%d%d%d" % (h, a, i0))
+            scales = keep.tile([P, (i1 - i0) * P], U8, name="w1_s%d%d%d" % (h, a, i0), align_bytes=64)
+            nc.vector.quantize_mx(out=codes[:].bitcast(FP8X4), scales=scales[:],
+                                  in_=w1_grouped[h, a, i0][:].rearrange("p i m j -> p (i m j)"))
+            for i in range(i0, i1):
+                cols = slice(P * (i - i0), P * (i - i0 + 1))
+                w1_q[4 * h + i, a] = (codes[:, cols], scales[:, cols])
 
         v2 = {}
 
@@ -180,26 +192,25 @@ def tile_list_joseki_lesson_gaps_kernel(tc, tab_words, tab_scales, tab2_words, t
         def reach_stage(x):
             reach = psum.tile([P, S], F32, name="reach", tag="bank_r%d" % (x % 2))
             for a in range(2):
-                nc.tensor.matmul_mx(out=reach[:], lhsT=w2_w[x, a].bitcast(FP4X4), lhsT_scale=w2_s[:, a, P * x:P * (x + 1)],
+                nc.tensor.matmul_mx(out=reach[:], lhsT=w2_w[:, 2 * a + x // 4, x % 4, :].bitcast(FP4X4),
+                                    lhsT_scale=w2_s[x // 4][:, a, x % 4, :],
                                     rhs=v_w[a][:].bitcast(FP8X4), rhs_scale=v_s[a][:], start=a == 0, stop=a == 1)
             if x == 0:
                 weighted[x] = cell([P, S], F32, "weighted0")
-                nc.vector.tensor_tensor(out=weighted[x][:], in0=reach[:], in1=wgs_sb[:], op=MULT)
+                nc.vector.tensor_tensor(out=weighted[x][:], in0=reach[:], in1=wg[x % 4][:], op=MULT)
             else:
                 reach_sb[x] = cell([P, S], F32, "reach%d" % x)
                 nc.scalar.copy(out=reach_sb[x][:], in_=reach[:])
 
         def shape_stage(x):
             shape_ps[x] = psum.tile([P, S], F32, name="shape", tag="bank_s%d" % (x % 4))
-            codes, scales = w1_q[x]
             for a in range(2):
-                nc.tensor.matmul_mx(out=shape_ps[x][:], lhsT=codes[:, P * a:P * (a + 1)].bitcast(FP8X4),
-                                    lhsT_scale=scales[:, P * a:P * (a + 1)],
+                nc.tensor.matmul_mx(out=shape_ps[x][:], lhsT=w1_q[x, a][0].bitcast(FP8X4), lhsT_scale=w1_q[x, a][1],
                                     rhs=v_w[a][:].bitcast(FP8X4), rhs_scale=v_s[a][:], start=a == 0, stop=a == 1)
 
         def weigh(x):
             weighted[x] = cell([P, S], F32, "weighted%d" % x)
-            nc.gpsimd.tensor_tensor(out=weighted[x][:], in0=reach_sb[x][:], in1=wgs_sb[:], op=MULT)
+            nc.gpsimd.tensor_tensor(out=weighted[x][:], in0=reach_sb[x][:], in1=wg[x % 4][:], op=MULT)
 
         def product_on_vector(x):
             lesson[x] = cell([P, S], F32, "lesson%d" % x)
@@ -209,50 +220,28 @@ def tile_list_joseki_lesson_gaps_kernel(tc, tab_words, tab_scales, tab2_words, t
             shape_sb = cell([P, S], F32, "shape%d" % x)
             nc.scalar.copy(out=shape_sb[:], in_=shape_ps[x][:])
             lesson[x] = cell([P, S], F32, "lesson%d" % x)
-            nc.gpsimd.tensor_tensor(out=lesson[x][:], in0=reach_sb[x][:], in1=wgs_sb[:], op=MULT)
+            nc.gpsimd.tensor_tensor(out=lesson[x][:], in0=reach_sb[x][:], in1=wg[x % 4][:], op=MULT)
             nc.gpsimd.tensor_tensor(out=lesson[x][:], in0=lesson[x][:], in1=shape_sb[:], op=MULT)
 
         def scatter(x):
             nc.vector.tensor_copy(out=page[x][:].indirect(edited[:]), in_=lesson[x][:])
 
-        blocks = (4, 2)
-        turned = {}
+        pairs, page_c, page_s, grouped_page = {}, {}, {}, {}
 
-        def turn_rows(x, tags, first=0):
-            h, quarter = x // 4, x % 4
-            count = blocks[h]
-            for bank_index in range(2):
-                bank = psum.tile([P, 4, P], F32, name="turn_bank", tag=tags % (first + bank_index))
-                for b in range(4):
-                    tb = 4 * bank_index + b
-                    nc.tensor.transpose(bank[:, b, :], page[x][:, P * tb:P * (tb + 1)], ident[:])
-                for b0 in range(0, 4, count):
-                    g = (4 * bank_index + b0) // count
-                    if quarter == 0:
-                        turned[h, g] = cell([P, count, 2, P, 2], BF16, "turned%d%d" % (h, g))
-                    nc.scalar.copy(out=turned[h, g][:, :, :, 32 * quarter:32 * (quarter + 1), :].rearrange("t b u q e -> t u b q e"),
-                                   in_=bank[:, b0:b0 + count, :].rearrange("t b (q u e) -> t u b q e", u=2, e=2))
+        def cast_page(x):
+            h, i = divmod(x, 4)
+            for c in range(2):
+                if i == 0:
+                    pairs[h, c] = cell([P, 2, PASS, 2], BF16, "pairs%d%d" % (h, c))
+                nc.scalar.copy(out=pairs[h, c][:, i // 2, :, i % 2], in_=page[x][:, PASS * c:PASS * (c + 1)])
 
-        page_c, page_s, grouped_page = {}, {}, {}
-
-        def turn_back(h, pair, tag):
-            count = blocks[h]
-            bank = psum.tile([P, 2, 2, P], F32, name="back_bank", tag=tag)
-            for b in range(2):
-                tb = 2 * pair + b
-                for u in range(2):
-                    nc.tensor.transpose(bank[:, b, u, :],
-                                        turned[h, tb // count][:, tb % count, u].rearrange("t p e -> t (p e)").bitcast(F32),
-                                        ident[:])
-            g = 2 * pair // count
-            if (2 * pair) % count == 0:
-                grouped_page[h, g] = cell([P, count * P, 4], BF16, "woven%d%d" % (h, g))
-            t0 = (2 * pair) % count * P
-            nc.scalar.copy(out=grouped_page[h, g][:, t0:t0 + 2 * P, :].bitcast(F32).rearrange("p (b t) u -> p b t u", b=2),
-                           in_=bank[:].rearrange("p b u t -> p b t u"))
+        def weave_page(h, c, copy):
+            grouped_page[h, c] = cell([P, PASS, 4], BF16, "woven%d%d" % (h, c))
+            copy(out=grouped_page[h, c][:].bitcast(F32),
+                 in_=pairs[h, c][:].rearrange("p u t e -> p (u t e)").bitcast(F32).rearrange("p (u t) -> p t u", u=2))
 
         def quant_page(h, g):
-            width = blocks[h] * P
+            width = PASS
             if g == 0:
                 page_c[h] = cell([P, T2], U32, "page_c%d" % h)
                 page_s[h] = keep.tile([P, T2], U8, name="page_s%d" % h, align_bytes=64)
@@ -261,85 +250,82 @@ def tile_list_joseki_lesson_gaps_kernel(tc, tab_words, tab_scales, tab2_words, t
                                   in_=grouped_page[h, g][:].rearrange("p t i -> p (t i)"))
 
         half, quarter = S2 // 2, S2 // 4
+        deal_wgs(0)
+        deal_wgs(1)
+        cast_w1(0, 0, 0, 2, nc.scalar.copy)
+        cast_w1(0, 0, 2, 4, nc.scalar.copy)
+        gather_v2("scales", 0, half, cell([P, half], U8, "v2_s_first"))
+        quant_w1(0, 0, 0, 2)
         reach_stage(0)
-        cast_w1(0)
-        quant_w1(0, 2)
-        cast_w1(1)
-        quant_w1(1, 1)
+        cast_w1(0, 1, 0, 2, nc.vector.tensor_copy)
+        cast_w1(0, 1, 2, 4, nc.scalar.copy)
+        quant_w1(0, 0, 2, 4)
+        quant_w1(0, 1, 0, 2)
         shape_stage(0)
+        quant_w1(0, 1, 2, 4)
+        gather_v2("scales", half, S2, cell([P, half], U8, "v2_s_late"))
         product_on_vector(0)
         reach_stage(1)
         shape_stage(1)
         products(1)
+        deal_w2_scales(1)
         scatter(0)
-        cast_w1(2)
-        cast_w1(3)
-        quant_w1(2, 1)
-        shape_stage(2)
+        deal_wgs(2)
+        deal_wgs(3)
         reach_stage(2)
+        shape_stage(2)
+        products(2)
         reach_stage(3)
-        weigh(2)
-        scatter(1)
-        product_on_vector(2)
-        cast_w1(4)
-        cast_w1(5)
-        quant_w1(3, 1)
-        quant_w1(4, 1)
         shape_stage(3)
-        shape_stage(4)
-        reach_stage(4)
-        reach_stage(5)
-        weigh(3)
+        scatter(1)
+        cast_w1(1, 0, 0, 4, nc.scalar.copy)
+        cast_w1(1, 1, 0, 4, nc.scalar.copy)
+        products(3)
         scatter(2)
-        product_on_vector(3)
-        cast_w1(6)
-        cast_w1(7)
-        quant_w1(5, 1)
-        shape_stage(5)
-        products(4)
-        reach_stage(6)
-        reach_stage(7)
-        turn_rows(0, "bank_b%d")
-        turn_rows(1, "bank_r%d")
-        turn_rows(2, "bank_s%d", 2)
+        quant_w1(1, 0, 0, 4)
+        quant_w1(1, 1, 0, 4)
+        for x in range(4, ROW_TILES):
+            reach_stage(x)
+        for x in range(4, ROW_TILES):
+            shape_stage(x)
+        weigh(4)
         scatter(3)
-        quant_w1(6, 1)
-        quant_w1(7, 1)
-        shape_stage(6)
-        shape_stage(7)
+        product_on_vector(4)
         products(5)
         scatter(4)
         products(6)
         scatter(5)
         products(7)
-        turn_rows(3, "bank_b%d")
-        turn_back(0, 0, "bank_r0")
-        turn_back(0, 1, "bank_r1")
-        turn_back(0, 2, "bank_b0")
-        turn_back(0, 3, "bank_b1")
-        turn_rows(4, "bank_r%d")
-        turn_rows(5, "bank_b%d")
+        for x in range(4):
+            cast_page(x)
+        weave_page(0, 0, nc.scalar.copy)
+        weave_page(0, 1, nc.scalar.copy)
+        cast_page(4)
+        cast_page(5)
         scatter(6)
-        turn_rows(6, "bank_r%d")
+        cast_page(6)
         scatter(7)
-        gather_v2("scales", 0, half, cell([P, half], U8, "v2_s_first"))
+        cast_page(7)
         quant_page(0, 0)
-        gather_v2(0, 0, quarter, cell([P, quarter], U32, "v2_first"))
+        gather_v2(0, 0, quarter, cell([P, quarter], U32, "v2_00"))
+        weave_page(1, 0, nc.vector.tensor_copy)
+        gather_v2(1, 0, quarter, cell([P, quarter], U32, "v2_10"))
+        quant_page(1, 0)
         quant_page(0, 1)
-        gather_v2(1, 0, half, cell([P, half], U32, "v2_second"))
-        gather_v2(0, quarter, half, cell([P, quarter], U32, "v2_third"))
-        turn_rows(7, "bank_s%d")
-        for pair in range(4):
-            turn_back(1, pair, "bank_s%d" % ((pair + 2) % 4))
-            quant_page(1, pair)
-            gather_v2(pair % 2, half + quarter * (pair // 2), half + quarter * (pair // 2 + 1),
-                      cell([P, quarter], U32, "v2_late%d" % pair))
-        gather_v2("scales", half, S2, cell([P, half], U8, "v2_s_late"))
+        weave_page(1, 1, nc.scalar.copy)
+        quant_page(1, 1)
+        gather_v2(0, quarter, half, cell([P, quarter], U32, "v2_01"))
+        gather_v2(1, quarter, half, cell([P, quarter], U32, "v2_11"))
+        gather_v2(0, half, half + quarter, cell([P, quarter], U32, "v2_02"))
+        gather_v2(1, half, half + quarter, cell([P, quarter], U32, "v2_12"))
 
         scores = {}
 
         def second_stage(n):
-            scores[n] = ring.tile([P, T2], F32, name="scores", tag="rows", bufs=ROW_TILES)
+            if n == 0:
+                scores[n] = cell([P, T2], F32, "scores0")
+            else:
+                scores[n] = ring.tile([P, T2], F32, name="scores", tag="rows", bufs=ROW_TILES)
             for c in range(2):
                 acc = psum.tile([P, PASS], F32, name="acc", tag=(("bank_r0", "bank_b0"), ("bank_r1", "bank_b1"), ("bank_s2", "bank_s0"), ("bank_s3", "bank_s1"))[n % 4][c])
                 for h in range(2):
@@ -355,6 +341,9 @@ def tile_list_joseki_lesson_gaps_kernel(tc, tab_words, tab_scales, tab2_words, t
         second_stage(0)
         second_stage(1)
         for n in range(MOVE_TILES):
+            if n == 1:
+                gather_v2(0, half + quarter, S2, cell([P, quarter], U32, "v2_03"))
+                gather_v2(1, half + quarter, S2, cell([P, quarter], U32, "v2_13"))
             if n + 2 < MOVE_TILES:
                 second_stage(n + 2)
             for m0, m1 in ([(0, PICK)] if n < MOVE_TILES - 1 else [(0, PICK // 2), (PICK // 2, PICK)]):

@@ -24,15 +24,15 @@ ROW_TILES = H // P
 MOVE_TILES = S2 // P
 SQUARES_ON_VECTOR = 0
 PLACE = {
-    "raw01": 2, "reach1": 0.25, "reach2": 2.25, "reach3": 4.25, "wg2": 6.25, "wg3": 8.25,
+    "raw01": 2, "wg2": 0.25, "reach1": 2.25, "reach2": 4.25, "reach3": 6.25, "wg3": 8.25,
     "raw10": 11, "reach4": 11, "reach5": 13, "reach6": 15, "reach7": 17,
     "raw11": 22, "pairs00": 19, "pairs01": 23, "shape3": 27, "shape6": 29,
-    "grouped012": 33, "lesson1": 32, "v2_s_late": 34, "lesson0": 34.5, "lesson2": 35.5, "shape1": 37, "shape2": 30, "lesson3": 31,
+    "grouped012": 33, "lesson1": 32, "lesson0": 34.5, "lesson2": 35.5, "shape1": 37, "shape2": 30, "lesson3": 31,
     "codes100": 34.5, "codes110": 36.5, "grouped110": 40, "weighted4": 40, "lesson4": 44, "shape5": 46, "lesson6": 45,
     "lesson5": 32, "lesson7": 30.5,
     "page_c0": 26.75, "v2_00": 30.75, "v2_10": 31.75,
-    "woven11": 56, "v2_01": 55.5, "v2_11": 56.5, "v2_02": 58, "v2_12": 59,
-    "w2_s1": 38.5, "scores0": 48, "v2_03": 48, "v2_13": 49,
+    "pairs11": 52, "v2_01": 52, "v2_11": 53, "v2_02": 54, "v2_12": 55, "v2_03": 52, "v2_13": 53,
+    "w2_s1": 38.5, "grouped010": 61, "w2_w1": 61,
 }
 
 
@@ -60,8 +60,10 @@ def tile_list_joseki_lesson_gaps_kernel(tc, tab_words, tab_scales, tab2_words, t
         w2_s_raw = keep.tile([P, 2, H], U8, name="w2_s_raw", align_bytes=64)
         tab2_s = keep.tile([P, T3], U8, name="tab2_s", align_bytes=64)
         nc.vector.memset(tab_s[:].bitcast(I32), 0)
-        nc.gpsimd.memset(w2_s_raw[:].bitcast(I32), 0)
-        nc.vector.memset(tab2_s[:].bitcast(I32), 0)
+        nc.vector.memset(w2_s_raw[:].bitcast(I32), 0)
+        ident = keep.tile([P, P], F32, name="ident")
+        make_identity(nc, ident[:])
+        nc.gpsimd.memset(tab2_s[:].bitcast(I32), 0)
 
         def load_words(src, a, tag):
             words = ring.tile([P, T], I32, name="words", tag=tag, align_bytes=64)
@@ -93,21 +95,28 @@ def tile_list_joseki_lesson_gaps_kernel(tc, tab_words, tab_scales, tab2_words, t
             nc.sync.dma_start(out=rows[:], in_=komi[PASS * g:PASS * (g + 1), :].rearrange("(c p) m -> p c m", p=P))
             return rows
 
+        w2_raw = {}
+
+        def load_w2(h):
+            w2_raw[h] = keep.tile([P, 2, H], U8, name="w2_raw%d" % h, align_bytes=64)
+            nc.sync.dma_start(out=w2_raw[h][:].bitcast(I32),
+                              in_=w2_words[:, :, H * h:H * (h + 1)].rearrange("a p c -> p a c").bitcast(I32))
+
         tab_w = [load_words(tab_words, 0, "tab_w0")]
         nc.sync.dma_start(corners[:], offs)
         wgs_sb = keep.tile([P, S], F32, name="wgs_sb")
         nc.sync.dma_start(out=wgs_sb[:], in_=wgs)
         load_scales(nc.sync, tab_s, tab_scales)
         tab_w.append(load_words(tab_words, 1, "tab_w1"))
-        w2_raw = keep.tile([P, 2, 2 * H], U8, name="w2_raw", align_bytes=64)
-        nc.sync.dma_start(out=w2_raw[:].bitcast(I32), in_=w2_words.rearrange("a p c -> p a c").bitcast(I32))
+        load_w2(0)
         load_scales(nc.sync, w2_s_raw, w2_scales)
-        load_w1(0, 0)
         nc.sync.dma_start(moves[:], offs2)
+        load_w1(0, 0)
         for q in range(4):
-            nc.sync.dma_start(out=tab2_s[32 * q:32 * q + 8, :].bitcast(I32),
-                              in_=tab2_scales[:, 4 * q:4 * q + 4, :].bitcast(I32))
+            nc.gpsimd.dma_start(out=tab2_s[32 * q:32 * q + 8, :].bitcast(I32),
+                                in_=tab2_scales[:, 4 * q:4 * q + 4, :].bitcast(I32))
         load_w1(0, 1)
+        load_w2(1)
         load_page(0)
         nc.sync.dma_start(edited[:], offs3)
         load_page(1)
@@ -122,9 +131,6 @@ def tile_list_joseki_lesson_gaps_kernel(tc, tab_words, tab_scales, tab2_words, t
         load_page(6)
         load_page(7)
 
-        ident = keep.tile([P, P], F32, name="ident")
-        make_identity(nc, ident[:])
-
         v_s, v_w = [], []
         for a in range(2):
             picked_s = keep.tile([P, S], U8, name="v_s%d" % a, align_bytes=64)
@@ -136,16 +142,19 @@ def tile_list_joseki_lesson_gaps_kernel(tc, tab_words, tab_scales, tab2_words, t
             v_w.append(picked_w)
         komi_sb = [load_komi(0), load_komi(1)]
 
-        w2_w = keep.tile([P, 4, 4, 2 * P], U8, name="w2_w", align_bytes=64)
-        w2_s = {}
-        nc.vector.tensor_copy(out=w2_w[:].bitcast(U16),
-                              in_=w2_raw[:].bitcast(U16).rearrange("p a (h m i) -> p (a h) i m", h=2, i=4))
+        w2_w, w2_s = {}, {}
+
+        def deal_w2_words(h):
+            w2_w[h] = cell([P, 2, 4, 2 * P], U8, "w2_w%d" % h)
+            nc.vector.tensor_copy(out=w2_w[h][:].bitcast(U16),
+                                  in_=w2_raw[h][:].bitcast(U16).rearrange("p a (m i) -> p a i m", i=4))
 
         def deal_w2_scales(h):
             w2_s[h] = cell([P, 2, 4, P], U8, "w2_s%d" % h)
             nc.gpsimd.tensor_copy(out=w2_s[h][:],
                                   in_=w2_s_raw[:, :, PASS * h:PASS * (h + 1)].rearrange("p a (m i) -> p a i m", i=4))
 
+        deal_w2_words(0)
         deal_w2_scales(0)
 
         wgs_t_ps = psum.tile([P, 4, P], F32, name="wgs_t_ps", tag="bank_s3")
@@ -192,7 +201,7 @@ def tile_list_joseki_lesson_gaps_kernel(tc, tab_words, tab_scales, tab2_words, t
         def reach_stage(x):
             reach = psum.tile([P, S], F32, name="reach", tag="bank_r%d" % (x % 2))
             for a in range(2):
-                nc.tensor.matmul_mx(out=reach[:], lhsT=w2_w[:, 2 * a + x // 4, x % 4, :].bitcast(FP4X4),
+                nc.tensor.matmul_mx(out=reach[:], lhsT=w2_w[x // 4][:, a, x % 4, :].bitcast(FP4X4),
                                     lhsT_scale=w2_s[x // 4][:, a, x % 4, :],
                                     rhs=v_w[a][:].bitcast(FP8X4), rhs_scale=v_s[a][:], start=a == 0, stop=a == 1)
             if x == 0:
@@ -255,6 +264,7 @@ def tile_list_joseki_lesson_gaps_kernel(tc, tab_words, tab_scales, tab2_words, t
         cast_w1(0, 0, 0, 2, nc.scalar.copy)
         cast_w1(0, 0, 2, 4, nc.scalar.copy)
         gather_v2("scales", 0, half, cell([P, half], U8, "v2_s_first"))
+        gather_v2("scales", half, S2, cell([P, half], U8, "v2_s_late"))
         quant_w1(0, 0, 0, 2)
         reach_stage(0)
         cast_w1(0, 1, 0, 2, nc.vector.tensor_copy)
@@ -263,7 +273,7 @@ def tile_list_joseki_lesson_gaps_kernel(tc, tab_words, tab_scales, tab2_words, t
         quant_w1(0, 1, 0, 2)
         shape_stage(0)
         quant_w1(0, 1, 2, 4)
-        gather_v2("scales", half, S2, cell([P, half], U8, "v2_s_late"))
+        deal_w2_words(1)
         product_on_vector(0)
         reach_stage(1)
         shape_stage(1)
@@ -322,10 +332,7 @@ def tile_list_joseki_lesson_gaps_kernel(tc, tab_words, tab_scales, tab2_words, t
         scores = {}
 
         def second_stage(n):
-            if n == 0:
-                scores[n] = cell([P, T2], F32, "scores0")
-            else:
-                scores[n] = ring.tile([P, T2], F32, name="scores", tag="rows", bufs=ROW_TILES)
+            scores[n] = ring.tile([P, T2], F32, name="scores", tag="rows", bufs=ROW_TILES)
             for c in range(2):
                 acc = psum.tile([P, PASS], F32, name="acc", tag=(("bank_r0", "bank_b0"), ("bank_r1", "bank_b1"), ("bank_s2", "bank_s0"), ("bank_s3", "bank_s1"))[n % 4][c])
                 for h in range(2):

@@ -32,7 +32,7 @@ PLACE = {
     "lesson5": 32, "lesson7": 30.5,
     "page_c0": 26.75, "v2_00": 30.75, "v2_10": 31.75,
     "pairs11": 52, "v2_01": 52, "v2_11": 53, "v2_02": 54, "v2_12": 55, "v2_03": 52, "v2_13": 53,
-    "w2_s1": 38.5, "grouped010": 61, "w2_w1": 61,
+    "shape7": 48, "woven01": 47, "grouped010": 61, "w2_w1": 61,
 }
 
 
@@ -156,6 +156,7 @@ def tile_list_joseki_lesson_gaps_kernel(tc, tab_words, tab_scales, tab2_words, t
 
         deal_w2_words(0)
         deal_w2_scales(0)
+        deal_w2_scales(1)
 
         wgs_t_ps = psum.tile([P, 4, P], F32, name="wgs_t_ps", tag="bank_s3")
         for b in range(4):
@@ -199,7 +200,7 @@ def tile_list_joseki_lesson_gaps_kernel(tc, tab_words, tab_scales, tab2_words, t
         reach_sb, shape_ps, weighted, lesson = {}, {}, {}, {}
 
         def reach_stage(x):
-            reach = psum.tile([P, S], F32, name="reach", tag="bank_r%d" % (x % 2))
+            reach = psum.tile([P, S], F32, name="reach", tag="bank_r%d" % (x > 0 and x % 2 == 0))
             for a in range(2):
                 nc.tensor.matmul_mx(out=reach[:], lhsT=w2_w[x // 4][:, a, x % 4, :].bitcast(FP4X4),
                                     lhsT_scale=w2_s[x // 4][:, a, x % 4, :],
@@ -246,8 +247,8 @@ def tile_list_joseki_lesson_gaps_kernel(tc, tab_words, tab_scales, tab2_words, t
 
         def weave_page(h, c, copy):
             grouped_page[h, c] = cell([P, PASS, 4], BF16, "woven%d%d" % (h, c))
-            copy(out=grouped_page[h, c][:].bitcast(F32),
-                 in_=pairs[h, c][:].rearrange("p u t e -> p (u t e)").bitcast(F32).rearrange("p (u t) -> p t u", u=2))
+            copy(out=grouped_page[h, c][:].bitcast(U32),
+                 in_=pairs[h, c][:].rearrange("p u t e -> p (u t e)").bitcast(U32).rearrange("p (u t) -> p t u", u=2))
 
         def quant_page(h, g):
             width = PASS
@@ -278,7 +279,6 @@ def tile_list_joseki_lesson_gaps_kernel(tc, tab_words, tab_scales, tab2_words, t
         reach_stage(1)
         shape_stage(1)
         products(1)
-        deal_w2_scales(1)
         scatter(0)
         deal_wgs(2)
         deal_wgs(3)
@@ -309,7 +309,7 @@ def tile_list_joseki_lesson_gaps_kernel(tc, tab_words, tab_scales, tab2_words, t
         for x in range(4):
             cast_page(x)
         weave_page(0, 0, nc.scalar.copy)
-        weave_page(0, 1, nc.scalar.copy)
+        weave_page(0, 1, nc.gpsimd.tensor_copy)
         cast_page(4)
         cast_page(5)
         scatter(6)

@@ -113,7 +113,7 @@ def tile_list_joseki_lesson_gaps_kernel(tc, tab_words, tab_scales, tab2_words, t
         nc.sync.dma_start(moves[:], offs2)
         load_w1(0, 0)
         for q in range(4):
-            nc.gpsimd.dma_start(out=tab2_s[32 * q:32 * q + 8, :].bitcast(I32),
+            nc.gpsimd.dma_start(out=tab2_s[32 * q + 8:32 * q + 16, :].bitcast(I32),
                                 in_=tab2_scales[:, 4 * q:4 * q + 4, :].bitcast(I32))
         load_w1(0, 1)
         load_w2(1)
@@ -339,7 +339,7 @@ def tile_list_joseki_lesson_gaps_kernel(tc, tab_words, tab_scales, tab2_words, t
                     words, word_cols = v2[h, n]
                     scales, scale_cols = v2["scales", n]
                     nc.tensor.matmul_mx(out=acc[:], lhsT=words[:, word_cols].bitcast(FP8X4),
-                                        lhsT_scale=scales[4 * h:P, scale_cols],
+                                        lhsT_scale=scales[8 + 4 * h:P, scale_cols],
                                         rhs=page_c[h][:, PASS * c:PASS * (c + 1)].bitcast(FP8X4),
                                         rhs_scale=page_s[h][:, PASS * c:PASS * (c + 1)],
                                         start=h == 0, stop=h == 1)
@@ -347,12 +347,13 @@ def tile_list_joseki_lesson_gaps_kernel(tc, tab_words, tab_scales, tab2_words, t
 
         second_stage(0)
         second_stage(1)
+        second_stage(2)
         for n in range(MOVE_TILES):
             if n == 1:
                 gather_v2(0, half + quarter, S2, cell([P, quarter], U32, "v2_03"))
                 gather_v2(1, half + quarter, S2, cell([P, quarter], U32, "v2_13"))
-            if n + 2 < MOVE_TILES:
-                second_stage(n + 2)
+            if n + 3 < MOVE_TILES:
+                second_stage(n + 3)
             for m0, m1 in ([(0, PICK)] if n < MOVE_TILES - 1 else [(0, PICK // 2), (PICK // 2, PICK)]):
                 gap = ring.tile([P, m1 - m0], F32, name="gap", bufs=MOVE_TILES + 1)
                 nc.vector.tensor_tensor(out=gap[:], in0=scores[n][:].indirect(open_lessons[:, m0 // 16:m1 // 16]),

@@ -22,18 +22,8 @@ P = 128
 PASS = 512
 ROW_TILES = H // P
 MOVE_TILES = S2 // P
-SQUARES_ON_VECTOR = 0
-PLACE = {
-    "raw01": 2, "wg2": 0.25, "reach1": 2.25, "reach2": 4.25, "reach3": 6.25, "wg3": 8.25,
-    "raw10": 11, "reach4": 11, "reach5": 13, "reach6": 15, "reach7": 17,
-    "raw11": 22, "pairs00": 19, "pairs01": 23, "shape3": 27, "shape6": 29,
-    "grouped012": 33, "lesson1": 32, "lesson0": 34.5, "lesson2": 35.5, "shape1": 37, "shape2": 30, "lesson3": 31,
-    "codes100": 34.5, "codes110": 36.5, "grouped110": 40, "weighted4": 40, "lesson4": 44, "shape5": 46, "lesson6": 45,
-    "lesson5": 32, "lesson7": 30.5,
-    "page_c0": 26.75, "v2_00": 30.75, "v2_10": 31.75,
-    "pairs11": 52, "v2_01": 52, "v2_11": 53, "v2_02": 54, "v2_12": 55, "v2_03": 52, "v2_13": 53,
-    "shape7": 48, "woven01": 47, "grouped010": 61, "w2_w1": 61,
-}
+AHEAD = 5
+SQUARES_ON_VECTOR = 2
 
 
 def tile_list_joseki_lesson_gaps_kernel(tc, tab_words, tab_scales, tab2_words, tab2_scales, w1, w2_words,
@@ -41,325 +31,362 @@ def tile_list_joseki_lesson_gaps_kernel(tc, tab_words, tab_scales, tab2_words, t
     nc = tc.nc
     with ExitStack() as ctx:
         lists = ctx.enter_context(tc.tile_pool(name="lists", bufs=1))
-        keep = ctx.enter_context(tc.tile_pool(name="keep", bufs=1))
-        ring = ctx.enter_context(tc.tile_pool(name="ring", bufs=1))
-        cells = ctx.enter_context(tc.tile_pool(name="cells", bufs=1))
+        sb = ctx.enter_context(tc.tile_pool(name="sb", bufs=1))
         psum = ctx.enter_context(tc.psum_pool(name="psum", bufs=1))
 
-        def cell(shape, dtype, name):
-            if name in PLACE:
-                return cells.tile(shape, dtype, name=name, tag=name, offset=int(1024 * PLACE[name]), align_bytes=64)
-            return ring.tile(shape, dtype, name=name, tag=name, align_bytes=64)
+        def tile(shape, dtype, name, tag=None, bufs=1):
+            return sb.tile(shape, dtype, name=name, tag=tag or name, bufs=bufs, align_bytes=64)
+
+        def bank(shape, name, b):
+            return psum.tile(shape, F32, name=name, tag="bank%d" % b)
 
         corners = lists.tile([P, S // 16], U16, name="corners")
         moves = lists.tile([P, S2 // 16], U16, name="moves")
         edited = lists.tile([P, S // 16], U16, name="edited")
         open_lessons = lists.tile([P, PICK // 16], U16, name="open_lessons")
 
-        tab_s = keep.tile([P, 2, T], U8, name="tab_s", align_bytes=64)
-        w2_s_raw = keep.tile([P, 2, H], U8, name="w2_s_raw", align_bytes=64)
-        tab2_s = keep.tile([P, T3], U8, name="tab2_s", align_bytes=64)
+        tab_s = tile([P, 2, T], U8, "tab_s")
+        w2_s_raw = tile([P, 2, H], U8, "w2_s_raw")
+        tab2_s = tile([P, T3], U8, "tab2_s")
         nc.vector.memset(tab_s[:].bitcast(I32), 0)
         nc.vector.memset(w2_s_raw[:].bitcast(I32), 0)
-        ident = keep.tile([P, P], F32, name="ident")
+        ident = tile([P, P], F32, "ident")
         make_identity(nc, ident[:])
         nc.gpsimd.memset(tab2_s[:].bitcast(I32), 0)
 
         def load_words(src, a, tag):
-            words = ring.tile([P, T], I32, name="words", tag=tag, align_bytes=64)
+            words = tile([P, T], I32, "words", tag)
             nc.sync.dma_start(out=words[:], in_=src[a].rearrange("p t i -> p (t i)").bitcast(I32))
             return words
 
-        def load_scales(queue, plane, src):
-            for r in range(4):
-                queue.dma_start(out=plane[r:P:32, :, :].bitcast(I32),
+        def load_scales(plane, src, rows):
+            for r in rows:
+                nc.sync.dma_start(out=plane[r:P:32, :, :].bitcast(I32),
                                   in_=src.rearrange("a (q r) t -> r q a t", r=4)[r].bitcast(I32))
 
         w1_raw = {}
 
-        def load_w1(h, a):
-            w1_raw[h, a] = cell([P, 4, PASS], F32, "raw%d%d" % (h, a))
-            nc.sync.dma_start(out=w1_raw[h, a][:], in_=w1[PASS * a:PASS * (a + 1), PASS * h:PASS * (h + 1)]
-                              .rearrange("(p j) c -> p j c", j=4))
+        def load_w1(a, c0, c1):
+            w1_raw[a, c0] = tile([P, 4, c1 - c0], F32, "w1_raw%d_%d" % (a, c0))
+            nc.sync.dma_start(out=w1_raw[a, c0][:],
+                              in_=w1[PASS * a:PASS * (a + 1), c0:c1].rearrange("(p j) c -> p j c", j=4))
 
         page = {}
 
         def load_page(x):
-            h, i = divmod(x, 4)
-            page[x] = ring.tile([P, T2], F32, name="page", tag="rows", bufs=ROW_TILES)
-            nc.sync.dma_start(out=page[x][:],
-                              in_=page0[PASS * h:PASS * (h + 1), :].rearrange("(p i) t -> p i t", i=4)[:, i, :])
+            page[x] = tile([P, T2], F32, "page", "rows", ROW_TILES)
+            if x < 4:
+                rows = page0[P * x:P * (x + 1), :]
+            else:
+                rows = page0[PASS:, :].rearrange("(p i) t -> p i t", i=4)[:, x - 4, :]
+            nc.sync.dma_start(out=page[x][:], in_=rows)
 
         def load_komi(g):
-            rows = ring.tile([P, 4, PICK], F32, name="komi_sb", tag="tab_w%d" % g, align_bytes=64)
+            rows = tile([P, 4, PICK], F32, "komi_sb", ("tab_w0", "wgs_t")[g])
             nc.sync.dma_start(out=rows[:], in_=komi[PASS * g:PASS * (g + 1), :].rearrange("(c p) m -> p c m", p=P))
             return rows
 
         w2_raw = {}
 
         def load_w2(h):
-            w2_raw[h] = keep.tile([P, 2, H], U8, name="w2_raw%d" % h, align_bytes=64)
+            w2_raw[h] = tile([P, 2, H], U8, "w2_raw%d" % h)
             nc.sync.dma_start(out=w2_raw[h][:].bitcast(I32),
                               in_=w2_words[:, :, H * h:H * (h + 1)].rearrange("a p c -> p a c").bitcast(I32))
 
-        tab_w = [load_words(tab_words, 0, "tab_w0")]
         nc.sync.dma_start(corners[:], offs)
-        wgs_sb = keep.tile([P, S], F32, name="wgs_sb")
+        wgs_sb = tile([P, S], F32, "wgs_sb")
         nc.sync.dma_start(out=wgs_sb[:], in_=wgs)
-        load_scales(nc.sync, tab_s, tab_scales)
-        tab_w.append(load_words(tab_words, 1, "tab_w1"))
         load_w2(0)
-        load_scales(nc.sync, w2_s_raw, w2_scales)
+        load_scales(tab_s, tab_scales, range(4))
+        tab_w = [load_words(tab_words, 0, "tab_w0")]
         nc.sync.dma_start(moves[:], offs2)
-        load_w1(0, 0)
         for q in range(4):
-            nc.gpsimd.dma_start(out=tab2_s[32 * q + 8:32 * q + 16, :].bitcast(I32),
-                                in_=tab2_scales[:, 4 * q:4 * q + 4, :].bitcast(I32))
-        load_w1(0, 1)
-        load_w2(1)
-        load_page(0)
+            nc.sync.dma_start(out=tab2_s[32 * q + 8:32 * q + 16, :].bitcast(I32),
+                              in_=tab2_scales[:, 4 * q:4 * q + 4, :].bitcast(I32))
+        load_w1(0, 0, 256)
+        tab_w.append(load_words(tab_words, 1, "tab_w1"))
+        load_scales(w2_s_raw, w2_scales, range(3))
+        load_w1(1, 0, 256)
+        load_scales(w2_s_raw, w2_scales, [3])
         nc.sync.dma_start(edited[:], offs3)
-        load_page(1)
-        load_w1(1, 0)
-        load_w1(1, 1)
+        load_page(0)
+        load_w1(0, 256, 512)
+        load_w1(1, 256, 512)
+        load_w2(1)
         nc.sync.dma_start(open_lessons[:], offs4)
+        load_page(1)
+        load_w1(0, 512, 1024)
         load_page(2)
-        load_page(3)
-        load_page(4)
-        load_page(5)
-        tab2_w = [load_words(tab2_words, a, "tab2_w%d" % a) for a in range(2)]
-        load_page(6)
-        load_page(7)
+        load_w1(1, 512, 1024)
+        for x in (4, 3, 5, 6, 7):
+            load_page(x)
 
         v_s, v_w = [], []
         for a in range(2):
-            picked_s = keep.tile([P, S], U8, name="v_s%d" % a, align_bytes=64)
+            picked_s = tile([P, S], U8, "v_s%d" % a)
             nc.vector.tensor_copy(out=picked_s[:], in_=tab_s[:, a, :].indirect(corners[:]))
             v_s.append(picked_s)
         for a in range(2):
-            picked_w = keep.tile([P, S], U32, name="v_w%d" % a, align_bytes=64)
+            picked_w = tile([P, S], U32, "v_w%d" % a)
             nc.vector.tensor_copy(out=picked_w[:], in_=tab_w[a][:].bitcast(U32).indirect(corners[:]))
             v_w.append(picked_w)
-        komi_sb = [load_komi(0), load_komi(1)]
 
-        w2_w, w2_s = {}, {}
+        w2_s_dealt = tile([P, 2, 4, P], U8, "w2_s_dealt")
+        nc.gpsimd.tensor_copy(out=w2_s_dealt[:], in_=w2_s_raw[:, :, PASS:].rearrange("p a (m i) -> p a i m", i=4))
 
-        def deal_w2_words(h):
-            w2_w[h] = cell([P, 2, 4, 2 * P], U8, "w2_w%d" % h)
-            nc.vector.tensor_copy(out=w2_w[h][:].bitcast(U16),
-                                  in_=w2_raw[h][:].bitcast(U16).rearrange("p a (m i) -> p a i m", i=4))
-
-        def deal_w2_scales(h):
-            w2_s[h] = cell([P, 2, 4, P], U8, "w2_s%d" % h)
-            nc.gpsimd.tensor_copy(out=w2_s[h][:],
-                                  in_=w2_s_raw[:, :, PASS * h:PASS * (h + 1)].rearrange("p a (m i) -> p a i m", i=4))
-
-        deal_w2_words(0)
-        deal_w2_scales(0)
-        deal_w2_scales(1)
-
-        wgs_t_ps = psum.tile([P, 4, P], F32, name="wgs_t_ps", tag="bank_s3")
+        wgs_t_ps = bank([P, 4, P], "wgs_t_ps", 7)
         for b in range(4):
             nc.tensor.transpose(wgs_t_ps[:, b, :], wgs_sb[:, P * b:P * (b + 1)], ident[:])
-        wgs_t = keep.tile([P, 4, 4, 4, 32], F32, name="wgs_t")
-        nc.scalar.copy(out=wgs_t[:],
-                       in_=wgs_t_ps[:].rearrange("j b (q i) -> j b i q", i=4).unsqueeze(3).to_broadcast([P, 4, 4, 4, 32]))
-        wg = {}
-
-        def deal_wgs(i):
-            bank = psum.tile([P, 4, P], F32, name="wg_bank", tag=("bank_b0", "bank_b1", "bank_s2", "bank_s3")[i])
+        wgs_t = tile([P, 2, 4, 2, 4, 32], F32, "wgs_t")
+        for g in range(2):
+            planes = wgs_t_ps[:].rearrange("j b (q i) -> j b i q", i=4)[:, :, 2 * g:2 * g + 2, :]
+            nc.scalar.copy(out=wgs_t[:, g], in_=planes.unsqueeze(3).to_broadcast([P, 4, 2, 4, 32]))
+        wg = {x: wgs_sb[:] for x in range(4)}
+        dealt_ps = {}
+        for i in range(4):
+            dealt_ps[i] = bank([P, 4, P], "wg_ps", 4 + i)
             for b in range(4):
-                nc.tensor.transpose(bank[:, b, :], wgs_t[:, b, i, :, :].rearrange("j g q -> j (g q)"), ident[:])
-            wg[i] = cell([P, S], F32, "wg%d" % i)
-            nc.scalar.copy(out=wg[i][:], in_=bank[:].rearrange("p b j -> p (b j)"))
+                nc.tensor.transpose(dealt_ps[i][:, b, :], wgs_t[:, i // 2, b, i % 2].rearrange("j g q -> j (g q)"), ident[:])
 
-        w1_grouped, w1_q = {}, {}
+        def deal_wgs(g):
+            two = tile([P, 2, S], F32, "wg", "w1_raw%d_0" % g)
+            for i in range(2):
+                wg[4 + 2 * g + i] = two[:, i, :]
+                nc.scalar.copy(out=two[:, i, :], in_=dealt_ps[2 * g + i][:].rearrange("p b j -> p (b j)"))
 
-        def cast_w1(h, a, i0, i1, copy):
-            w1_grouped[h, a, i0] = cell([P, i1 - i0, P, 4], BF16, "grouped%d%d%d" % (h, a, i0))
-            copy(out=w1_grouped[h, a, i0][:].rearrange("p i m j -> p m j i"),
-                 in_=w1_raw[h, a][:].rearrange("p j (m i) -> p m j i", i=4)[:, :, :, i0:i1])
+        tab2_w = [load_words(tab2_words, a, "tab2_w%d" % a) for a in range(2)]
+        komi_sb = [load_komi(0), load_komi(1)]
 
-        def quant_w1(h, a, i0, i1):
-            codes = cell([P, (i1 - i0) * P], U32, "codes%d%d%d" % (h, a, i0))
-            scales = keep.tile([P, (i1 - i0) * P], U8, name="w1_s%d%d%d" % (h, a, i0), align_bytes=64)
+        grouped, w1_q = {}, {}
+
+        def cast_natural(a, x0, x1):
+            c0 = 256 * (x0 // 2)
+            grouped[a, x0] = tile([P, (x1 - x0) * P, 4], BF16, "grouped%d_%d" % (a, x0))
+            nc.scalar.copy(out=grouped[a, x0][:].rearrange("p (c i) j -> p c j i", i=4),
+                           in_=w1_raw[a, c0][:, :, P * x0 - c0:P * x1 - c0].rearrange("p j (c i) -> p c j i", i=4))
+
+        def cast_dealt(a, x0, x1):
+            grouped[a, x0] = tile([P, (x1 - x0) * P, 4], BF16, "grouped%d_%d" % (a, x0))
+            nc.scalar.copy(out=grouped[a, x0][:].rearrange("p (i m) j -> p m j i", m=P),
+                           in_=w1_raw[a, PASS][:].rearrange("p j (m i) -> p m j i", i=4)[:, :, :, x0 - 4:x1 - 4])
+
+        def quant_w1(a, x0, x1):
+            codes = tile([P, (x1 - x0) * P], U32, "w1_codes%d_%d" % (a, x0))
+            scales = tile([P, (x1 - x0) * P], U8, "w1_scales%d_%d" % (a, x0))
             nc.vector.quantize_mx(out=codes[:].bitcast(FP8X4), scales=scales[:],
-                                  in_=w1_grouped[h, a, i0][:].rearrange("p i m j -> p (i m j)"))
-            for i in range(i0, i1):
-                cols = slice(P * (i - i0), P * (i - i0 + 1))
-                w1_q[4 * h + i, a] = (codes[:, cols], scales[:, cols])
+                                  in_=grouped[a, x0][:].rearrange("p c j -> p (c j)"))
+            for x in range(x0, x1):
+                cols = slice(P * (x - x0), P * (x - x0 + 1))
+                w1_q[x, a] = (codes[:, cols], scales[:, cols])
 
         v2 = {}
 
-        def gather_v2(part, n0, n1, picked):
+        def gather_v2(part, n0, n1, tag=None):
+            picked = tile([P, n1 - n0], U8 if part == "scales" else U32, "v2_%s_%d" % (part, n0), tag)
             window = tab2_s[:] if part == "scales" else tab2_w[part][:].bitcast(U32)
             nc.vector.tensor_copy(out=picked[:], in_=window.indirect(moves[:, n0 // 16:n1 // 16]))
             for n in range(n0 // P, n1 // P):
                 v2[part, n] = (picked, slice(P * n - n0, P * (n + 1) - n0))
 
-        reach_sb, shape_ps, weighted, lesson = {}, {}, {}, {}
+        w2_dealt, behind_cast = {}, {}
+        reach_ps, reach_sb, shape_ps, shape_sb, weighted, lesson = {}, {}, {}, {}, {}, {}
+        on_vector = (0, 2, 4)
+        shape_bank = (4, 5, 0, 2, 3, 0, 2, 1)
+        reach_bank = (0, 2, 4, 5, 1) + shape_bank[5:]
+        lesson_slot = "ABBAABAB"
 
         def reach_stage(x):
-            reach = psum.tile([P, S], F32, name="reach", tag="bank_r%d" % (x > 0 and x % 2 == 0))
+            reach_ps[x] = bank([P, S], "reach", reach_bank[x])
             for a in range(2):
-                nc.tensor.matmul_mx(out=reach[:], lhsT=w2_w[x // 4][:, a, x % 4, :].bitcast(FP4X4),
-                                    lhsT_scale=w2_s[x // 4][:, a, x % 4, :],
+                if x < 4:
+                    words, scales = w2_raw[0][:, a, 2 * P * x:2 * P * (x + 1)], w2_s_raw[:, a, P * x:P * (x + 1)]
+                else:
+                    words, scales = w2_dealt[0][:, a, x - 4, :], w2_s_dealt[:, a, x - 4, :]
+                nc.tensor.matmul_mx(out=reach_ps[x][:], lhsT=words.bitcast(FP4X4), lhsT_scale=scales,
                                     rhs=v_w[a][:].bitcast(FP8X4), rhs_scale=v_s[a][:], start=a == 0, stop=a == 1)
-            if x == 0:
-                weighted[x] = cell([P, S], F32, "weighted0")
-                nc.vector.tensor_tensor(out=weighted[x][:], in0=reach[:], in1=wg[x % 4][:], op=MULT)
-            else:
-                reach_sb[x] = cell([P, S], F32, "reach%d" % x)
-                nc.scalar.copy(out=reach_sb[x][:], in_=reach[:])
+            if x == 2:
+                both = tile([P, 2, S], F32, "reach23", "w1_raw1_256")
+                reach_sb[2], reach_sb[3] = both[:, 0, :], both[:, 1, :]
+            elif x == 4:
+                reach_sb[x] = behind_cast[0][:, 1, :]
+            elif x not in (0, 3):
+                reach_sb[x] = tile([P, S], F32, "reach_sb", bufs=3)[:]
+            if x > 0:
+                nc.scalar.copy(out=reach_sb[x], in_=reach_ps[x][:])
 
         def shape_stage(x):
-            shape_ps[x] = psum.tile([P, S], F32, name="shape", tag="bank_s%d" % (x % 4))
+            shape_ps[x] = bank([P, S], "shape", shape_bank[x])
             for a in range(2):
                 nc.tensor.matmul_mx(out=shape_ps[x][:], lhsT=w1_q[x, a][0].bitcast(FP8X4), lhsT_scale=w1_q[x, a][1],
                                     rhs=v_w[a][:].bitcast(FP8X4), rhs_scale=v_s[a][:], start=a == 0, stop=a == 1)
+            if x not in on_vector:
+                if x == 3:
+                    shape_sb[x] = behind_cast[0][:, 0, :]
+                elif x == ROW_TILES - 1:
+                    shape_sb[x] = tile([P, S], F32, "shape_last")[:]
+                else:
+                    shape_sb[x] = tile([P, S], F32, "shape_sb", bufs=3)[:]
+                nc.scalar.copy(out=shape_sb[x], in_=shape_ps[x][:])
 
         def weigh(x):
-            weighted[x] = cell([P, S], F32, "weighted%d" % x)
-            nc.gpsimd.tensor_tensor(out=weighted[x][:], in0=reach_sb[x][:], in1=wg[x % 4][:], op=MULT)
+            if x == 0:
+                weighted[x] = tile([P, S], F32, "weighted0")
+                nc.vector.tensor_tensor(out=weighted[x][:], in0=reach_ps[x][:], in1=wg[x], op=MULT)
+            else:
+                weighted[x] = tile([P, S], F32, "weighted")
+                nc.gpsimd.tensor_tensor(out=weighted[x][:], in0=reach_sb[x], in1=wg[x], op=MULT)
 
-        def product_on_vector(x):
-            lesson[x] = cell([P, S], F32, "lesson%d" % x)
-            nc.vector.tensor_tensor(out=lesson[x][:], in0=shape_ps[x][:], in1=weighted[x][:], op=MULT)
-
-        def products(x):
-            shape_sb = cell([P, S], F32, "shape%d" % x)
-            nc.scalar.copy(out=shape_sb[:], in_=shape_ps[x][:])
-            lesson[x] = cell([P, S], F32, "lesson%d" % x)
-            nc.gpsimd.tensor_tensor(out=lesson[x][:], in0=reach_sb[x][:], in1=wg[x % 4][:], op=MULT)
-            nc.gpsimd.tensor_tensor(out=lesson[x][:], in0=lesson[x][:], in1=shape_sb[:], op=MULT)
+        def multiply(x):
+            lesson[x] = tile([P, S], F32, "lesson" + lesson_slot[x])
+            if x in on_vector:
+                nc.vector.tensor_tensor(out=lesson[x][:], in0=shape_ps[x][:], in1=weighted[x][:], op=MULT)
+            else:
+                nc.gpsimd.tensor_tensor(out=lesson[x][:], in0=shape_sb[x], in1=weighted[x][:], op=MULT)
 
         def scatter(x):
             nc.vector.tensor_copy(out=page[x][:].indirect(edited[:]), in_=lesson[x][:])
 
-        pairs, page_c, page_s, grouped_page = {}, {}, {}, {}
-
-        def cast_page(x):
-            h, i = divmod(x, 4)
-            for c in range(2):
-                if i == 0:
-                    pairs[h, c] = cell([P, 2, PASS, 2], BF16, "pairs%d%d" % (h, c))
-                nc.scalar.copy(out=pairs[h, c][:, i // 2, :, i % 2], in_=page[x][:, PASS * c:PASS * (c + 1)])
-
-        def weave_page(h, c, copy):
-            grouped_page[h, c] = cell([P, PASS, 4], BF16, "woven%d%d" % (h, c))
-            copy(out=grouped_page[h, c][:].bitcast(U32),
-                 in_=pairs[h, c][:].rearrange("p u t e -> p (u t e)").bitcast(U32).rearrange("p (u t) -> p t u", u=2))
-
-        def quant_page(h, g):
-            width = PASS
-            if g == 0:
-                page_c[h] = cell([P, T2], U32, "page_c%d" % h)
-                page_s[h] = keep.tile([P, T2], U8, name="page_s%d" % h, align_bytes=64)
-            cols = slice(width * g, width * (g + 1))
-            nc.vector.quantize_mx(out=page_c[h][:, cols].bitcast(FP8X4), scales=page_s[h][:, cols],
-                                  in_=grouped_page[h, g][:].rearrange("p t i -> p (t i)"))
-
-        half, quarter = S2 // 2, S2 // 4
+        quarter = S2 // 4
+        gather_v2("scales", 0, S2)
+        cast_natural(0, 0, 2)
         deal_wgs(0)
-        deal_wgs(1)
-        cast_w1(0, 0, 0, 2, nc.scalar.copy)
-        cast_w1(0, 0, 2, 4, nc.scalar.copy)
-        gather_v2("scales", 0, half, cell([P, half], U8, "v2_s_first"))
-        gather_v2("scales", half, S2, cell([P, half], U8, "v2_s_late"))
-        quant_w1(0, 0, 0, 2)
+        quant_w1(0, 0, 2)
         reach_stage(0)
-        cast_w1(0, 1, 0, 2, nc.vector.tensor_copy)
-        cast_w1(0, 1, 2, 4, nc.scalar.copy)
-        quant_w1(0, 0, 2, 4)
-        quant_w1(0, 1, 0, 2)
-        shape_stage(0)
-        quant_w1(0, 1, 2, 4)
-        deal_w2_words(1)
-        product_on_vector(0)
+        weigh(0)
+        cast_natural(1, 0, 1)
+        cast_natural(1, 1, 2)
+        deal_wgs(1)
         reach_stage(1)
+        quant_w1(1, 0, 1)
+        shape_stage(0)
+        quant_w1(1, 1, 2)
         shape_stage(1)
-        products(1)
+        multiply(0)
+        weigh(1)
+        multiply(1)
         scatter(0)
-        deal_wgs(2)
-        deal_wgs(3)
+        cast_natural(0, 2, 4)
+        cast_natural(1, 2, 4)
+        quant_w1(0, 2, 4)
+        quant_w1(1, 2, 4)
         reach_stage(2)
-        shape_stage(2)
-        products(2)
         reach_stage(3)
-        shape_stage(3)
+        weigh(2)
+        shape_stage(2)
         scatter(1)
-        cast_w1(1, 0, 0, 4, nc.scalar.copy)
-        cast_w1(1, 1, 0, 4, nc.scalar.copy)
-        products(3)
+        w2_dealt[0] = tile([P, 2, 4, 2 * P], U8, "w2_dealt")
+        nc.scalar.copy(out=w2_dealt[0][:].bitcast(U16),
+                       in_=w2_raw[1][:].bitcast(U16).rearrange("p a (m i) -> p a i m", i=4))
+        cast_dealt(0, 4, 8)
+        behind_cast[0] = tile([P, 2, S], F32, "behind_cast", "w1_raw0_512")
+        shape_stage(3)
+        reach_stage(4)
+        multiply(2)
         scatter(2)
-        quant_w1(1, 0, 0, 4)
-        quant_w1(1, 1, 0, 4)
-        for x in range(4, ROW_TILES):
-            reach_stage(x)
-        for x in range(4, ROW_TILES):
-            shape_stage(x)
+        weigh(3)
+        multiply(3)
         weigh(4)
+        cast_dealt(1, 4, 6)
+        quant_w1(0, 4, 8)
+        quant_w1(1, 4, 6)
+        shape_stage(4)
+        shape_stage(5)
         scatter(3)
-        product_on_vector(4)
-        products(5)
+        cast_dealt(1, 6, 8)
+        reach_stage(5)
+        quant_w1(1, 6, 8)
+        multiply(4)
         scatter(4)
-        products(6)
-        scatter(5)
-        products(7)
+        for x in (6, 7):
+            shape_stage(x)
+            reach_stage(x)
+        for x in range(5, ROW_TILES):
+            weigh(x)
+            multiply(x)
+            if x + 1 < ROW_TILES:
+                scatter(x)
+
+        woven, page_c, page_s = {}, {}, {}
+        turned = tile([P, 2, 8, P, 2], BF16, "turned", "w1_raw1_512")
         for x in range(4):
-            cast_page(x)
-        weave_page(0, 0, nc.scalar.copy)
-        weave_page(0, 1, nc.gpsimd.tensor_copy)
-        cast_page(4)
-        cast_page(5)
-        scatter(6)
-        cast_page(6)
-        scatter(7)
-        cast_page(7)
-        quant_page(0, 0)
-        gather_v2(0, 0, quarter, cell([P, quarter], U32, "v2_00"))
-        weave_page(1, 0, nc.vector.tensor_copy)
-        gather_v2(1, 0, quarter, cell([P, quarter], U32, "v2_10"))
-        quant_page(1, 0)
+            for c in range(2):
+                turn_ps = bank([P, 4, P], "turn_ps", 4 + 2 * (x % 2) + c)
+                for b in range(4):
+                    t0 = PASS * c + P * b
+                    nc.tensor.transpose(turn_ps[:, b, :], page[x][:, t0:t0 + P], ident[:])
+                nc.scalar.copy(out=turned[:, :, 4 * c:4 * (c + 1), 32 * x:32 * (x + 1), :],
+                               in_=turn_ps[:].rearrange("t b (q u e) -> t u b q e", u=2, e=2))
+        for c in (1, 0):
+            woven[0, c] = tile([P, PASS, 4], BF16, "woven0_%d" % c)
+            for g in range(2):
+                back_ps = bank([P, 2, 2, P], "back_ps", (3, 0, 4, 5)[2 * c + g])
+                for b in range(2):
+                    for u in range(2):
+                        words = turned[:, u, 4 * c + 2 * g + b, :, :].rearrange("t p e -> t (p e)").bitcast(F32)
+                        nc.tensor.transpose(back_ps[:, b, u, :], words, ident[:])
+                nc.scalar.copy(out=woven[0, c][:, 256 * g:256 * (g + 1), :].bitcast(F32).rearrange("p (b t) u -> p b t u", b=2),
+                               in_=back_ps[:].rearrange("p b u t -> p b t u"))
+
+        page_codes = [tile([P, 2, PASS], U32, "page_c0", "shape_last"), tile([P, 2, PASS], U32, "page_c1")]
+
+        def quant_page(h, c):
+            page_c[h, c] = page_codes[h][:, c, :]
+            page_s[h, c] = tile([P, PASS], U8, "page_s%d_%d" % (h, c))
+            nc.vector.quantize_mx(out=page_c[h, c].bitcast(FP8X4), scales=page_s[h, c][:],
+                                  in_=woven[h, c][:].rearrange("p t i -> p (t i)"))
+
+        scatter(ROW_TILES - 1)
         quant_page(0, 1)
-        weave_page(1, 1, nc.scalar.copy)
+        for c, tag, copy in ((0, "w1_raw1_512", nc.scalar.copy), (1, "weighted", nc.gpsimd.tensor_copy)):
+            pairs = tile([P, 2, PASS, 2], BF16, "pairs", tag)
+            for i in range(4):
+                copy(out=pairs[:, i // 2, :, i % 2], in_=page[4 + i][:, PASS * c:PASS * (c + 1)])
+            woven[1, c] = tile([P, PASS, 4], BF16, "woven1_%d" % c)
+            copy(out=woven[1, c][:].bitcast(U32),
+                 in_=pairs[:].rearrange("p u t e -> p (u t e)").bitcast(U32).rearrange("p (u t) -> p t u", u=2))
+        def gather_words(picked, g, a):
+            nc.vector.tensor_copy(out=picked, in_=tab2_w[a][:].bitcast(U32).indirect(moves[:, 16 * g:16 * (g + 1)]))
+            for n in (2 * g, 2 * g + 1):
+                v2[a, n] = (picked, slice(P * (n % 2), P * (n % 2 + 1)))
+
+        v2_first = tile([P, 2, quarter], U32, "v2_first", "woven0_1")
+        for a in range(2):
+            gather_words(v2_first[:, a, :], 0, a)
+        quant_page(0, 0)
         quant_page(1, 1)
-        gather_v2(0, quarter, half, cell([P, quarter], U32, "v2_01"))
-        gather_v2(1, quarter, half, cell([P, quarter], U32, "v2_11"))
-        gather_v2(0, half, half + quarter, cell([P, quarter], U32, "v2_02"))
-        gather_v2(1, half, half + quarter, cell([P, quarter], U32, "v2_12"))
+        quant_page(1, 0)
+        v2_rest = tile([P, 3, 2, quarter], U32, "v2_rest", "woven1_0")
+        for g in range(1, 4):
+            for a in range(2):
+                gather_words(v2_rest[:, g - 1, a, :], g, a)
 
         scores = {}
 
         def second_stage(n):
-            scores[n] = ring.tile([P, T2], F32, name="scores", tag="rows", bufs=ROW_TILES)
-            for c in range(2):
-                acc = psum.tile([P, PASS], F32, name="acc", tag=(("bank_r0", "bank_b0"), ("bank_r1", "bank_b1"), ("bank_s2", "bank_s0"), ("bank_s3", "bank_s1"))[n % 4][c])
+            scores[n] = tile([P, T2], F32, "scores", "rows", ROW_TILES)
+            for c in (1, 0):
+                acc = bank([P, PASS], "acc", ((2, 1), (6, 7), (4, 5), (3, 0))[n % 4][c])
                 for h in range(2):
                     words, word_cols = v2[h, n]
                     scales, scale_cols = v2["scales", n]
                     nc.tensor.matmul_mx(out=acc[:], lhsT=words[:, word_cols].bitcast(FP8X4),
                                         lhsT_scale=scales[8 + 4 * h:P, scale_cols],
-                                        rhs=page_c[h][:, PASS * c:PASS * (c + 1)].bitcast(FP8X4),
-                                        rhs_scale=page_s[h][:, PASS * c:PASS * (c + 1)],
+                                        rhs=page_c[h, c].bitcast(FP8X4),
+                                        rhs_scale=page_s[h, c][:],
                                         start=h == 0, stop=h == 1)
                 nc.scalar.copy(out=scores[n][:, PASS * c:PASS * (c + 1)], in_=acc[:])
 
-        second_stage(0)
-        second_stage(1)
-        second_stage(2)
+        for n in range(AHEAD):
+            second_stage(n)
         for n in range(MOVE_TILES):
-            if n == 1:
-                gather_v2(0, half + quarter, S2, cell([P, quarter], U32, "v2_03"))
-                gather_v2(1, half + quarter, S2, cell([P, quarter], U32, "v2_13"))
-            if n + 3 < MOVE_TILES:
-                second_stage(n + 3)
+            if n + AHEAD < MOVE_TILES:
+                second_stage(n + AHEAD)
             for m0, m1 in ([(0, PICK)] if n < MOVE_TILES - 1 else [(0, PICK // 2), (PICK // 2, PICK)]):
-                gap = ring.tile([P, m1 - m0], F32, name="gap", bufs=MOVE_TILES + 1)
-                nc.vector.tensor_tensor(out=gap[:], in0=scores[n][:].indirect(open_lessons[:, m0 // 16:m1 // 16]),
+                gap = tile([P, m1 - m0], F32, "gap", bufs=MOVE_TILES + 1)[:]
+                nc.vector.tensor_tensor(out=gap, in0=scores[n][:].indirect(open_lessons[:, m0 // 16:m1 // 16]),
                                         in1=komi_sb[n // 4][:, n % 4, m0:m1], op=SUB)
                 if n < SQUARES_ON_VECTOR:
-                    nc.vector.tensor_tensor(out=gap[:], in0=gap[:], in1=gap[:], op=MULT)
+                    nc.vector.tensor_tensor(out=gap, in0=gap, in1=gap, op=MULT)
                 else:
-                    nc.scalar.activation(out=gap[:], in_=gap[:], func=ACT.Square)
-                nc.sync.dma_start(out=out[P * n:P * (n + 1), m0:m1], in_=gap[:])
+                    nc.scalar.activation(out=gap, in_=gap, func=ACT.Square)
+                nc.sync.dma_start(out=out[P * n:P * (n + 1), m0:m1], in_=gap)

@@ -337,28 +337,31 @@ def tile_list_joseki_lesson_gaps_kernel(tc, tab_words, tab_scales, tab2_words, t
 
         scatter(ROW_TILES - 1)
         quant_page(0, 1)
-        for c, tag, copy in ((0, "w1_raw1_512", nc.scalar.copy), (1, "weighted", nc.gpsimd.tensor_copy)):
-            pairs = tile([P, 2, PASS, 2], BF16, "pairs", tag)
-            for i in range(4):
-                copy(out=pairs[:, i // 2, :, i % 2], in_=page[4 + i][:, PASS * c:PASS * (c + 1)])
+        pairs = tile([P, 2, 2, PASS, 2], BF16, "pairs", "w1_raw1_512")
+        for i in range(4):
+            for c in (1, 0):
+                nc.scalar.copy(out=pairs[:, c, i // 2, :, i % 2], in_=page[4 + i][:, PASS * c:PASS * (c + 1)])
+        for c in (1, 0):
             woven[1, c] = tile([P, PASS, 4], BF16, "woven1_%d" % c)
-            copy(out=woven[1, c][:].bitcast(U32),
-                 in_=pairs[:].rearrange("p u t e -> p (u t e)").bitcast(U32).rearrange("p (u t) -> p t u", u=2))
+            nc.scalar.copy(out=woven[1, c][:].bitcast(U32),
+                           in_=pairs[:, c].rearrange("p u t e -> p (u t e)").bitcast(U32).rearrange("p (u t) -> p t u", u=2))
+
         def gather_words(picked, g, a):
             nc.vector.tensor_copy(out=picked, in_=tab2_w[a][:].bitcast(U32).indirect(moves[:, 16 * g:16 * (g + 1)]))
             for n in (2 * g, 2 * g + 1):
                 v2[a, n] = (picked, slice(P * (n % 2), P * (n % 2 + 1)))
 
-        v2_first = tile([P, 2, quarter], U32, "v2_first", "woven0_1")
-        for a in range(2):
-            gather_words(v2_first[:, a, :], 0, a)
+        v2_first = tile([P, 2, 2, quarter], U32, "v2_first", "woven0_1")
+        for g in range(2):
+            for a in range(2):
+                gather_words(v2_first[:, g, a, :], g, a)
         quant_page(0, 0)
         quant_page(1, 1)
         quant_page(1, 0)
-        v2_rest = tile([P, 3, 2, quarter], U32, "v2_rest", "woven1_0")
-        for g in range(1, 4):
+        v2_rest = tile([P, 2, 2, quarter], U32, "v2_rest", "woven1_0")
+        for g in range(2):
             for a in range(2):
-                gather_words(v2_rest[:, g - 1, a, :], g, a)
+                gather_words(v2_rest[:, g, a, :], 2 + g, a)
 
         scores = {}
 

@@ -103,11 +103,10 @@ def tile_list_joseki_lesson_gaps_kernel(tc, tab_words, tab_scales, tab2_words, t
         for q in range(4):
             nc.sync.dma_start(out=tab2_s[32 * q + 8:32 * q + 16, :].bitcast(I32),
                               in_=tab2_scales[:, 4 * q:4 * q + 4, :].bitcast(I32))
-        load_w1(0, 0, 256)
         tab_w.append(load_words(tab_words, 1, "tab_w1"))
-        load_scales(w2_s_raw, w2_scales, range(3))
+        load_scales(w2_s_raw, w2_scales, range(4))
+        load_w1(0, 0, 256)
         load_w1(1, 0, 256)
-        load_scales(w2_s_raw, w2_scales, [3])
         nc.sync.dma_start(edited[:], offs3)
         load_page(0)
         load_w1(0, 256, 512)
@@ -132,7 +131,7 @@ def tile_list_joseki_lesson_gaps_kernel(tc, tab_words, tab_scales, tab2_words, t
             v_w.append(picked_w)
 
         w2_s_dealt = tile([P, 2, 4, P], U8, "w2_s_dealt")
-        nc.gpsimd.tensor_copy(out=w2_s_dealt[:], in_=w2_s_raw[:, :, PASS:].rearrange("p a (m i) -> p a i m", i=4))
+        nc.vector.tensor_copy(out=w2_s_dealt[:], in_=w2_s_raw[:, :, PASS:].rearrange("p a (m i) -> p a i m", i=4))
 
         wgs_t_ps = bank([P, 4, P], "wgs_t_ps", 7)
         for b in range(4):
@@ -149,7 +148,7 @@ def tile_list_joseki_lesson_gaps_kernel(tc, tab_words, tab_scales, tab2_words, t
                 nc.tensor.transpose(dealt_ps[i][:, b, :], wgs_t[:, i // 2, b, i % 2].rearrange("j g q -> j (g q)"), ident[:])
 
         def deal_wgs(g):
-            two = tile([P, 2, S], F32, "wg", "w1_raw%d_0" % g)
+            two = tile([P, 2, S], F32, "wg%d" % g)
             for i in range(2):
                 wg[4 + 2 * g + i] = two[:, i, :]
                 nc.scalar.copy(out=two[:, i, :], in_=dealt_ps[2 * g + i][:].rearrange("p b j -> p (b j)"))
@@ -192,7 +191,7 @@ def tile_list_joseki_lesson_gaps_kernel(tc, tab_words, tab_scales, tab2_words, t
         reach_ps, reach_sb, shape_ps, shape_sb, weighted, lesson = {}, {}, {}, {}, {}, {}
         on_vector = (0, 2, 4)
         shape_bank = (4, 5, 0, 2, 3, 0, 2, 1)
-        reach_bank = (0, 2, 4, 5, 1) + shape_bank[5:]
+        reach_bank = (0, 2, 4, 5, 1, 3) + shape_bank[6:]
         lesson_slot = "ABBAABAB"
 
         def reach_stage(x):
@@ -207,8 +206,10 @@ def tile_list_joseki_lesson_gaps_kernel(tc, tab_words, tab_scales, tab2_words, t
             if x == 2:
                 both = tile([P, 2, S], F32, "reach23", "w1_raw1_256")
                 reach_sb[2], reach_sb[3] = both[:, 0, :], both[:, 1, :]
-            elif x == 4:
-                reach_sb[x] = behind_cast[0][:, 1, :]
+            elif x == 1:
+                reach_sb[x] = tile([P, S], F32, "reach1", "w1_raw1_0")[:]
+            elif x in (4, 5):
+                reach_sb[x] = behind_cast[0][:, x - 3, :]
             elif x not in (0, 3):
                 reach_sb[x] = tile([P, S], F32, "reach_sb", bufs=3)[:]
             if x > 0:
@@ -230,7 +231,7 @@ def tile_list_joseki_lesson_gaps_kernel(tc, tab_words, tab_scales, tab2_words, t
 
         def weigh(x):
             if x == 0:
-                weighted[x] = tile([P, S], F32, "weighted0")
+                weighted[x] = tile([P, S], F32, "weighted0", "grouped1_0")
                 nc.vector.tensor_tensor(out=weighted[x][:], in0=reach_ps[x][:], in1=wg[x], op=MULT)
             else:
                 weighted[x] = tile([P, S], F32, "weighted")
@@ -246,19 +247,20 @@ def tile_list_joseki_lesson_gaps_kernel(tc, tab_words, tab_scales, tab2_words, t
         def scatter(x):
             nc.vector.tensor_copy(out=page[x][:].indirect(edited[:]), in_=lesson[x][:])
 
-        quarter = S2 // 4
-        gather_v2("scales", 0, S2)
-        cast_natural(0, 0, 2)
+        half, quarter = S2 // 2, S2 // 4
+        gather_v2("scales", 0, half)
+        gather_v2("scales", half, S2, "tab_w1")
         deal_wgs(0)
+        deal_wgs(1)
+        cast_natural(0, 0, 2)
         quant_w1(0, 0, 2)
         reach_stage(0)
-        weigh(0)
         cast_natural(1, 0, 1)
         cast_natural(1, 1, 2)
-        deal_wgs(1)
         reach_stage(1)
         quant_w1(1, 0, 1)
         shape_stage(0)
+        weigh(0)
         quant_w1(1, 1, 2)
         shape_stage(1)
         multiply(0)
@@ -278,9 +280,10 @@ def tile_list_joseki_lesson_gaps_kernel(tc, tab_words, tab_scales, tab2_words, t
         nc.scalar.copy(out=w2_dealt[0][:].bitcast(U16),
                        in_=w2_raw[1][:].bitcast(U16).rearrange("p a (m i) -> p a i m", i=4))
         cast_dealt(0, 4, 8)
-        behind_cast[0] = tile([P, 2, S], F32, "behind_cast", "w1_raw0_512")
+        behind_cast[0] = tile([P, 3, S], F32, "behind_cast", "w1_raw0_512")
         shape_stage(3)
         reach_stage(4)
+        reach_stage(5)
         multiply(2)
         scatter(2)
         weigh(3)
@@ -293,7 +296,6 @@ def tile_list_joseki_lesson_gaps_kernel(tc, tab_words, tab_scales, tab2_words, t
         shape_stage(5)
         scatter(3)
         cast_dealt(1, 6, 8)
-        reach_stage(5)
         quant_w1(1, 6, 8)
         multiply(4)
         scatter(4)

@@ -15,6 +15,7 @@ U8 = mybir.dt.uint8
 FP8X4 = mybir.dt.float8_e4m3fn_x4
 FP4X4 = mybir.dt.float4_e2m1fn_x4
 MULT = mybir.AluOpType.mult
+ADD = mybir.AluOpType.add
 SUB = mybir.AluOpType.subtract
 ACT = mybir.ActivationFunctionType
 
@@ -115,9 +116,8 @@ def tile_list_joseki_lesson_gaps_kernel(tc, tab_words, tab_scales, tab2_words, t
         nc.sync.dma_start(open_lessons[:], offs4)
         load_page(1)
         load_w1(0, 512, 1024)
-        load_page(2)
         load_w1(1, 512, 1024)
-        for x in (4, 3, 5, 6, 7):
+        for x in (2, 4, 3, 5, 6, 7):
             load_page(x)
 
         v_s, v_w = [], []
@@ -342,7 +342,11 @@ def tile_list_joseki_lesson_gaps_kernel(tc, tab_words, tab_scales, tab2_words, t
         pairs = tile([P, 2, 2, PASS, 2], BF16, "pairs", "w1_raw1_512")
         for i in range(4):
             for c in (1, 0):
-                nc.scalar.copy(out=pairs[:, c, i // 2, :, i % 2], in_=page[4 + i][:, PASS * c:PASS * (c + 1)])
+                rows = page[4 + i][:, PASS * c:PASS * (c + 1)]
+                if i < 2:
+                    nc.gpsimd.tensor_scalar(out=pairs[:, c, 0, :, i], in0=rows, scalar1=1.0, scalar2=0.0, op0=MULT, op1=ADD)
+                else:
+                    nc.scalar.copy(out=pairs[:, c, 1, :, i - 2], in_=rows)
         for c in (1, 0):
             woven[1, c] = tile([P, PASS, 4], BF16, "woven1_%d" % c)
             nc.scalar.copy(out=woven[1, c][:].bitcast(U32),

@@ -189,10 +189,10 @@ def tile_list_joseki_lesson_gaps_kernel(tc, tab_words, tab_scales, tab2_words, t
 
         w2_dealt, behind_cast = {}, {}
         reach_ps, reach_sb, shape_ps, shape_sb, weighted, lesson = {}, {}, {}, {}, {}, {}
-        on_vector = (0, 2, 4)
+        on_vector = (0, 2)
         shape_bank = (4, 5, 0, 2, 3, 0, 2, 1)
         reach_bank = (0, 2, 4, 5, 1, 3) + shape_bank[6:]
-        lesson_slot = "ABBAABAB"
+        lesson_slot = "ABBABABA"
 
         def reach_stage(x):
             reach_ps[x] = bank([P, S], "reach", reach_bank[x])
@@ -294,9 +294,9 @@ def tile_list_joseki_lesson_gaps_kernel(tc, tab_words, tab_scales, tab2_words, t
         quant_w1(1, 4, 6)
         shape_stage(4)
         shape_stage(5)
-        scatter(3)
         cast_dealt(1, 6, 8)
         quant_w1(1, 6, 8)
+        scatter(3)
         multiply(4)
         scatter(4)
         for x in (6, 7):

@@ -311,7 +311,7 @@ def tile_list_joseki_lesson_gaps_kernel(tc, tab_words, tab_scales, tab2_words, t
         woven, page_c, page_s = {}, {}, {}
         turned = tile([P, 2, 8, P, 2], BF16, "turned", "w1_raw1_512")
         for x in range(4):
-            for c in range(2):
+            for c in (1, 0):
                 turn_ps = bank([P, 4, P], "turn_ps", 4 + 2 * (x % 2) + c)
                 for b in range(4):
                     t0 = PASS * c + P * b
@@ -339,7 +339,7 @@ def tile_list_joseki_lesson_gaps_kernel(tc, tab_words, tab_scales, tab2_words, t
 
         scatter(ROW_TILES - 1)
         quant_page(0, 1)
-        pairs = tile([P, 2, 2, PASS, 2], BF16, "pairs", "w1_raw1_512")
+        pairs = tile([P, 2, 2, PASS, 2], BF16, "pairs", "weighted")
         for i in range(4):
             for c in (1, 0):
                 rows = page[4 + i][:, PASS * c:PASS * (c + 1)]

@@ -164,8 +164,8 @@ def tile_list_joseki_lesson_gaps_kernel(tc, tab_words, tab_scales, tab2_words, t
             nc.scalar.copy(out=grouped[a, x0][:].rearrange("p (c i) j -> p c j i", i=4),
                            in_=w1_raw[a, c0][:, :, P * x0 - c0:P * x1 - c0].rearrange("p j (c i) -> p c j i", i=4))
 
-        def cast_dealt(a, x0, x1):
-            grouped[a, x0] = tile([P, (x1 - x0) * P, 4], BF16, "grouped%d_%d" % (a, x0))
+        def cast_dealt(a, x0, x1, into=None):
+            grouped[a, x0] = into if into is not None else tile([P, (x1 - x0) * P, 4], BF16, "grouped%d_%d" % (a, x0))
             nc.scalar.copy(out=grouped[a, x0][:].rearrange("p (i m) j -> p m j i", m=P),
                            in_=w1_raw[a, PASS][:].rearrange("p j (m i) -> p m j i", i=4)[:, :, :, x0 - 4:x1 - 4])
 
@@ -247,6 +247,15 @@ def tile_list_joseki_lesson_gaps_kernel(tc, tab_words, tab_scales, tab2_words, t
         def scatter(x):
             nc.vector.tensor_copy(out=page[x][:].indirect(edited[:]), in_=lesson[x][:])
 
+        def turn(x):
+            for c in (1, 0):
+                turn_ps = bank([P, 4, P], "turn_ps", 4 + 2 * (x % 2) + c)
+                for b in range(4):
+                    t0 = PASS * c + P * b
+                    nc.tensor.transpose(turn_ps[:, b, :], page[x][:, t0:t0 + P], ident[:])
+                nc.scalar.copy(out=turned[:, :, 4 * c:4 * (c + 1), 32 * x:32 * (x + 1), :],
+                               in_=turn_ps[:].rearrange("t b (q u e) -> t u b q e", u=2, e=2))
+
         half, quarter = S2 // 2, S2 // 4
         gather_v2("scales", 0, half)
         gather_v2("scales", half, S2, "tab_w1")
@@ -279,7 +288,9 @@ def tile_list_joseki_lesson_gaps_kernel(tc, tab_words, tab_scales, tab2_words, t
         w2_dealt[0] = tile([P, 2, 4, 2 * P], U8, "w2_dealt")
         nc.scalar.copy(out=w2_dealt[0][:].bitcast(U16),
                        in_=w2_raw[1][:].bitcast(U16).rearrange("p a (m i) -> p a i m", i=4))
-        cast_dealt(0, 4, 8)
+        cast_dealt(0, 4, 6)
+        last_two = tile([P, 2, 2 * P, 4], BF16, "last_two")
+        cast_dealt(0, 6, 8, last_two[:, 0])
         behind_cast[0] = tile([P, 3, S], F32, "behind_cast", "w1_raw0_512")
         shape_stage(3)
         reach_stage(4)
@@ -290,12 +301,22 @@ def tile_list_joseki_lesson_gaps_kernel(tc, tab_words, tab_scales, tab2_words, t
         multiply(3)
         weigh(4)
         cast_dealt(1, 4, 6)
-        quant_w1(0, 4, 8)
+        quant_w1(0, 4, 6)
         quant_w1(1, 4, 6)
+        cast_dealt(1, 6, 8, last_two[:, 1])
+        turned = tile([P, 2, 8, P, 2], BF16, "turned", "w1_raw1_512")
+        turn(0)
         shape_stage(4)
         shape_stage(5)
-        cast_dealt(1, 6, 8)
-        quant_w1(1, 6, 8)
+        turn(1)
+        last_codes = tile([P, 2, 2, P], U32, "last_codes")
+        last_scales = tile([P, 2, 2, P], U8, "last_scales")
+        nc.vector.quantize_mx(out=last_codes[:].rearrange("p a x c -> p (a x c)").bitcast(FP8X4),
+                              scales=last_scales[:].rearrange("p a x c -> p (a x c)"),
+                              in_=last_two[:].rearrange("p a c j -> p (a c j)"))
+        for a in range(2):
+            for x in (6, 7):
+                w1_q[x, a] = (last_codes[:, a, x - 6, :], last_scales[:, a, x - 6, :])
         scatter(3)
         multiply(4)
         scatter(4)
@@ -309,15 +330,8 @@ def tile_list_joseki_lesson_gaps_kernel(tc, tab_words, tab_scales, tab2_words, t
                 scatter(x)
 
         woven, page_c, page_s = {}, {}, {}
-        turned = tile([P, 2, 8, P, 2], BF16, "turned", "w1_raw1_512")
-        for x in range(4):
-            for c in (1, 0):
-                turn_ps = bank([P, 4, P], "turn_ps", 4 + 2 * (x % 2) + c)
-                for b in range(4):
-                    t0 = PASS * c + P * b
-                    nc.tensor.transpose(turn_ps[:, b, :], page[x][:, t0:t0 + P], ident[:])
-                nc.scalar.copy(out=turned[:, :, 4 * c:4 * (c + 1), 32 * x:32 * (x + 1), :],
-                               in_=turn_ps[:].rearrange("t b (q u e) -> t u b q e", u=2, e=2))
+        turn(2)
+        turn(3)
         for c in (1, 0):
             woven[0, c] = tile([P, PASS, 4], BF16, "woven0_%d" % c)
             for g in range(2):

@@ -49,11 +49,13 @@ def tile_list_joseki_lesson_gaps_kernel(tc, tab_words, tab_scales, tab2_words, t
         tab_s = tile([P, 2, T], U8, "tab_s")
         w2_s_raw = tile([P, 2, H], U8, "w2_s_raw")
         tab2_s = tile([P, T3], U8, "tab2_s")
+        v2_s = tile([P, S2], U8, "v2_s")
         nc.vector.memset(tab_s[:].bitcast(I32), 0)
         nc.vector.memset(w2_s_raw[:].bitcast(I32), 0)
         ident = tile([P, P], F32, "ident")
         make_identity(nc, ident[:])
         nc.gpsimd.memset(tab2_s[:].bitcast(I32), 0)
+        nc.gpsimd.memset(v2_s[:].bitcast(I32), 0)
 
         def load_words(src, a, tag):
             words = tile([P, T], I32, "words", tag)
@@ -101,9 +103,7 @@ def tile_list_joseki_lesson_gaps_kernel(tc, tab_words, tab_scales, tab2_words, t
         load_scales(tab_s, tab_scales, range(4))
         tab_w = [load_words(tab_words, 0, "tab_w0")]
         nc.sync.dma_start(moves[:], offs2)
-        for q in range(4):
-            nc.sync.dma_start(out=tab2_s[32 * q + 8:32 * q + 16, :].bitcast(I32),
-                              in_=tab2_scales[:, 4 * q:4 * q + 4, :].bitcast(I32))
+        nc.sync.dma_start(out=tab2_s[0:P:4, :].bitcast(I32), in_=tab2_scales.rearrange("a z t -> (a z) t").bitcast(I32))
         tab_w.append(load_words(tab_words, 1, "tab_w1"))
         load_scales(w2_s_raw, w2_scales, range(4))
         load_w1(0, 0, 256)
@@ -154,7 +154,6 @@ def tile_list_joseki_lesson_gaps_kernel(tc, tab_words, tab_scales, tab2_words, t
                 nc.scalar.copy(out=two[:, i, :], in_=dealt_ps[2 * g + i][:].rearrange("p b j -> p (b j)"))
 
         tab2_w = [load_words(tab2_words, a, "tab2_w%d" % a) for a in range(2)]
-        komi_sb = [load_komi(0), load_komi(1)]
 
         grouped, w1_q = {}, {}
 
@@ -180,12 +179,10 @@ def tile_list_joseki_lesson_gaps_kernel(tc, tab_words, tab_scales, tab2_words, t
 
         v2 = {}
 
-        def gather_v2(part, n0, n1, tag=None):
-            picked = tile([P, n1 - n0], U8 if part == "scales" else U32, "v2_%s_%d" % (part, n0), tag)
-            window = tab2_s[:] if part == "scales" else tab2_w[part][:].bitcast(U32)
-            nc.vector.tensor_copy(out=picked[:], in_=window.indirect(moves[:, n0 // 16:n1 // 16]))
-            for n in range(n0 // P, n1 // P):
-                v2[part, n] = (picked, slice(P * n - n0, P * (n + 1) - n0))
+        def gather_v2_scales(n0, n1, tag=None):
+            picked = tile([P, n1 - n0], U8, "v2_rows%d" % n0, tag)
+            nc.vector.tensor_copy(out=picked[:], in_=tab2_s[:].indirect(moves[:, n0 // 16:n1 // 16]))
+            return picked
 
         w2_dealt, behind_cast = {}, {}
         reach_ps, reach_sb, shape_ps, shape_sb, weighted, lesson = {}, {}, {}, {}, {}, {}
@@ -257,8 +254,13 @@ def tile_list_joseki_lesson_gaps_kernel(tc, tab_words, tab_scales, tab2_words, t
                                in_=turn_ps[:].rearrange("t b (q u e) -> t u b q e", u=2, e=2))
 
         half, quarter = S2 // 2, S2 // 4
-        gather_v2("scales", 0, half)
-        gather_v2("scales", half, S2, "tab_w1")
+        v2_rows = [gather_v2_scales(0, half), gather_v2_scales(half, S2, "tab_w1")]
+        for g in range(2):
+            for a in range(2):
+                for r in range(4):
+                    nc.sync.dma_start(out=v2_s[8 + 4 * a + r:P:32, half * g:half * (g + 1)].bitcast(I32),
+                                      in_=v2_rows[g][64 * a + 4 * r:64 * (a + 1):16, :].bitcast(I32))
+        komi_sb = [load_komi(0), load_komi(1)]
         deal_wgs(0)
         deal_wgs(1)
         cast_natural(0, 0, 2)
@@ -391,9 +393,8 @@ def tile_list_joseki_lesson_gaps_kernel(tc, tab_words, tab_scales, tab2_words, t
                 acc = bank([P, PASS], "acc", ((2, 1), (6, 7), (4, 5), (3, 0))[n % 4][c])
                 for h in range(2):
                     words, word_cols = v2[h, n]
-                    scales, scale_cols = v2["scales", n]
                     nc.tensor.matmul_mx(out=acc[:], lhsT=words[:, word_cols].bitcast(FP8X4),
-                                        lhsT_scale=scales[8 + 4 * h:P, scale_cols],
+                                        lhsT_scale=v2_s[8 + 4 * h:P, P * n:P * (n + 1)],
                                         rhs=page_c[h, c].bitcast(FP8X4),
                                         rhs_scale=page_s[h, c][:],
                                         start=h == 0, stop=h == 1)

@@ -24,7 +24,7 @@ PASS = 512
 ROW_TILES = H // P
 MOVE_TILES = S2 // P
 AHEAD = 5
-SQUARES_ON_VECTOR = 2
+SQUARES_ON_VECTOR = 1
 
 
 def tile_list_joseki_lesson_gaps_kernel(tc, tab_words, tab_scales, tab2_words, tab2_scales, w1, w2_words,
@@ -357,7 +357,7 @@ def tile_list_joseki_lesson_gaps_kernel(tc, tab_words, tab_scales, tab2_words, t
         quant_page(0, 1)
         pairs = tile([P, 2, 2, PASS, 2], BF16, "pairs", "weighted")
         for i in range(4):
-            for c in (1, 0):
+            for c in (0, 1):
                 rows = page[4 + i][:, PASS * c:PASS * (c + 1)]
                 if i < 2:
                     nc.gpsimd.tensor_scalar(out=pairs[:, c, 0, :, i], in0=rows, scalar1=1.0, scalar2=0.0, op0=MULT, op1=ADD)
@@ -365,42 +365,56 @@ def tile_list_joseki_lesson_gaps_kernel(tc, tab_words, tab_scales, tab2_words, t
                     nc.scalar.copy(out=pairs[:, c, 1, :, i - 2], in_=rows)
         for c in (1, 0):
             woven[1, c] = tile([P, PASS, 4], BF16, "woven1_%d" % c)
-            nc.scalar.copy(out=woven[1, c][:].bitcast(U32),
-                           in_=pairs[:, c].rearrange("p u t e -> p (u t e)").bitcast(U32).rearrange("p (u t) -> p t u", u=2))
+            if c == 1:
+                nc.scalar.copy(out=woven[1, c][:].bitcast(U32),
+                               in_=pairs[:, c].rearrange("p u t e -> p (u t e)").bitcast(U32).rearrange("p (u t) -> p t u", u=2))
+            else:
+                nc.vector.tensor_copy(out=woven[1, c][:].bitcast(I32),
+                                      in_=pairs[:, c].rearrange("p u t e -> p (u t e)").bitcast(I32).rearrange("p (u t) -> p t u", u=2))
 
         def gather_words(picked, g, a):
             nc.vector.tensor_copy(out=picked, in_=tab2_w[a][:].bitcast(U32).indirect(moves[:, 16 * g:16 * (g + 1)]))
             for n in (2 * g, 2 * g + 1):
                 v2[a, n] = (picked, slice(P * (n % 2), P * (n % 2 + 1)))
 
-        v2_first = tile([P, 2, 2, quarter], U32, "v2_first", "woven0_1")
-        for g in range(2):
-            for a in range(2):
-                gather_words(v2_first[:, g, a, :], g, a)
+        v2_first = tile([P, 2, quarter], U32, "v2_first", "woven0_1")
+        for a in range(2):
+            gather_words(v2_first[:, a, :], 0, a)
         quant_page(0, 0)
-        quant_page(1, 1)
         quant_page(1, 0)
-        v2_rest = tile([P, 2, 2, quarter], U32, "v2_rest", "woven1_0")
-        for g in range(2):
+        quant_page(1, 1)
+        v2_rest = tile([P, 3, 2, quarter], U32, "v2_rest", "woven1_1")
+        for g in range(3):
             for a in range(2):
-                gather_words(v2_rest[:, g, a, :], 2 + g, a)
+                gather_words(v2_rest[:, g, a, :], 1 + g, a)
 
-        scores = {}
+        scores, acc = {}, {}
+
+        def second_pass(n, c, h):
+            if h == 0:
+                acc[n, c] = bank([P, PASS], "acc", ((2, 1), (6, 7), (4, 5), (3, 0))[n % 4][c])
+            words, word_cols = v2[h, n]
+            nc.tensor.matmul_mx(out=acc[n, c][:], lhsT=words[:, word_cols].bitcast(FP8X4),
+                                lhsT_scale=v2_s[8 + 4 * h:P, P * n:P * (n + 1)],
+                                rhs=page_c[h, c].bitcast(FP8X4), rhs_scale=page_s[h, c][:], start=h == 0, stop=h == 1)
+            if h == 1:
+                if n not in scores:
+                    scores[n] = tile([P, T2], F32, "scores", "rows", ROW_TILES)
+                nc.scalar.copy(out=scores[n][:, PASS * c:PASS * (c + 1)], in_=acc[n, c][:])
 
         def second_stage(n):
-            scores[n] = tile([P, T2], F32, "scores", "rows", ROW_TILES)
             for c in (1, 0):
-                acc = bank([P, PASS], "acc", ((2, 1), (6, 7), (4, 5), (3, 0))[n % 4][c])
                 for h in range(2):
-                    words, word_cols = v2[h, n]
-                    nc.tensor.matmul_mx(out=acc[:], lhsT=words[:, word_cols].bitcast(FP8X4),
-                                        lhsT_scale=v2_s[8 + 4 * h:P, P * n:P * (n + 1)],
-                                        rhs=page_c[h, c].bitcast(FP8X4),
-                                        rhs_scale=page_s[h, c][:],
-                                        start=h == 0, stop=h == 1)
-                nc.scalar.copy(out=scores[n][:, PASS * c:PASS * (c + 1)], in_=acc[:])
+                    if (n, c) not in acc or h == 1:
+                        second_pass(n, c, h)
 
-        for n in range(AHEAD):
+        for c in (1, 0):
+            for n in range(2):
+                second_pass(n, c, 0)
+        for c in (0, 1):
+            for n in range(2):
+                second_pass(n, c, 1)
+        for n in range(2, AHEAD):
             second_stage(n)
         for n in range(MOVE_TILES):
             if n + AHEAD < MOVE_TILES:

@@ -356,13 +356,13 @@ def tile_list_joseki_lesson_gaps_kernel(tc, tab_words, tab_scales, tab2_words, t
         scatter(ROW_TILES - 1)
         quant_page(0, 1)
         pairs = tile([P, 2, 2, PASS, 2], BF16, "pairs", "weighted")
-        for i in range(4):
+        for c in (0, 1):
+            for i in range(2):
+                nc.gpsimd.tensor_scalar(out=pairs[:, c, 0, :, i], in0=page[4 + i][:, PASS * c:PASS * (c + 1)],
+                                        scalar1=1.0, scalar2=0.0, op0=MULT, op1=ADD)
+        for i in range(2):
             for c in (0, 1):
-                rows = page[4 + i][:, PASS * c:PASS * (c + 1)]
-                if i < 2:
-                    nc.gpsimd.tensor_scalar(out=pairs[:, c, 0, :, i], in0=rows, scalar1=1.0, scalar2=0.0, op0=MULT, op1=ADD)
-                else:
-                    nc.scalar.copy(out=pairs[:, c, 1, :, i - 2], in_=rows)
+                nc.scalar.copy(out=pairs[:, c, 1, :, i], in_=page[6 + i][:, PASS * c:PASS * (c + 1)])
         for c in (1, 0):
             woven[1, c] = tile([P, PASS, 4], BF16, "woven1_%d" % c)
             if c == 1:
@@ -423,7 +423,7 @@ def tile_list_joseki_lesson_gaps_kernel(tc, tab_words, tab_scales, tab2_words, t
                 gap = tile([P, m1 - m0], F32, "gap", bufs=MOVE_TILES + 1)[:]
                 nc.vector.tensor_tensor(out=gap, in0=scores[n][:].indirect(open_lessons[:, m0 // 16:m1 // 16]),
                                         in1=komi_sb[n // 4][:, n % 4, m0:m1], op=SUB)
-                if n < SQUARES_ON_VECTOR:
+                if n >= MOVE_TILES - SQUARES_ON_VECTOR:
                     nc.vector.tensor_tensor(out=gap, in0=gap, in1=gap, op=MULT)
                 else:
                     nc.scalar.activation(out=gap, in_=gap, func=ACT.Square)

from contextlib import ExitStack

import concourse.mybir as mybir
from concourse.masks import make_identity

K, H, T, S, T2, S2, T3, PICK = 1024, 1024, 2048, 512, 1024, 1024, 2048, 512
FLOPS = 2 * (2 * K * H * S + H * S2 * T2)

F32 = mybir.dt.float32
BF16 = mybir.dt.bfloat16
I32 = mybir.dt.int32
U32 = mybir.dt.uint32
U16 = mybir.dt.uint16
U8 = mybir.dt.uint8
FP8X4 = mybir.dt.float8_e4m3fn_x4
FP4X4 = mybir.dt.float4_e2m1fn_x4
MULT = mybir.AluOpType.mult
ADD = mybir.AluOpType.add
SUB = mybir.AluOpType.subtract
ACT = mybir.ActivationFunctionType

P = 128
PASS = 512
ROW_TILES = H // P
MOVE_TILES = S2 // P
AHEAD = 5
SQUARES_ON_VECTOR = 1


def tile_list_joseki_lesson_gaps_kernel(tc, tab_words, tab_scales, tab2_words, tab2_scales, w1, w2_words,
                                                      w2_scales, page0, wgs, komi, offs, offs2, offs3, offs4, out):
    nc = tc.nc
    with ExitStack() as ctx:
        lists = ctx.enter_context(tc.tile_pool(name="lists", bufs=1))
        sb = ctx.enter_context(tc.tile_pool(name="sb", bufs=1))
        psum = ctx.enter_context(tc.psum_pool(name="psum", bufs=1))

        def tile(shape, dtype, name, tag=None, bufs=1):
            return sb.tile(shape, dtype, name=name, tag=tag or name, bufs=bufs, align_bytes=64)

        def bank(shape, name, b):
            return psum.tile(shape, F32, name=name, tag="bank%d" % b)

        corners = lists.tile([P, S // 16], U16, name="corners")
        moves = lists.tile([P, S2 // 16], U16, name="moves")
        edited = lists.tile([P, S // 16], U16, name="edited")
        open_lessons = lists.tile([P, PICK // 16], U16, name="open_lessons")

        tab_s = tile([P, 2, T], U8, "tab_s")
        w2_s_raw = tile([P, 2, H], U8, "w2_s_raw")
        tab2_s = tile([P, T3], U8, "tab2_s")
        v2_s = tile([P, S2], U8, "v2_s")
        nc.vector.memset(tab_s[:].bitcast(I32), 0)
        nc.vector.memset(w2_s_raw[:].bitcast(I32), 0)
        ident = tile([P, P], F32, "ident")
        make_identity(nc, ident[:])
        nc.gpsimd.memset(tab2_s[:].bitcast(I32), 0)
        nc.gpsimd.memset(v2_s[:].bitcast(I32), 0)

        def load_words(src, a, tag):
            words = tile([P, T], I32, "words", tag)
            nc.sync.dma_start(out=words[:], in_=src[a].rearrange("p t i -> p (t i)").bitcast(I32))
            return words

        def load_scales(plane, src, rows):
            for r in rows:
                nc.sync.dma_start(out=plane[r:P:32, :, :].bitcast(I32),
                                  in_=src.rearrange("a (q r) t -> r q a t", r=4)[r].bitcast(I32))

        w1_raw = {}

        def load_w1(a, c0, c1):
            w1_raw[a, c0] = tile([P, 4, c1 - c0], F32, "w1_raw%d_%d" % (a, c0))
            nc.sync.dma_start(out=w1_raw[a, c0][:],
                              in_=w1[PASS * a:PASS * (a + 1), c0:c1].rearrange("(p j) c -> p j c", j=4))

        page = {}

        def load_page(x):
            page[x] = tile([P, T2], F32, "page", "rows", ROW_TILES)
            if x < 4:
                rows = page0[P * x:P * (x + 1), :]
            else:
                rows = page0[PASS:, :].rearrange("(p i) t -> p i t", i=4)[:, x - 4, :]
            nc.sync.dma_start(out=page[x][:], in_=rows)

        def load_komi(g):
            rows = tile([P, 4, PICK], F32, "komi_sb", ("tab_w0", "wgs_t")[g])
            nc.sync.dma_start(out=rows[:], in_=komi[PASS * g:PASS * (g + 1), :].rearrange("(c p) m -> p c m", p=P))
            return rows

        w2_raw = {}

        def load_w2(h):
            w2_raw[h] = tile([P, 2, H], U8, "w2_raw%d" % h)
            nc.sync.dma_start(out=w2_raw[h][:].bitcast(I32),
                              in_=w2_words[:, :, H * h:H * (h + 1)].rearrange("a p c -> p a c").bitcast(I32))

        nc.sync.dma_start(corners[:], offs)
        wgs_sb = tile([P, S], F32, "wgs_sb")
        nc.sync.dma_start(out=wgs_sb[:], in_=wgs)
        load_w2(0)
        load_scales(tab_s, tab_scales, range(4))
        tab_w = [load_words(tab_words, 0, "tab_w0")]
        nc.sync.dma_start(moves[:], offs2)
        nc.sync.dma_start(out=tab2_s[0:P:4, :].bitcast(I32), in_=tab2_scales.rearrange("a z t -> (a z) t").bitcast(I32))
        tab_w.append(load_words(tab_words, 1, "tab_w1"))
        load_scales(w2_s_raw, w2_scales, range(4))
        load_w1(0, 0, 256)
        load_w1(1, 0, 256)
        nc.sync.dma_start(edited[:], offs3)
        load_page(0)
        load_w1(0, 256, 512)
        load_w1(1, 256, 512)
        load_w2(1)
        nc.sync.dma_start(open_lessons[:], offs4)
        load_page(1)
        load_w1(0, 512, 1024)
        load_w1(1, 512, 1024)
        for x in (2, 4, 3, 5, 6, 7):
            load_page(x)

        v_s, v_w = [], []
        for a in range(2):
            picked_s = tile([P, S], U8, "v_s%d" % a)
            nc.vector.tensor_copy(out=picked_s[:], in_=tab_s[:, a, :].indirect(corners[:]))
            v_s.append(picked_s)
        for a in range(2):
            picked_w = tile([P, S], U32, "v_w%d" % a)
            nc.vector.tensor_copy(out=picked_w[:], in_=tab_w[a][:].bitcast(U32).indirect(corners[:]))
            v_w.append(picked_w)

        w2_s_dealt = tile([P, 2, 4, P], U8, "w2_s_dealt")
        nc.vector.tensor_copy(out=w2_s_dealt[:], in_=w2_s_raw[:, :, PASS:].rearrange("p a (m i) -> p a i m", i=4))

        wgs_t_ps = bank([P, 4, P], "wgs_t_ps", 7)
        for b in range(4):
            nc.tensor.transpose(wgs_t_ps[:, b, :], wgs_sb[:, P * b:P * (b + 1)], ident[:])
        wgs_t = tile([P, 2, 4, 2, 4, 32], F32, "wgs_t")
        for g in range(2):
            planes = wgs_t_ps[:].rearrange("j b (q i) -> j b i q", i=4)[:, :, 2 * g:2 * g + 2, :]
            nc.scalar.copy(out=wgs_t[:, g], in_=planes.unsqueeze(3).to_broadcast([P, 4, 2, 4, 32]))
        wg = {x: wgs_sb[:] for x in range(4)}
        dealt_ps = {}
        for i in range(4):
            dealt_ps[i] = bank([P, 4, P], "wg_ps", 4 + i)
            for b in range(4):
                nc.tensor.transpose(dealt_ps[i][:, b, :], wgs_t[:, i // 2, b, i % 2].rearrange("j g q -> j (g q)"), ident[:])

        def deal_wgs(g):
            two = tile([P, 2, S], F32, "wg%d" % g)
            for i in range(2):
                wg[4 + 2 * g + i] = two[:, i, :]
                nc.scalar.copy(out=two[:, i, :], in_=dealt_ps[2 * g + i][:].rearrange("p b j -> p (b j)"))

        tab2_w = [load_words(tab2_words, a, "tab2_w%d" % a) for a in range(2)]

        grouped, w1_q = {}, {}

        def cast_natural(a, x0, x1):
            c0 = 256 * (x0 // 2)
            grouped[a, x0] = tile([P, (x1 - x0) * P, 4], BF16, "grouped%d_%d" % (a, x0))
            nc.scalar.copy(out=grouped[a, x0][:].rearrange("p (c i) j -> p c j i", i=4),
                           in_=w1_raw[a, c0][:, :, P * x0 - c0:P * x1 - c0].rearrange("p j (c i) -> p c j i", i=4))

        def cast_dealt(a, x0, x1, into=None):
            grouped[a, x0] = into if into is not None else tile([P, (x1 - x0) * P, 4], BF16, "grouped%d_%d" % (a, x0))
            nc.scalar.copy(out=grouped[a, x0][:].rearrange("p (i m) j -> p m j i", m=P),
                           in_=w1_raw[a, PASS][:].rearrange("p j (m i) -> p m j i", i=4)[:, :, :, x0 - 4:x1 - 4])

        def quant_w1(a, x0, x1):
            codes = tile([P, (x1 - x0) * P], U32, "w1_codes%d_%d" % (a, x0))
            scales = tile([P, (x1 - x0) * P], U8, "w1_scales%d_%d" % (a, x0))
            nc.vector.quantize_mx(out=codes[:].bitcast(FP8X4), scales=scales[:],
                                  in_=grouped[a, x0][:].rearrange("p c j -> p (c j)"))
            for x in range(x0, x1):
                cols = slice(P * (x - x0), P * (x - x0 + 1))
                w1_q[x, a] = (codes[:, cols], scales[:, cols])

        v2 = {}

        def gather_v2_scales(n0, n1, tag=None):
            picked = tile([P, n1 - n0], U8, "v2_rows%d" % n0, tag)
            nc.vector.tensor_copy(out=picked[:], in_=tab2_s[:].indirect(moves[:, n0 // 16:n1 // 16]))
            return picked

        w2_dealt, behind_cast = {}, {}
        reach_ps, reach_sb, shape_ps, shape_sb, weighted, lesson = {}, {}, {}, {}, {}, {}
        on_vector = (0, 2)
        shape_bank = (4, 5, 0, 2, 3, 0, 2, 1)
        reach_bank = (0, 2, 4, 5, 1, 3) + shape_bank[6:]
        lesson_slot = "ABBABABA"

        def reach_stage(x):
            reach_ps[x] = bank([P, S], "reach", reach_bank[x])
            for a in range(2):
                if x < 4:
                    words, scales = w2_raw[0][:, a, 2 * P * x:2 * P * (x + 1)], w2_s_raw[:, a, P * x:P * (x + 1)]
                else:
                    words, scales = w2_dealt[0][:, a, x - 4, :], w2_s_dealt[:, a, x - 4, :]
                nc.tensor.matmul_mx(out=reach_ps[x][:], lhsT=words.bitcast(FP4X4), lhsT_scale=scales,
                                    rhs=v_w[a][:].bitcast(FP8X4), rhs_scale=v_s[a][:], start=a == 0, stop=a == 1)
            if x == 2:
                both = tile([P, 2, S], F32, "reach23", "w1_raw1_256")
                reach_sb[2], reach_sb[3] = both[:, 0, :], both[:, 1, :]
            elif x == 1:
                reach_sb[x] = tile([P, S], F32, "reach1", "w1_raw1_0")[:]
            elif x in (4, 5):
                reach_sb[x] = behind_cast[0][:, x - 3, :]
            elif x not in (0, 3):
                reach_sb[x] = tile([P, S], F32, "reach_sb", bufs=3)[:]
            if x > 0:
                nc.scalar.copy(out=reach_sb[x], in_=reach_ps[x][:])

        def shape_stage(x):
            shape_ps[x] = bank([P, S], "shape", shape_bank[x])
            for a in range(2):
                nc.tensor.matmul_mx(out=shape_ps[x][:], lhsT=w1_q[x, a][0].bitcast(FP8X4), lhsT_scale=w1_q[x, a][1],
                                    rhs=v_w[a][:].bitcast(FP8X4), rhs_scale=v_s[a][:], start=a == 0, stop=a == 1)
            if x not in on_vector:
                if x == 3:
                    shape_sb[x] = behind_cast[0][:, 0, :]
                elif x == ROW_TILES - 1:
                    shape_sb[x] = tile([P, S], F32, "shape_last")[:]
                else:
                    shape_sb[x] = tile([P, S], F32, "shape_sb", bufs=3)[:]
                nc.scalar.copy(out=shape_sb[x], in_=shape_ps[x][:])

        def weigh(x):
            if x == 0:
                weighted[x] = tile([P, S], F32, "weighted0", "grouped1_0")
                nc.vector.tensor_tensor(out=weighted[x][:], in0=reach_ps[x][:], in1=wg[x], op=MULT)
            else:
                weighted[x] = tile([P, S], F32, "weighted")
                nc.gpsimd.tensor_tensor(out=weighted[x][:], in0=reach_sb[x], in1=wg[x], op=MULT)

        def multiply(x):
            lesson[x] = tile([P, S], F32, "lesson" + lesson_slot[x])
            if x in on_vector:
                nc.vector.tensor_tensor(out=lesson[x][:], in0=shape_ps[x][:], in1=weighted[x][:], op=MULT)
            else:
                nc.gpsimd.tensor_tensor(out=lesson[x][:], in0=shape_sb[x], in1=weighted[x][:], op=MULT)

        def scatter(x):
            nc.vector.tensor_copy(out=page[x][:].indirect(edited[:]), in_=lesson[x][:])

        def turn(x):
            for c in (1, 0):
                turn_ps = bank([P, 4, P], "turn_ps", 4 + 2 * (x % 2) + c)
                for b in range(4):
                    t0 = PASS * c + P * b
                    nc.tensor.transpose(turn_ps[:, b, :], page[x][:, t0:t0 + P], ident[:])
                nc.scalar.copy(out=turned[:, :, 4 * c:4 * (c + 1), 32 * x:32 * (x + 1), :],
                               in_=turn_ps[:].rearrange("t b (q u e) -> t u b q e", u=2, e=2))

        half, quarter = S2 // 2, S2 // 4
        v2_rows = [gather_v2_scales(0, half), gather_v2_scales(half, S2, "tab_w1")]
        for g in range(2):
            for a in range(2):
                for r in range(4):
                    nc.sync.dma_start(out=v2_s[8 + 4 * a + r:P:32, half * g:half * (g + 1)].bitcast(I32),
                                      in_=v2_rows[g][64 * a + 4 * r:64 * (a + 1):16, :].bitcast(I32))
        komi_sb = [load_komi(0), load_komi(1)]
        deal_wgs(0)
        deal_wgs(1)
        cast_natural(0, 0, 2)
        quant_w1(0, 0, 2)
        reach_stage(0)
        cast_natural(1, 0, 1)
        cast_natural(1, 1, 2)
        reach_stage(1)
        quant_w1(1, 0, 1)
        shape_stage(0)
        weigh(0)
        quant_w1(1, 1, 2)
        shape_stage(1)
        multiply(0)
        weigh(1)
        multiply(1)
        scatter(0)
        cast_natural(0, 2, 4)
        cast_natural(1, 2, 4)
        quant_w1(0, 2, 4)
        quant_w1(1, 2, 4)
        reach_stage(2)
        reach_stage(3)
        weigh(2)
        shape_stage(2)
        scatter(1)
        w2_dealt[0] = tile([P, 2, 4, 2 * P], U8, "w2_dealt")
        nc.scalar.copy(out=w2_dealt[0][:].bitcast(U16),
                       in_=w2_raw[1][:].bitcast(U16).rearrange("p a (m i) -> p a i m", i=4))
        cast_dealt(0, 4, 6)
        last_two = tile([P, 2, 2 * P, 4], BF16, "last_two")
        cast_dealt(0, 6, 8, last_two[:, 0])
        behind_cast[0] = tile([P, 3, S], F32, "behind_cast", "w1_raw0_512")
        shape_stage(3)
        reach_stage(4)
        reach_stage(5)
        multiply(2)
        scatter(2)
        weigh(3)
        multiply(3)
        weigh(4)
        cast_dealt(1, 4, 6)
        quant_w1(0, 4, 6)
        quant_w1(1, 4, 6)
        cast_dealt(1, 6, 8, last_two[:, 1])
        turned = tile([P, 2, 8, P, 2], BF16, "turned", "w1_raw1_512")
        turn(0)
        shape_stage(4)
        shape_stage(5)
        turn(1)
        last_codes = tile([P, 2, 2, P], U32, "last_codes")
        last_scales = tile([P, 2, 2, P], U8, "last_scales")
        nc.vector.quantize_mx(out=last_codes[:].rearrange("p a x c -> p (a x c)").bitcast(FP8X4),
                              scales=last_scales[:].rearrange("p a x c -> p (a x c)"),
                              in_=last_two[:].rearrange("p a c j -> p (a c j)"))
        for a in range(2):
            for x in (6, 7):
                w1_q[x, a] = (last_codes[:, a, x - 6, :], last_scales[:, a, x - 6, :])
        scatter(3)
        multiply(4)
        scatter(4)
        for x in (6, 7):
            shape_stage(x)
            reach_stage(x)
        for x in range(5, ROW_TILES):
            weigh(x)
            multiply(x)
            if x + 1 < ROW_TILES:
                scatter(x)

        woven, page_c, page_s = {}, {}, {}
        turn(2)
        turn(3)
        for c in (1, 0):
            woven[0, c] = tile([P, PASS, 4], BF16, "woven0_%d" % c)
            for g in range(2):
                back_ps = bank([P, 2, 2, P], "back_ps", (3, 0, 4, 5)[2 * c + g])
                for b in range(2):
                    for u in range(2):
                        words = turned[:, u, 4 * c + 2 * g + b, :, :].rearrange("t p e -> t (p e)").bitcast(F32)
                        nc.tensor.transpose(back_ps[:, b, u, :], words, ident[:])
                nc.scalar.copy(out=woven[0, c][:, 256 * g:256 * (g + 1), :].bitcast(F32).rearrange("p (b t) u -> p b t u", b=2),
                               in_=back_ps[:].rearrange("p b u t -> p b t u"))

        page_codes = [tile([P, 2, PASS], U32, "page_c0", "shape_last"), tile([P, 2, PASS], U32, "page_c1")]

        def quant_page(h, c):
            page_c[h, c] = page_codes[h][:, c, :]
            page_s[h, c] = tile([P, PASS], U8, "page_s%d_%d" % (h, c))
            nc.vector.quantize_mx(out=page_c[h, c].bitcast(FP8X4), scales=page_s[h, c][:],
                                  in_=woven[h, c][:].rearrange("p t i -> p (t i)"))

        scatter(ROW_TILES - 1)
        quant_page(0, 1)
        pairs = tile([P, 2, 2, PASS, 2], BF16, "pairs", "weighted")
        for c in (0, 1):
            for i in range(2):
                nc.gpsimd.tensor_scalar(out=pairs[:, c, 0, :, i], in0=page[4 + i][:, PASS * c:PASS * (c + 1)],
                                        scalar1=1.0, scalar2=0.0, op0=MULT, op1=ADD)
        for i in range(2):
            for c in (0, 1):
                nc.scalar.copy(out=pairs[:, c, 1, :, i], in_=page[6 + i][:, PASS * c:PASS * (c + 1)])
        for c in (1, 0):
            woven[1, c] = tile([P, PASS, 4], BF16, "woven1_%d" % c)
            if c == 1:
                nc.scalar.copy(out=woven[1, c][:].bitcast(U32),
                               in_=pairs[:, c].rearrange("p u t e -> p (u t e)").bitcast(U32).rearrange("p (u t) -> p t u", u=2))
            else:
                nc.vector.tensor_copy(out=woven[1, c][:].bitcast(I32),
                                      in_=pairs[:, c].rearrange("p u t e -> p (u t e)").bitcast(I32).rearrange("p (u t) -> p t u", u=2))

        def gather_words(picked, g, a):
            nc.vector.tensor_copy(out=picked, in_=tab2_w[a][:].bitcast(U32).indirect(moves[:, 16 * g:16 * (g + 1)]))
            for n in (2 * g, 2 * g + 1):
                v2[a, n] = (picked, slice(P * (n % 2), P * (n % 2 + 1)))

        v2_first = tile([P, 2, quarter], U32, "v2_first", "woven0_1")
        for a in range(2):
            gather_words(v2_first[:, a, :], 0, a)
        quant_page(0, 0)
        quant_page(1, 0)
        quant_page(1, 1)
        v2_rest = tile([P, 3, 2, quarter], U32, "v2_rest", "woven1_1")
        for g in range(3):
            for a in range(2):
                gather_words(v2_rest[:, g, a, :], 1 + g, a)

        scores, acc = {}, {}

        def second_pass(n, c, h):
            if h == 0:
                acc[n, c] = bank([P, PASS], "acc", ((2, 1), (6, 7), (4, 5), (3, 0))[n % 4][c])
            words, word_cols = v2[h, n]
            nc.tensor.matmul_mx(out=acc[n, c][:], lhsT=words[:, word_cols].bitcast(FP8X4),
                                lhsT_scale=v2_s[8 + 4 * h:P, P * n:P * (n + 1)],
                                rhs=page_c[h, c].bitcast(FP8X4), rhs_scale=page_s[h, c][:], start=h == 0, stop=h == 1)
            if h == 1:
                if n not in scores:
                    scores[n] = tile([P, T2], F32, "scores", "rows", ROW_TILES)
                nc.scalar.copy(out=scores[n][:, PASS * c:PASS * (c + 1)], in_=acc[n, c][:])

        def second_stage(n):
            for c in (1, 0):
                for h in range(2):
                    if (n, c) not in acc or h == 1:
                        second_pass(n, c, h)

        for c in (1, 0):
            for n in range(2):
                second_pass(n, c, 0)
        for c in (0, 1):
            for n in range(2):
                second_pass(n, c, 1)
        for n in range(2, AHEAD):
            second_stage(n)
        for n in range(MOVE_TILES):
            if n + AHEAD < MOVE_TILES:
                second_stage(n + AHEAD)
            for m0, m1 in ([(0, PICK)] if n < MOVE_TILES - 1 else [(0, PICK // 2), (PICK // 2, PICK)]):
                gap = tile([P, m1 - m0], F32, "gap", bufs=MOVE_TILES + 1)[:]
                nc.vector.tensor_tensor(out=gap, in0=scores[n][:].indirect(open_lessons[:, m0 // 16:m1 // 16]),
                                        in1=komi_sb[n // 4][:, n % 4, m0:m1], op=SUB)
                if n >= MOVE_TILES - SQUARES_ON_VECTOR:
                    nc.vector.tensor_tensor(out=gap, in0=gap, in1=gap, op=MULT)
                else:
                    nc.scalar.activation(out=gap, in_=gap, func=ACT.Square)
                nc.sync.dma_start(out=out[P * n:P * (n + 1), m0:m1], in_=gap)
